import numpy as np, ml_dtypes
CORES = [48,51,52,55]
N = 4
import mx_ref
BF = ml_dtypes.bfloat16
def cut(t, i, w=512):
    return t[:, w * i:w * i + w]
def pick(q, e):
    c = np.concatenate([q[0].reshape(128, -1, 4), np.zeros((128, 1, 4), np.uint8)], axis=1); s = np.concatenate([q[1], np.ones((16, 1), np.uint8)], axis=1)
    return (np.ascontiguousarray(c[:, e].reshape(128, -1)), np.ascontiguousarray(s[:, e]))
def join(*qs):
    return (np.concatenate([q[0] for q in qs], axis=1), np.concatenate([q[1] for q in qs], axis=1))
def put(q, e, v):
    c, s = q[0].reshape(128, -1, 4).copy(), q[1].copy(); c[:, e] = v[0].reshape(128, -1, 4); s[:, e] = v[1]
    return (c.reshape(128, -1), s)
def pk(c, s):
    return (np.ascontiguousarray(c), mx_ref.live(s))
def emit(q):
    return q[0], q[1]
def decode(q):
    o = []
    for b in range(4):
        e = np.zeros((128, 128, 4), np.float32); e[np.arange(128), np.arange(128), b] = 1
        o.append(mx_ref.matmul(mx_ref.quantize(e.reshape(128, 512).astype(BF)), q))
    return np.stack(o, axis=2).reshape(128, -1)
def f(rng, *shape):
    return mx_ref.flush((rng.standard_normal(shape, dtype=np.float32) * np.exp2(rng.integers(-2, 3, shape[:-1] + (1,)))).astype(BF))
def wide(rng, *shape, cols=0):
    v = rng.standard_normal(shape, dtype=np.float32) * np.exp2(rng.integers(-12, 13, shape)).astype(np.float32)
    if cols: v *= np.repeat(np.exp2(rng.integers(-cols, cols + 1, shape[:-2] + (1, shape[-1] // 4))) * (rng.random(shape[:-2] + (1, shape[-1] // 4)) > 0.0625), 4, axis=-1).astype(np.float32)
    return mx_ref.flush(v.astype(BF))
P, K, O = 256, 64, 2
def places(t, j):
    return (j + t * np.arange(N)[:, None]) % P
def checks(tab, u):
    return np.stack([mx_ref.matmul(mx_ref.quantize(np.ascontiguousarray(u[r])), tab[r])[:2] for r in range(N)], axis=1)
def judge(c, g, t):
    j = np.arange(P)
    p = (j + t) % N
    at = places(t, j)
    c, a = c[np.arange(N)[:, None], at], np.abs(g[np.arange(N)[:, None], at])
    s = c[p, j]
    for r in range(N):
        s = np.where(p == r, s, s - c[r])
    bad = np.argsort(-np.abs(s), kind="stable")[:K]
    a[p, j] = -1
    return bad, np.argmax(a, axis=0)[bad]
def rebuilt(tab, bad, lost, t):
    at = places(t, bad)
    v = decode(join(*[pick(tab[r], at[r]) for r in range(N)])).reshape(128, N, K, 4)
    new = np.zeros((128, K, 4), np.float32)
    for k in range(K):
        p = (bad[k] + t) % N
        x = v[:, p, k]
        for r in range(N):
            if r != p and r != lost[k]: x = x - v[:, r, k]
        new[:, k] = x
    return mx_ref.quantize(np.ascontiguousarray(new.reshape(128, -1).astype(BF)))
def data(rng):
    return f(rng, N, 128, 4 * P).astype(np.float32).reshape(N, 128, P, 4)
def striped(v):
    v = v.copy()
    for r in range(N):
        j = np.arange(r, P, N)
        v[r][:, j] = 0
        v[r][:, j] = np.sum(v[:, :, j], axis=0)
    return v
def harm(rng, v, stripes, size):
    for j in stripes:
        v[(j + rng.integers(1, N)) % N][:, j] = size * rng.standard_normal((128, 4))
def queries(rng):
    q = np.array(f(rng, 1, 128, 512))
    q[:, :, 8:] = 0
    return np.concatenate([q] * N)
def draw(rng, v, q=None):
    v = v.astype(np.float32).reshape(N, 128, 4 * P)
    v[np.abs(v) < np.float32(2.0 ** -16)] = 0
    return {"tb": v.astype(BF), "u": queries(rng) if q is None else q, "w": f(rng, N, 128, 512 * O)}
def setup_inputs(rng):
    v = striped(data(rng))
    harm(rng, v, rng.permutation(P)[:K + 6], 8)
    return draw(rng, v)
def setup_inputs_again(rng):
    v, q = striped(data(rng) * np.float32(2.0 ** -8)), queries(rng)
    s = np.where(q[0, :, 4:8].astype(np.float32) < 0, -1.0, 1.0)
    q[:, :, :4] = (np.abs(q[:, :, :4].astype(np.float32)) * s).astype(BF)
    q[:, :32, :4] = 0
    on = (np.arange(128) < 32)[:, None]
    at = N * rng.permutation(P // N)[:K // 2] + 2 * rng.integers(0, N // 2, K // 2) + np.arange(K // 2) % 2
    for j in at:
        p = int(j) % N
        m = (p + int(rng.integers(1, N))) % N
        if p % 2:
            m = ((p + 1) // 2 + N // 2 * int(rng.integers(0, 2))) % N
            if m == p: m = (m + N // 2) % N
        v[m][:, j] = 2.0 ** -4 * (1 + rng.random((128, 4))) * s * on
        v[p][:, j] = (2.0 ** 5 if p % 2 else -2.0 ** 5) * (1 + rng.random((128, 4))) * s
    return draw(rng, v, q)
def setup_inputs_one(rng):
    v, q = striped(data(rng)), queries(rng)
    s = np.where(q[0, :, :4].astype(np.float32) < 0, -1.0, 1.0)
    q[:, :, 4:8] = (np.abs(q[:, :, 4:8].astype(np.float32)) * s).astype(BF)
    m, i = int(rng.integers(0, N)), np.arange(P)
    at = rng.permutation(np.flatnonzero((i % N != m) & ((i - m + 1) % N != m)))[:2 * K]
    size = np.repeat([2.0 ** 16, 2.0 ** 11], K)
    v[m][:, at] = (1 + rng.random((128, 2 * K, 4))) * s[:, None] * size[:, None]
    return draw(rng, v, q)
def setup_inputs_spread(rng):
    q = (queries(rng).astype(np.float32) * np.float32(2.0 ** 20)).astype(BF)
    return draw(rng, wide(rng, N, 128, 4 * P, cols=6), q)
def setup_inputs_ties(rng):
    v, q = np.zeros((N, 128, P, 4), np.float32), queries(rng)
    s = np.where(q[0, :, 4:8].astype(np.float32) < 0, -1.0, 1.0)
    q[:, :32, :4] = 0
    on = (np.arange(128) < 32)[:, None]
    for p in range(N):
        at = p + N * rng.permutation(P // N)
        for g in range(P // N // 3):
            x = 2.0 ** -2 * rng.standard_normal((N, 128, 1, 4))
            a, b, m = (p + 1 + rng.permutation(N - 1)[:3]) % N
            x[p] *= 2.0 ** 22
            x[m] = x[p]
            x[a, :, 0] = np.where(on, 2.0 ** 23 * (1 + rng.random((128, 4))) * s, x[a, :, 0])
            x[b] = x[a] * rng.choice([-1.0, 1.0])
            v[:, :, at[3 * g:3 * g + 3]] = x * rng.choice([-1.0, 1.0], (3, 1))
    return draw(rng, v, q)
def setup_inputs_zero(rng):
    v = striped(data(rng))
    lo, hi = int(rng.integers(0, K // 4 + 1)), int(rng.integers(K // 2, P - K // 4 + 1))
    v[:, :, :hi] = 0
    v[:, :, hi + K // 4:] = 0
    for j in range(lo, lo + K // 4):
        m, n = (j + 1 + rng.permutation(N - 1)[:2]) % N
        v[m][:, j] = 4 * rng.standard_normal((128, 4))
        v[n][:, j] = -v[m][:, j]
    harm(rng, v, np.arange(hi, hi + K // 4), 8)
    return draw(rng, v)
def check_inputs(d):
    b = []
    for k, lo, hi in (("tb", -16, 24), ("u", -30, 30), ("w", -30, 30)):
        v = np.abs(d[k].astype(np.float32))
        if not (np.isfinite(v).all() and ((v == 0) | (v >= 2.0 ** lo) & (v <= 2.0 ** hi)).all()): b.append("a value of " + k)
    q = d["u"].astype(np.float32)
    if (q[:, :, 8:] != 0).any(): b.append("u has numbers behind its first 2 columns")
    if (q != q[:1]).any(): b.append("u isn't the same on all ranks")
    return b
def reference(tb, u, w):
    tab = [mx_ref.quantize(np.ascontiguousarray(tb[r])) for r in range(N)]
    bs = np.zeros((N, 4, K), np.float32)
    for t in range(2):
        c, g = checks(tab, u)
        bad, lost = judge(c, g, t)
        new = rebuilt(tab, bad, lost, t)
        at = places(t, bad)
        for r in range(N):
            e = np.flatnonzero(lost == r)
            tab[r] = put(tab[r], at[r, e], pick(new, e))
        bs[:, 2 * t] = bad
        bs[:, 2 * t + 1] = lost
    oc, osc, y = np.zeros((N, 128, 4 * P), np.uint8), np.zeros((N, 16, P), np.uint8), np.zeros((N, 128, O * P), np.float32)
    for r in range(N):
        oc[r], osc[r] = emit(tab[r])
        for o in range(O):
            y[r, :, o * P:o * P + P] = mx_ref.matmul(mx_ref.quantize(np.ascontiguousarray(cut(w[r], o))), tab[r])
    return {"oc": oc, "osc": osc, "bs": bs, "y": y}

@@ -1,0 +1,663 @@
+from concourse.bass import DstId, RemoteDMATransfer
+from concourse.mybir import dt, AluOpType as Op, AxisListType, ActivationFunctionType as Act
+
+N, P, K = 4, 256, 64
+R1, R2 = 352, 608
+BUILD = ((0, 2), (1, 3))
+TINY = 2.0 ** -110
+
+F, B, I, U16, CODES = "float32", "bfloat16", "int32", "uint16", "float8_e4m3fn_x4"
+SCRATCH, LOG, _TOP = {}, {}, {}
+
+
+def _own(dtype, **kw):
+    for n, c in kw.items():
+        SCRATCH[n] = ("sbuf", [128, c], dtype)
+        LOG[n] = (n, 0, c, dtype)
+
+
+def _slab(slab, dtype, **kw):
+    for n, c in kw.items():
+        at = _TOP.get(slab, 0)
+        LOG[n] = (slab, at, c, dtype)
+        _TOP[slab] = at + (c + 15) // 16 * 16
+        SCRATCH[slab] = ("sbuf", [128, _TOP[slab]], dtype)
+
+
+_own(B, tbt=1040, ut=512, wt=1024, zt=512, eb=2048, ub0=512, ub1=512, h0=512, h1=512)
+for _n, _c in dict(tq=256, tw=512, tx=768, uq=128, uc=128, ug=128, eq=512, wq=256, tz=256, sla=64, slb=64,
+                   laa=128, lab=128, psa=128, psb=128, ou=256).items():
+    _own(CODES, **{_n: _c})
+    _own("uint8", **{_n + "_s": _c})
+for _n in ("pa", "pu"):
+    SCRATCH[_n] = ("psum", [128, 2048], F)
+    LOG[_n] = (_n, 0, 2048, F)
+_own(F, ones=128, idn=128, l0=16, l1=16, xs=256, xd=128, ys=512, fr=640, ft=512)
+_slab("fs", F, jc=2, jp=2, cf=8, rr=16, wm=8, wl=8, wl1=6, wmg=8, r9=4, ma=12, mb=12, m0=16, rho=4, cs=8, cs2=8, csf=8, cso=2,
+      kk=6, tr=8, ofrf=4, zf=32, kt=128, va=128, vb=128, d0a=16, d0b=8,
+      jl=16, jex=64, jr=256, tri=512, oh=512, prc=520, prg=390, rep=8, nrep=8, kra=12, krb=12, kro=16, kr0=16, pm=130, src1=2,
+      oho=128, sqc=8, gq=6, junk=1024)
+for _t in "01":
+    _slab("fs", F, **{n + _t: c for n, c in dict(sq=16, sc=16, ex=64, sa=2, nd=2, dl=2, row=256, xx=512, cm=512, po=2, mm=256, mt=256,
+                                                 lw=8, aa=4, ab=4, ac=4, nm=256, nt=256, nw=8, na=4, nb=4, nc=8,
+                                                 ga=8, gm=8, gx=2, ge=8, gw=8, gn=2, pay=2, er=64, lr=64, bsf=128).items()})
+    _slab("is_", I, **{n + _t: c for n, c in dict(wi=4, rq=2, rl=2, ra=2, rb=2, e1=2, e2=2, e3=2, e4=2, rk=6, rf=6,
+                                                  fi=4, fj=4, fk=4, fa=8, fl=4, fm=4, fd=8, fe=8, fo=8, bi=64, bj=128).items()})
+    _slab("us", U16, **{n + _t: c for n, c in dict(off=4, rfo=6, ofs=8, exo=4).items()})
+_slab("is_", I, pi=4, ci=8, csi=8, csj=8, kki=6, tri32=8)
+_slab("us", U16, ofr=4, ofu=32, ofv=32, fou=16)
+
+SEMAPHORES = ["sv", "ss", "st", "sg", "dl_u", "dl_t0", "dl_t1", "dl_w", "dl_x", "dl_x_s", "dbs0", "dbs1", "dy0", "dy1", "doc", "ls",
+              "a0", "a1", "ha0", "ha1", "hb0", "hb1"]
+_QS = {"v": "sv", "s": "ss", "t": "st", "g": "sg"}
+
+
+def W(name, c0=0, c1=None, step=1, p0=0, p1=128):
+    return (name, c0, LOG[name][2] if c1 is None else c1, step, p0, p1)
+
+
+def rank_program(g, core, T, topo):
+    r = T.rank_of(core)
+    if r is None:
+        return
+    queue = {"v": g.vector, "s": g.scalar, "t": g.tensor, "g": g, "y": g.sync}
+    total, known, snap, log = {}, {q: {} for q in queue}, {}, {}
+
+    def ap(w):
+        n, c0, c1, st, p0, p1 = w
+        n, at = LOG[n][:2]
+        c0, c1 = c0 + at, c1 + at
+        return T[n][p0:p1, c0:c1] if st == 1 else T[n][p0:p1, c0:c1:st]
+
+    def wait(q, tok):
+        s, v = tok
+        if known[q].get(s, 0) >= v:
+            return
+        queue[q].wait_ge(T.sem[s], v)
+        known[q][s] = v
+        for a, b in snap.get(tok, {}).items():
+            if known[q].get(a, 0) < b:
+                known[q][a] = b
+
+    def meet(a, b):
+        if a[4] >= b[5] or b[4] >= a[5]:
+            return False
+        if a[0] in ("pa", "pu"):
+            return a[1] // 512 <= (b[2] - 1) // 512 and b[1] // 512 <= (a[2] - 1) // 512
+        if a[1] >= b[2] or b[1] >= a[2]:
+            return False
+        return not (a[3] == b[3] and a[3] > 1 and (a[1] - b[1]) % a[3])
+
+    def order(q, reads, writes):
+        need = {}
+        for ws, isw in ((reads, False), (writes, True)):
+            for w in ws:
+                for w2, isw2, tok, q2 in log.get(w[0], ()):
+                    if (isw or isw2 or (w[0] in ("pa", "pu") and q != q2)) and meet(w, w2):
+                        need[tok[0]] = max(need.get(tok[0], 0), tok[1])
+        for s in sorted(need):
+            wait(q, (s, need[s]))
+
+    def record(q, reads, writes, tok):
+        for ws, isw in ((reads, False), (writes, True)):
+            for w in ws:
+                log.setdefault(w[0], []).append((w, isw, tok, q))
+
+    def done(q, ins, reads, writes, sem=None, by=1):
+        s = sem or _QS[q]
+        total[s] = total.get(s, 0) + by
+        ins.then_inc(T.sem[s], by)
+        tok = (s, total[s])
+        snap[tok] = dict(known[q])
+        record(q, reads, writes, tok)
+        return tok
+
+    def tt(out, a, b, op):
+        order("v", [a, b], [out])
+        return done("v", g.vector.tensor_tensor(ap(out), ap(a), ap(b), op), [a, b], [out])
+
+    def ts(out, a, s1, op0, s2=None, op1=None):
+        rd = [a] + [s for s in (s1, s2) if isinstance(s, tuple)]
+        order("v", rd, [out])
+        x1, x2 = [ap(s) if isinstance(s, tuple) else s for s in (s1, s2)]
+        ins = g.vector.tensor_scalar(ap(out), ap(a), x1, x2, op0, op1) if op1 is not None else g.vector.tensor_scalar(ap(out), ap(a), x1, None, op0)
+        return done("v", ins, rd, [out])
+
+    def cp(out, a, q="v"):
+        order(q, [a], [out])
+        ins = g.vector.tensor_copy(ap(out), ap(a)) if q == "v" else g.scalar.activation(ap(out), ap(a), Act.Copy)
+        return done(q, ins, [a], [out])
+
+    def red(out, a, op):
+        order("v", [a], [out])
+        return done("v", g.vector.tensor_reduce(ap(out), ap(a), AxisListType.X, op), [a], [out])
+
+    def fill(out, c):
+        order("v", [], [out])
+        return done("v", g.vector.memset(ap(out), c), [], [out])
+
+    def turn(out, a):
+        order("v", [a], [out])
+        return done("v", g.vector.transpose(ap(out), ap(a)), [a], [out])
+
+    def scan(out, d0, d1):
+        order("v", [d0, d1], [out])
+        return done("v", g.vector.tensor_tensor_scan(ap(out), ap(d0), ap(d1), 0.0, Op.mult, Op.subtract), [d0, d1], [out])
+
+    def act(out, a, f, off=None, scale=None, bias=None, acc=None):
+        rd = [a] + [w for w in (off, scale, bias) if w is not None]
+        wr = [out] + ([acc] if acc is not None else [])
+        order("s", rd, wr)
+        src = ap(a) if off is None else ap(a).indirect(ap(off))
+        kw = {}
+        if scale is not None: kw["scale"] = ap(scale)
+        if bias is not None: kw["bias"] = ap(bias)
+        if acc is not None: kw["accum_out"] = ap(acc)
+        return done("s", g.scalar.activation(ap(out), src, f, **kw), rd, wr)
+
+    junk = [0]
+
+    def acc(out, a):
+        n = a[2] - a[1]
+        if junk[0] + n > 1024:
+            junk[0] = 0
+        j = W("junk", junk[0], junk[0] + n)
+        junk[0] += n
+        return act(j, a, Act.Copy, acc=out)
+
+    def iota(out, pattern, base=0, cm=0):
+        order("g", [], [out])
+        kw = {} if LOG[out[0]][3] == I else {"allow_small_or_imprecise_dtypes": True}
+        return done("g", g.iota(ap(out), pattern, base, cm, **kw), [], [out])
+
+    def quant(name, c0, src, s0, n):
+        q, s, x = W(name, c0, c0 + n), W(name + "_s", c0, c0 + n), W(src, s0, s0 + 4 * n)
+        order("v", [x], [q, s])
+        return done("v", g.vector.quantize_mx(ap(q), ap(s), ap(x)), [x], [q, s])
+
+    def mm(bank, lhs, l0, rhs, r0, n=128):
+        rd = [W(lhs, l0, l0 + 128), W(lhs + "_s", l0, l0 + 128), W(rhs, r0, r0 + n), W(rhs + "_s", r0, r0 + n)]
+        o = W("pu" if bank > 3 else "pa", 512 * (bank % 4), 512 * (bank % 4) + n)
+        order("t", rd, [o])
+        return done("t", g.tensor.matmul_mx(ap(o), ap(rd[0]), ap(rd[1]), ap(rd[2]), ap(rd[3]), True, True), rd, [o])
+
+    def pick(dst, d0, src, width, off, o0, n):
+        o, a, f = W(dst, d0, d0 + n), W(src, 0, width), W(off, o0, o0 + n // 16)
+        order("v", [a, f], [o])
+        done("v", g.vector.tensor_copy(ap(o).bitcast(dt.uint32), ap(a).bitcast(dt.uint32).indirect(ap(f))), [a, f], [o])
+        o, a = W(dst + "_s", d0, d0 + n), W(src + "_s", 0, width)
+        act(o, a, Act.Copy, off=f)
+
+    def raw(w):
+        return ap(w).bitcast(dt.uint8) if LOG[w[0]][3] == CODES else ap(w)
+
+    def load(q, w, src, sem):
+        order(q, [], [w])
+        return done(q, queue[q].dma_start(ap(w), src), [], [w], sem, 16)
+
+    def move(q, out, a, sem):
+        order(q, [a], [out])
+        return done(q, queue[q].dma_start(raw(out), raw(a)), [a], [out], sem, 16)
+
+    def store(q, dst, a, sem):
+        order(q, [a], [])
+        return done(q, queue[q].dma_start(dst, raw(a)), [a], [], sem, 16)
+
+    peers = [c for c in T.cores if c != core]
+
+    def did(c):
+        a = topo.addr(c)
+        return DstId(rid=a[0], pnc=a[1])
+
+    def mask(engs):
+        m = 0
+        for e in engs:
+            m |= 1 << e
+        return m
+
+    def send(parts, sem, after=()):
+        order("g", [p[0] for p in parts], [])
+        for tok in after:
+            wait("g", tok)
+        g.remote_dma_fused([RemoteDMATransfer(dst_ids=[did(c) for c in cs], dma_engine_mask=mask(es), remote_sem=T.sem[sem],
+                                              srcs=[raw(a)], dsts=[raw(b)] * len(cs)) for a, b, cs, es in parts], local_sem=T.sem["ls"])
+        total["ls"] = total.get("ls", 0) + sum(len(p[3]) for p in parts)
+        record("g", [p[0] for p in parts], [], ("ls", total["ls"]))
+
+    def lands(sem, count, views):
+        total[sem] = count
+        record("r", [], views, (sem, count))
+
+    alle = topo.engines(core, peers[0])
+
+    load("y", W("ut", 0, 8), T.u[:, 0:8], "dl_u")
+    load("y", W("tbt", 0, 512), T.tb[:, 0:512], "dl_t0")
+    load("s", W("tbt", 512, 1024), T.tb[:, 512:1024], "dl_t1")
+
+    iota(W("pi", 0, 1), [[0, 1]], 0, 1)
+    iota(W("pi", 1, 2), [[0, 1]], 1, 1)
+    iota(W("pi", 2, 4), [[128, 2]], r, 1)
+    iota(W("jc"), [[128, 2]], 0, 1)
+    iota(W("rr"), [[1, 4], [0, 4]])
+    fill(W("ut", 8, 512), 0.0)
+    fill(W("ones"), 1.0)
+    order("g", [W("ones")], [W("idn")])
+    done("g", g.affine_select(ap(W("idn")), ap(W("ones")), [[-1, 128]], Op.is_equal, 0.0, 0, 1), [W("ones")], [W("idn")])
+    iota(W("kt"), [[16, 4], [0, 2], [1, 16]])
+    iota(W("kk", 0, 4), [[0, 2], [16, 2]])
+    iota(W("kk", 4, 6), [[16, 2]], 96)
+    iota(W("tr"), [[16, 8]], 512)
+    iota(W("ofrf"), [[2, 2], [0, 2]])
+
+    ts(W("ci", 0, 2), W("pi", 0, 2), 3, Op.bitwise_and)
+    ts(W("ci", 2, 3), W("pi", 0, 1), 15, Op.bitwise_and)
+    ts(W("ci", 3, 4), W("pi", 0, 1), 4, Op.arith_shift_right, 1, Op.bitwise_and)
+    ts(W("ci", 4, 6), W("pi", 2, 4), 255, Op.bitwise_and)
+    cp(W("cf", 0, 6), W("ci", 0, 6))
+    q0, q1, xf, gf, i1 = W("cf", 0, 1), W("cf", 1, 2), W("cf", 2, 3), W("cf", 3, 4), W("cf", 4, 6)
+    rr4 = W("rr", 0, 16, 4)
+    ts(W("wm", 0, 4), rr4, q0, Op.is_equal)
+    ts(W("wm", 4, 8), rr4, q0, Op.not_equal)
+    fill(W("exo0", 0, 2), 7)
+    fill(W("exo0", 2, 4), 15)
+    fill(W("exo1", 0, 2), 3)
+    fill(W("exo1", 2, 4), 7)
+    fill(W("jl"), 0.0)
+    fill(W("d0a"), 1.0)
+    fill(W("d0b"), 1.0)
+    fill(W("d0a", 0, 16, 8), 0.0)
+    fill(W("d0a", 4, 16, 8), -1.0)
+    fill(W("d0b", 0, 8, 4), 0.0)
+    fill(W("d0b", 1, 8, 4), -1.0)
+    cp(W("jl", 7, 16, 8), W("jc"))
+    fill(W("eb"), 0.0)
+
+    quant("uq", 0, "ut", 0, 128)
+    quant("tq", 0, "tbt", 0, 128)
+    mm(0, "tq", 0, "uq", 0)
+    quant("tq", 128, "tbt", 512, 128)
+    mm(1, "tq", 128, "uq", 0)
+    cp(W("l0", 4 * r, 4 * r + 2), W("pa", 0, 2))
+    cp(W("l0", 4 * r + 2, 4 * r + 4), W("pa", 512, 514), "s")
+    mine = W("l0", 4 * r, 4 * r + 4)
+    send([(mine, mine, peers, alle)], "a0")
+    lands("a0", 3 * len(alle), [W("l0", 4 * o, 4 * o + 4) for o in range(N) if o != r])
+
+    def near(n):
+        for a in range(4):
+            b = a ^ 1
+            cp(W(n, 64, 128, 1, 32 * a, 32 * a + 32), W(n, 0, 64, 1, 32 * b, 32 * b + 32))
+
+    def far(n):
+        cp(W(n, 128, 256, 1, 0, 64), W(n, 0, 128, 1, 64, 128), "s")
+        cp(W(n, 128, 256, 1, 64, 128), W(n, 0, 128, 1, 0, 64), "s")
+
+    act(W("jex"), W("jl"), Act.Abs, off=W("exo0"))
+    turn(W("jr", 0, 64), W("jex"))
+    near("jr")
+    far("jr")
+    if r:
+        cp(W("tbt", 1024, 1040), W("tbt", 0, 16))
+        quant("tz", 0, "tbt", 4 * r, 256)
+        mm(2, "tz", 0, "uq", 0)
+        mm(3, "tz", 128, "uq", 0)
+    for b in range(4):
+        cp(W("eb", 512 * b + b, 512 * b + 512, 4), W("idn"), "s")
+    for h in range(2):
+        ts(W("tri", 256 * h, 256 * h + 256), W("jr"), W("jc", h, h + 1), Op.is_ge)
+    if r:
+        mine = W("l1", 4 * r, 4 * r + 4)
+        cp(W("l1", 4 * r, 4 * r + 2), W("pa", 1024, 1026))
+        cp(W("l1", 4 * r + 2, 4 * r + 4), W("pa", 1536, 1538), "s")
+        send([(mine, mine, peers, alle)], "a1")
+    lands("a1", len(alle) * (3 if r == 0 else 2), [W("l1", 4 * o, 4 * o + 4) for o in range(1, N) if o != r])
+    iota(W("va"), [[0, 2], [1, 64]], R1)
+    iota(W("vb"), [[0, 2], [1, 64]], R2)
+    iota(W("fr", 0, 512), [[16, 16], [0, 2], [1, 16]])
+    for h in range(2):
+        ts(W("wmg", 4 * h, 4 * h + 4), rr4, q0, Op.not_equal)
+    ts(W("r9"), rr4, -9.0, Op.add)
+    for h in range(2):
+        tt(W("wl", 4 * h, 4 * h + 4), W("r9"), W("wmg", 0, 4), Op.mult)
+    ts(W("jp"), W("jc"), 2304.0, Op.add)
+    ts(W("kk"), W("kk"), xf, Op.add)
+    ts(W("ofrf"), W("ofrf"), gf, Op.add)
+    cp(W("kki"), W("kk"))
+    cp(W("ofr"), W("ofrf"))
+    fill(W("zt"), 0.0)
+    quant("tw", 320, "zt", 0, 128)
+    ready = [("sv", total["sv"])]
+    if r in BUILD[0]:
+        quant("eq", 0, "eb", 0, 512)
+        quant("psa", 0, "zt", 0, 128)
+        fill(W("h0"), 0.0)
+    order("y", [W("l0")], [])
+    load("y", W("wt"), T.w[:, 0:1024], "dl_w")
+
+    def roles():
+        ts(W("ma"), W("rr", 0, 12), q1, Op.is_lt)
+        ts(W("mb"), W("rr", 0, 12), q1, Op.is_ge)
+        ts(W("m0"), W("rr"), q1, Op.is_equal)
+        cp(W("rho", 0, 1), q1)
+        tt(W("rho", 1, 4), W("rr", 0, 12, 4), W("mb", 0, 12, 4), Op.add)
+        for h in range(2):
+            ts(W("cs", 4 * h, 4 * h + 4), W("rho"), W("jc", h, h + 1), Op.add)
+            ts(W("cs2", 4 * h, 4 * h + 4), W("rho"), 256.0, Op.mult)
+        cp(W("csi"), W("cs"))
+        ts(W("csj"), W("csi"), 255, Op.bitwise_and)
+        cp(W("csf"), W("csj"))
+        tt(W("csf"), W("csf"), W("cs2"), Op.add)
+        for h in range(2):
+            ts(W("wl1", 3 * h, 3 * h + 3), W("rho", 1, 4), -9.0, Op.add)
+        ts(W("cso"), i1, 256.0 * r, Op.add)
+        for h in range(2):
+            cp(W("pm", 65 * h + 64, 65 * h + 65), W("cf", 4 + h, 5 + h))
+        ts(W("tr"), W("tr"), xf, Op.add)
+        cp(W("tri32"), W("tr"))
+        fill(W("zf"), 0.0)
+        ts(W("zf"), W("zf"), q0, Op.add)
+        cp(W("ofu"), W("zf"))
+        ts(W("zf"), W("zf"), 4.0, Op.add)
+        cp(W("ofv"), W("zf"))
+        fill(W("fr", 512, 640), 0.0)
+    roles()
+
+    def count(t, gap1, gap2):
+        n = str(t)
+        src, off = (W("sc0"), W("exo0")) if t == 0 else (W("sc1", 0, 8), W("exo1"))
+        s2 = W("sc0", 7, 16, 8) if t == 0 else W("sc1", 3, 8, 4)
+        rn = "row" + n
+        act(W("sa" + n), s2, Act.Abs)
+        act(W("ex" + n), src, Act.Abs, off=off)
+        gap1()
+        for h in range(2):
+            s = W("sa" + n, h, h + 1)
+            ts(W("nd" + n, h, h + 1), s, 1.5 * 2.0 ** -24, Op.mult, s, Op.add)
+        for h in range(2):
+            ts(W("dl" + n, h, h + 1), W("nd" + n, h, h + 1), TINY, Op.max, W("sa" + n, h, h + 1), Op.subtract)
+        turn(W(rn, 0, 64), W("ex" + n))
+        near(rn)
+        for h in range(2):
+            act(W("xx" + n, 256 * h, 256 * h + 256), W("tri", 256 * h, 256 * h + 256), Act.Identity, scale=W("dl" + n, h, h + 1), bias=W("sa" + n, h, h + 1))
+        far(rn)
+        for c in (0, 128):
+            for h in range(2):
+                tt(W("cm" + n, 256 * h + c, 256 * h + c + 128), W(rn, c, c + 128), W("xx" + n, 256 * h + c, 256 * h + c + 128), Op.is_ge)
+        for h in range(2):
+            acc(W("po" + n, h, h + 1), W("cm" + n, 256 * h, 256 * h + 256))
+        gap2()
+
+    def listed(t, names, vals):
+        m, mt, lw, a, b, c = [x + str(t) for x in names]
+        for h in range(2):
+            ts(W(m, 128 * h, 128 * h + 128), W("kt"), W("po%d" % t, h, h + 1), Op.is_equal, W(vals, h, h + 1), Op.mult)
+        for h in range(2):
+            turn(W(mt, 128 * h, 128 * h + 128), W(m, 128 * h, 128 * h + 128))
+        for y in range(4):
+            acc(W(lw, y, y + 1), W(mt, 32 * y, 32 * y + 32))
+        for y in range(4):
+            red(W(lw, 4 + y, 5 + y), W(mt, 128 + 32 * y, 160 + 32 * y), Op.add)
+        tt(W(a), W(lw, 0, 4), W(lw, 4, 8), Op.add)
+        for k in range(4):
+            tt(W(b, 0, 4, 1, 32 * k, 32 * k + 32), W(a, 0, 4, 1, 32 * k, 32 * k + 32), W(a, 0, 4, 1, 32 * (k ^ 1), 32 * (k ^ 1) + 32), Op.add)
+        for k in range(2):
+            tt(W(c, 0, 4, 1, 64 * k, 64 * k + 64), W(b, 0, 4, 1, 64 * k, 64 * k + 64), W(b, 0, 4, 1, 64 - 64 * k, 128 - 64 * k), Op.add)
+        return W(c, 0, 4)
+
+    def lost(t, n, wl, parts):
+        k = n // 2
+        s = str(t)
+        src = "gm0" if t == 0 else "ga1"
+        if 0 in parts:
+            if t == 0:
+                tt(W("gm0"), W("ga0"), W("wmg"), Op.mult)
+            for h in range(2):
+                red(W("gx" + s, h, h + 1), W(src, k * h, k * h + k), Op.max)
+        if 1 in parts:
+            for h in range(2):
+                ts(W("ge" + s, k * h, k * h + k), W(src, k * h, k * h + k), W("gx" + s, h, h + 1), Op.is_equal)
+            tt(W("gw" + s, 0, n), W("ge" + s, 0, n), W(wl), Op.mult)
+        if 2 in parts:
+            for h in range(2):
+                red(W("gn" + s, h, h + 1), W("gw" + s, k * h, k * h + k), Op.min)
+            for h in range(2):
+                ts(W("pay" + s, h, h + 1), W("gn" + s, h, h + 1), 256.0, Op.mult, W("jp", h, h + 1), Op.add)
+
+    def gather(t, lists):
+        n = "ab"[t]
+        src, width = (("tq", 256), ("tw", 448))[t]
+        off = "off%d" % t
+        cp(W(off), lists)
+        sl, la = "sl" + n, "la" + n
+        bs = BUILD[t]
+        if r in bs:
+            d = bs.index(r)
+            o = 1 - d
+            pick(sl, 32 * o, src, width, off, 2 * o, 32)
+            to = T.cores[bs[o]]
+            for s in ("", "_s"):
+                send([(W(sl + s, 32 * o, 32 * o + 32), W(la + s, 32 * r, 32 * r + 32), [to], topo.engines(core, to))], "ha%d" % t, ready)
+            pick(la, 32 * r, src, width, off, 2 * d, 32)
+            cnt = 0
+            for i in range(N):
+                if i != r:
+                    cnt += 2 * len(topo.engines(T.cores[i], core)) // (1 if i in bs else 2)
+            lands("ha%d" % t, cnt, [W(la + s, 32 * i, 32 * i + 32) for s in ("", "_s") for i in range(N) if i != r])
+        else:
+            pick(sl, 0, src, width, off, 0, 64)
+            for s in ("", "_s"):
+                send([(W(sl + s, 32 * d, 32 * d + 32), W(la + s, 32 * r, 32 * r + 32), [T.cores[bs[d]]], topo.engines(core, T.cores[bs[d]])[d::2])
+                      for d in range(2)], "ha%d" % t, ready)
+
+    def buildlist(t):
+        s, d = str(t), BUILD[t].index(r)
+        wi = W("wi" + s, 2 * d, 2 * d + 2)
+        if t == 0:
+            ts(W("rq" + s), wi, 3, Op.bitwise_and)
+        else:
+            ts(W("ra" + s), wi, 1, Op.add)
+            ts(W("rq" + s), W("ra" + s), 3, Op.bitwise_and)
+        ts(W("rl" + s), wi, 8, Op.arith_shift_right)
+        a, b = W("ra" + s), W("rb" + s)
+        tt(a, W("rq" + s), W("rl" + s), Op.min)
+        tt(b, W("rq" + s), W("rl" + s), Op.max)
+        ts(W("rk" + s, 0, 2), W("rq" + s), 32, Op.mult)
+        ts(W("e1" + s), a, 0, Op.is_equal, 32, Op.mult)
+        ts(W("e2" + s), b, 1, Op.is_equal, 1, Op.add)
+        ts(W("e3" + s), b, 3, Op.is_equal, -32, Op.mult)
+        ts(W("e4" + s), a, 2, Op.is_equal, 1, Op.add)
+        tt(W("rk" + s, 2, 4), W("e1" + s), W("e2" + s), Op.mult)
+        tt(W("rk" + s, 4, 6), W("e3" + s), W("e4" + s), Op.mult)
+        tt(W("rf" + s), W("rk" + s), W("kki"), Op.add)
+        cp(W("rfo" + s), W("rf" + s))
+
+    def build(t):
+        s, n, d = str(t), "ab"[t], BUILD[t].index(r)
+        la, ps, hh = "la" + n, "ps" + n, "h" + s
+        pick(ps, 0, la, 128, "rfo" + s, 0, 96)
+        for b in range(4):
+            mm(4 + b, "eq", 128 * b, ps, 0)
+        at = 96 if d == 0 else 0
+        for b in range(4):
+            cp(W("xs", 64 * b, 64 * b + 64), W("pu", 512 * b + 32, 512 * b + 96), "s")
+
+        def first(b):
+            tt(W("xd", 32 * b, 32 * b + 32), W("pu", 512 * b, 512 * b + 32), W("xs", 64 * b, 64 * b + 32), Op.subtract)
+
+        def second(b):
+            tt(W(hh, 4 * at + b, 4 * at + 128, 4), W("xd", 32 * b, 32 * b + 32), W("xs", 64 * b + 32, 64 * b + 64), Op.subtract)
+        first(0)
+        for b in range(1, 4):
+            first(b)
+            second(b - 1)
+        second(3)
+        dst, base = ("tw", 256) if t == 0 else ("tx", 512)
+        quant(dst, base + 128 * d, hh, 0, 128)
+        c = base + 96 + 32 * d
+        for x in ("", "_s"):
+            v = W(dst + x, c, c + 32)
+            send([(v, v, peers, alle)], "hb%d" % t)
+
+    def built(t):
+        dst, base = ("tw", 256) if t == 0 else ("tx", 512)
+        lands("hb%d" % t, sum(2 * len(topo.engines(T.cores[b], core)) for b in BUILD[t] if b != r),
+              [W(dst + x, base + 96 + 32 * d, base + 128 + 32 * d) for x in ("", "_s") for d in range(2) if BUILD[t][d] != r])
+
+    def mapped(t):
+        s = str(t)
+        i = W("fi" + s)
+        if t == 0 or r == 0:
+            ts(i, W("wi" + s), 255, Op.bitwise_and)
+        else:
+            ts(W("fj" + s), W("wi" + s), r, Op.add)
+            ts(i, W("fj" + s), 255, Op.bitwise_and)
+        ts(W("fl" + s), W("wi" + s), 8, Op.arith_shift_right)
+        ts(W("fk" + s), i, 240, Op.bitwise_and)
+        ts(W("fm" + s), W("fl" + s), r, Op.is_equal)
+        tt(W("fa" + s, 0, 4), i, W("fk" + s), Op.add)
+        ts(W("fa" + s, 4, 8), W("fa" + s, 0, 4), 16, Op.add)
+        tt(W("fd" + s), W("fa" + s), W("tri32"), Op.subtract)
+        for c in (0, 4):
+            tt(W("fe" + s, c, c + 4), W("fd" + s, c, c + 4), W("fm" + s), Op.mult)
+        tt(W("fo" + s), W("fe" + s), W("tri32"), Op.add)
+        cp(W("ofs" + s), W("fo" + s))
+        win, off, src = W("fr"), W("ofs" + s), W("va" if t == 0 else "vb")
+        order("v", [off, src], [win])
+        done("v", g.vector.tensor_copy(ap(win).indirect(ap(off)), ap(src)), [off, src], [win])
+
+    def bsout(t):
+        s = str(t)
+        cp(W("bi" + s, 0, 64, 1, 0, 1), W("lr" + s, 0, 64, 1, 0, 1))
+        ts(W("bj" + s, 0, 64, 1, 0, 1), W("bi" + s, 0, 64, 1, 0, 1), 255, Op.bitwise_and)
+        ts(W("bj" + s, 64, 128, 1, 0, 1), W("bi" + s, 0, 64, 1, 0, 1), 8, Op.arith_shift_right)
+        cp(W("bsf" + s, 0, 128, 1, 0, 1), W("bj" + s, 0, 128, 1, 0, 1))
+        for i in range(2):
+            store("y", T.bs[2 * t + i:2 * t + i + 1, :], W("bsf" + s, 64 * i, 64 * i + 64, 1, 0, 1), "dbs%d" % t)
+
+    def listrow(t, w):
+        s = str(t)
+        act(W("er" + s), w, Act.Copy, off=W("ofr"))
+        turn(W("lr" + s), W("er" + s))
+
+    for h in range(2):
+        for m in range(2):
+            tt(W("sq0", 8 * h + 4 * m, 8 * h + 4 * m + 4), W("l0", 2 * h, 16, 4), W("wm", 4 * m, 4 * m + 4), Op.mult)
+    for h in range(2):
+        act(W("ga0", 4 * h, 4 * h + 4), W("l0", 2 * h + 1, 16, 4), Act.Abs)
+    scan(W("sc0"), W("d0a"), W("sq0"))
+    count(0, lambda: lost(0, 8, "wl", (0,)), lambda: lost(0, 8, "wl", (1,)))
+    gather(0, listed(0, ("mm", "mt", "lw", "aa", "ab", "ac"), "jc"))
+    lost(0, 8, "wl", (2,))
+    w0 = listed(0, ("nm", "nt", "nw", "na", "nb", "nc"), "pay0")
+    cp(W("wi0"), w0)
+    if r in BUILD[0]:
+        buildlist(0)
+    listrow(0, w0)
+    act(W("ub0"), W("ut"), Act.Copy, off=W("ofu"))
+    act(W("ub1"), W("ut"), Act.Copy, off=W("ofv"))
+
+    def keep():
+        cp(W("l1", 0, 4), W("l0", 0, 4))
+        tt(W("kra"), W("l1", 0, 12), W("ma"), Op.mult)
+        tt(W("krb"), W("l1", 4, 16), W("mb"), Op.mult)
+        tt(W("kro", 4, 16), W("kra"), W("krb"), Op.add)
+        tt(W("kr0"), W("l1"), W("m0"), Op.mult)
+        for h in range(2):
+            red(W("kro", 2 * h, 2 * h + 1), W("kr0", 2 * h, 16, 4), Op.add)
+
+    def hot():
+        for e in range(8):
+            ts(W("oh", 64 * e, 64 * e + 64), W("lr0"), W("csf", e, e + 1), Op.is_equal)
+        for e in range(8):
+            acc(W("rep", e, e + 1), W("oh", 64 * e, 64 * e + 64))
+        for h in range(2):
+            ts(W("oho", 64 * h, 64 * h + 64), W("lr0"), W("cso", h, h + 1), Op.is_equal)
+        for h in range(2):
+            tt(W("pm", 65 * h, 65 * h + 64), W("oho", 64 * h, 64 * h + 64), W("va", 0, 64), Op.mult)
+        for h in range(2):
+            red(W("src1", h, h + 1), W("pm", 65 * h, 65 * h + 65), Op.max)
+        ts(W("nrep"), W("rep"), -1.0, Op.mult, 1.0, Op.add)
+        for h in range(2):
+            tt(W("prc", 260 * h + 64, 260 * h + 260, 65), W("kro", 2 * h, 16, 4), W("nrep", 4 * h, 4 * h + 4), Op.mult)
+            tt(W("prg", 195 * h + 64, 195 * h + 195, 65), W("kro", 4 + 2 * h + 1, 16, 4), W("nrep", 4 * h + 1, 4 * h + 4), Op.mult)
+
+    def spare():
+        quant("tx", 0, "tbt", 0, 256)
+        quant("wq", 0, "wt", 0, 256)
+        if r in BUILD[1]:
+            quant("eq", 0, "eb", 0, 512)
+            quant("psb", 0, "zt", 0, 128)
+            fill(W("h1"), 0.0)
+
+    if r in BUILD[0]:
+        build(0)
+    keep()
+    hot()
+    quant("uc", 0, "ub0", 0, 128)
+    quant("ug", 0, "ub1", 0, 128)
+    quant("tw", 0, "tbt", 0, 256)
+    if r in BUILD[1]:
+        spare()
+        mapped(0)
+        bsout(0)
+    built(0)
+
+    mm(0, "uc", 0, "tw", 320)
+    mm(1, "ug", 0, "tw", 320)
+    for e in range(8):
+        tt(W("prc", 65 * e, 65 * e + 64), W("pa", 32, 96), W("oh", 64 * e, 64 * e + 64), Op.mult)
+        if e < 6:
+            acc(W("sqc", e, e + 1), W("prc", 65 * e, 65 * e + 65))
+    for e in (6, 7):
+        red(W("sqc", e, e + 1), W("prc", 65 * e, 65 * e + 65), Op.add)
+    scan(W("sc1", 0, 8), W("d0b"), W("sqc"))
+
+    def gs(es):
+        for e in es:
+            o = 64 * (4 * (e // 3) + e % 3 + 1)
+            tt(W("prg", 65 * e, 65 * e + 64), W("pa", 544, 608), W("oh", o, o + 64), Op.mult)
+
+    count(1, lambda: gs(range(3)), lambda: gs(range(3, 6)))
+    gather(1, listed(1, ("mm", "mt", "lw", "aa", "ab", "ac"), "src1"))
+    for e in range(6):
+        acc(W("gq", e, e + 1), W("prg", 65 * e, 65 * e + 65))
+    act(W("ga1", 0, 6), W("gq"), Act.Abs)
+    lost(1, 6, "wl1", (0, 1, 2))
+    w1 = listed(1, ("nm", "nt", "nw", "na", "nb", "nc"), "pay1")
+    cp(W("wi1"), w1)
+    if r in BUILD[1]:
+        buildlist(1)
+        build(1)
+    else:
+        spare()
+        mapped(0)
+    built(1)
+    for x in ("", "_s"):
+        move("y", W("tx" + x, R1, R1 + 64), W("tw" + x, R1, R1 + 64), "dl_x" + x)
+    mapped(1)
+    turn(W("ft"), W("fr", 0, 512))
+    cp(W("fou"), W("ft", 0, 512, 32))
+    if r in BUILD[0]:
+        bsout(0)
+    listrow(1, w1)
+    bsout(1)
+
+    for c in range(2):
+        pick("ou", 128 * c, "tx", 672, "fou", 8 * c, 128)
+        for o in range(2):
+            mm(2 * c + o, "wq", 128 * o, "ou", 128 * c)
+
+    def scales(ks):
+        for k in ks:
+            store("y", T.osc[4 * k:4 * k + 4, 0:256], W("ou_s", 0, 256, 1, 32 * k, 32 * k + 4), "doc")
+
+    store("y", T.oc[:, 0:1024], W("ou"), "doc")
+    scales((0, 1))
+    for c in range(2):
+        for o in range(2):
+            v = W("ys", 256 * o + 128 * c, 256 * o + 128 * c + 128)
+            cp(v, W("pa", 512 * (2 * c + o), 512 * (2 * c + o) + 128), "vs"[o])
+            store("ys"[o], T.y[:, 256 * o + 128 * c:256 * o + 128 * c + 128], v, "dy%d" % o)
+    scales((2, 3))
+    for s in sorted(total):
+        wait("g", (s, total[s]))

@@ -5,6 +5,7 @@ N, P, K = 4, 256, 64
 R1, R2 = 352, 608
 BUILD = ((0, 2), (1, 3))
 TINY = 2.0 ** -110
+UNIT = 4096.0
 
 F, B, I, U16, CODES = "float32", "bfloat16", "int32", "uint16", "float8_e4m3fn_x4"
 SCRATCH, LOG, _TOP = {}, {}, {}
@@ -14,6 +15,12 @@ def _own(dtype, **kw):
     for n, c in kw.items():
         SCRATCH[n] = ("sbuf", [128, c], dtype)
         LOG[n] = (n, 0, c, dtype)
+
+
+def _cube(**kw):
+    for n, (a, b) in kw.items():
+        SCRATCH[n] = ("sbuf", [128, a, b], F)
+        LOG[n] = (n, 0, a * b, F)
 
 
 def _slab(slab, dtype, **kw):
@@ -33,18 +40,18 @@ for _n in ("pa", "pu"):
     SCRATCH[_n] = ("psum", [128, 2048], F)
     LOG[_n] = (_n, 0, 2048, F)
 _own(F, ones=128, idn=128, l0=16, l1=16, xs=256, xd=128, ys=512, fr=640, ft=512)
-_slab("fs", F, jc=2, jp=2, cf=8, rr=16, wm=8, wl=8, wl1=6, wmg=8, r9=4, ma=12, mb=12, m0=16, rho=4, cs=8, cs2=8, csf=8, cso=2,
-      kk=6, tr=8, ofrf=4, zf=32, kt=128, va=128, vb=128, d0a=16, d0b=8,
-      jl=16, jex=64, jr=256, tri=512, oh=512, prc=520, prg=390, rep=8, nrep=8, kra=12, krb=12, kro=16, kr0=16, pm=130, src1=2,
+_cube(row0=(2, 128), row1=(2, 128), kt=(4, 32), mm0=(4, 64), mm1=(4, 64))
+_slab("fs", F, jc=2, jpa=2, jpc=2, jpb=2, cf=12, rr=16, rh=8, wm=16, wl=8, wl1=6, wmg=8, r9=4, ma=12, mb=12, m0=16, rho=4, cs=8, cs2=8,
+      csf=8, cso=2, gm=40, mrow=32, kk=6, tr=8, ofrf=4, zf=32, va=128, vb=128, d0a=8, d0b=8,
+      oh=512, prc=520, prg=390, rep=8, nrep=8, kra=12, krb=12, kro=16, kr0=16, pm=130, src1=2,
       oho=128, sqc=8, gq=6, junk=1024)
 for _t in "01":
-    _slab("fs", F, **{n + _t: c for n, c in dict(sq=16, sc=16, ex=64, sa=2, nd=2, dl=2, row=256, xx=512, cm=512, po=2, mm=256, mt=256,
-                                                 lw=8, aa=4, ab=4, ac=4, nm=256, nt=256, nw=8, na=4, nb=4, nc=8,
-                                                 ga=8, gm=8, gx=2, ge=8, gw=8, gn=2, pay=2, er=64, lr=64, bsf=128).items()})
-    _slab("is_", I, **{n + _t: c for n, c in dict(wi=4, rq=2, rl=2, ra=2, rb=2, e1=2, e2=2, e3=2, e4=2, rk=6, rf=6,
+    _slab("fs", F, **{n + _t: c for n, c in dict(sq=16, sc=16, ex=64, sa=2, nd=2, dl=2, th=80, cm=544, po=2, mt=256, lw=4, ab=4, ac=4,
+                                                 ga=8, gx=2, gy=8, ge=8, gw=8, gn=2, pay=2, er=64, lr=64, bsf=128).items()})
+    _slab("is_", I, **{n + _t: c for n, c in dict(wj=4, wi=4, rq=2, rl=2, ra=2, rb=2, e1=2, e2=2, e3=2, e4=2, rk=6, rf=6,
                                                   fi=4, fj=4, fk=4, fa=8, fl=4, fm=4, fd=8, fe=8, fo=8, bi=64, bj=128).items()})
     _slab("us", U16, **{n + _t: c for n, c in dict(off=4, rfo=6, ofs=8, exo=4).items()})
-_slab("is_", I, pi=4, ci=8, csi=8, csj=8, kki=6, tri32=8)
+_slab("is_", I, pi=4, ci=12, csi=8, csj=8, kki=6, tri32=8)
 _slab("us", U16, ofr=4, ofu=32, ofv=32, fou=16)
 
 SEMAPHORES = ["sv", "ss", "st", "sg", "dl_u", "dl_t0", "dl_t1", "dl_w", "dl_x", "dl_x_s", "dbs0", "dbs1", "dy0", "dy1", "doc", "ls",
@@ -56,6 +63,10 @@ def W(name, c0=0, c1=None, step=1, p0=0, p1=128):
     return (name, c0, LOG[name][2] if c1 is None else c1, step, p0, p1)
 
 
+def C(name, a0, a1, b0, b1, p0=0, p1=128):
+    return (name, 0, LOG[name][2], 1, p0, p1, (a0, a1, b0, b1))
+
+
 def rank_program(g, core, T, topo):
     r = T.rank_of(core)
     if r is None:
@@ -64,7 +75,10 @@ def rank_program(g, core, T, topo):
     total, known, snap, log = {}, {q: {} for q in queue}, {}, {}
 
     def ap(w):
-        n, c0, c1, st, p0, p1 = w
+        n, c0, c1, st, p0, p1 = w[:6]
+        if len(w) > 6:
+            a0, a1, b0, b1 = w[6]
+            return T[n][p0:p1, a0, b0:b1] if a1 == a0 + 1 else T[n][p0:p1, a0:a1, b0:b1]
         n, at = LOG[n][:2]
         c0, c1 = c0 + at, c1 + at
         return T[n][p0:p1, c0:c1] if st == 1 else T[n][p0:p1, c0:c1:st]
@@ -84,6 +98,9 @@ def rank_program(g, core, T, topo):
             return False
         if a[0] in ("pa", "pu"):
             return a[1] // 512 <= (b[2] - 1) // 512 and b[1] // 512 <= (a[2] - 1) // 512
+        if len(a) > 6 and len(b) > 6:
+            x, y = a[6], b[6]
+            return x[0] < y[1] and y[0] < x[1] and x[2] < y[3] and y[2] < x[3]
         if a[1] >= b[2] or b[1] >= a[2]:
             return False
         return not (a[3] == b[3] and a[3] > 1 and (a[1] - b[1]) % a[3])
@@ -144,16 +161,13 @@ def rank_program(g, core, T, topo):
         order("v", [d0, d1], [out])
         return done("v", g.vector.tensor_tensor_scan(ap(out), ap(d0), ap(d1), 0.0, Op.mult, Op.subtract), [d0, d1], [out])
 
-    def act(out, a, f, off=None, scale=None, bias=None, acc=None):
-        rd = [a] + [w for w in (off, scale, bias) if w is not None]
+    def act(out, a, f, off=None, acc=None):
+        rd = [a] + [w for w in (off,) if w is not None]
         wr = [out] + ([acc] if acc is not None else [])
         order("s", rd, wr)
         src = ap(a) if off is None else ap(a).indirect(ap(off))
-        kw = {}
-        if scale is not None: kw["scale"] = ap(scale)
-        if bias is not None: kw["bias"] = ap(bias)
-        if acc is not None: kw["accum_out"] = ap(acc)
-        return done("s", g.scalar.activation(ap(out), src, f, **kw), rd, wr)
+        ins = g.scalar.activation(ap(out), src, f) if acc is None else g.scalar.activation(ap(out), src, f, accum_out=ap(acc))
+        return done("s", ins, rd, wr)
 
     junk = [0]
 
@@ -239,38 +253,41 @@ def rank_program(g, core, T, topo):
     iota(W("pi", 2, 4), [[128, 2]], r, 1)
     iota(W("jc"), [[128, 2]], 0, 1)
     iota(W("rr"), [[1, 4], [0, 4]])
+    iota(W("rh"), [[1, 4], [0, 2]])
+    iota(W("mrow"), [[1, 32]])
     fill(W("ut", 8, 512), 0.0)
     fill(W("ones"), 1.0)
     order("g", [W("ones")], [W("idn")])
     done("g", g.affine_select(ap(W("idn")), ap(W("ones")), [[-1, 128]], Op.is_equal, 0.0, 0, 1), [W("ones")], [W("idn")])
-    iota(W("kt"), [[16, 4], [0, 2], [1, 16]])
+    for y in range(4):
+        iota(C("kt", y, y + 1, 0, 32), [[0, 2], [1, 16]], 16 * y)
     iota(W("kk", 0, 4), [[0, 2], [16, 2]])
     iota(W("kk", 4, 6), [[16, 2]], 96)
     iota(W("tr"), [[16, 8]], 512)
     iota(W("ofrf"), [[2, 2], [0, 2]])
 
+    fill(W("eb"), 0.0)
+    pp = W("pi", 0, 1)
     ts(W("ci", 0, 2), W("pi", 0, 2), 3, Op.bitwise_and)
-    ts(W("ci", 2, 3), W("pi", 0, 1), 15, Op.bitwise_and)
-    ts(W("ci", 3, 4), W("pi", 0, 1), 4, Op.arith_shift_right, 1, Op.bitwise_and)
+    ts(W("ci", 2, 3), pp, 15, Op.bitwise_and)
+    ts(W("ci", 3, 4), pp, 4, Op.arith_shift_right, 1, Op.bitwise_and)
     ts(W("ci", 4, 6), W("pi", 2, 4), 255, Op.bitwise_and)
-    cp(W("cf", 0, 6), W("ci", 0, 6))
+    ts(W("ci", 6, 7), pp, 31, Op.bitwise_and)
+    ts(W("ci", 7, 8), pp, 5, Op.arith_shift_right, 1, Op.bitwise_and)
+    ts(W("ci", 8, 9), pp, 6, Op.arith_shift_right)
+    fill(W("d0a"), 1.0)
+    fill(W("exo0", 0, 2), 14)
+    cp(W("cf", 0, 9), W("ci", 0, 9))
+    fill(W("exo0", 2, 4), 15)
+    fill(W("d0a", 0, 1), 0.0)
     q0, q1, xf, gf, i1 = W("cf", 0, 1), W("cf", 1, 2), W("cf", 2, 3), W("cf", 3, 4), W("cf", 4, 6)
     rr4 = W("rr", 0, 16, 4)
-    ts(W("wm", 0, 4), rr4, q0, Op.is_equal)
-    ts(W("wm", 4, 8), rr4, q0, Op.not_equal)
-    fill(W("exo0", 0, 2), 7)
-    fill(W("exo0", 2, 4), 15)
-    fill(W("exo1", 0, 2), 3)
-    fill(W("exo1", 2, 4), 7)
-    fill(W("jl"), 0.0)
-    fill(W("d0a"), 1.0)
-    fill(W("d0b"), 1.0)
-    fill(W("d0a", 0, 16, 8), 0.0)
-    fill(W("d0a", 4, 16, 8), -1.0)
-    fill(W("d0b", 0, 8, 4), 0.0)
-    fill(W("d0b", 1, 8, 4), -1.0)
-    cp(W("jl", 7, 16, 8), W("jc"))
-    fill(W("eb"), 0.0)
+    ts(W("wm", 0, 8), W("rh"), q0, Op.is_equal)
+    ts(W("wm", 8, 16), W("rh"), q0, Op.not_equal)
+    fill(W("d0a", 4, 5), -1.0)
+    fill(W("gm", 2, 3), 1.0)
+    ts(W("gm", 0, 2), W("cf", 7, 9), -1.0, Op.mult, 1.0, Op.add)
+    ts(W("gm", 3, 35), W("mrow"), W("cf", 6, 7), Op.is_ge)
 
     quant("uq", 0, "ut", 0, 128)
     quant("tq", 0, "tbt", 0, 128)
@@ -283,54 +300,47 @@ def rank_program(g, core, T, topo):
     send([(mine, mine, peers, alle)], "a0")
     lands("a0", 3 * len(alle), [W("l0", 4 * o, 4 * o + 4) for o in range(N) if o != r])
 
-    def near(n):
-        for a in range(4):
-            b = a ^ 1
-            cp(W(n, 64, 128, 1, 32 * a, 32 * a + 32), W(n, 0, 64, 1, 32 * b, 32 * b + 32))
-
-    def far(n):
-        cp(W(n, 128, 256, 1, 0, 64), W(n, 0, 128, 1, 64, 128), "s")
-        cp(W(n, 128, 256, 1, 64, 128), W(n, 0, 128, 1, 0, 64), "s")
-
-    act(W("jex"), W("jl"), Act.Abs, off=W("exo0"))
-    turn(W("jr", 0, 64), W("jex"))
-    near("jr")
-    far("jr")
     if r:
         cp(W("tbt", 1024, 1040), W("tbt", 0, 16))
         quant("tz", 0, "tbt", 4 * r, 256)
         mm(2, "tz", 0, "uq", 0)
         mm(3, "tz", 128, "uq", 0)
-    for b in range(4):
-        cp(W("eb", 512 * b + b, 512 * b + 512, 4), W("idn"), "s")
     for h in range(2):
-        ts(W("tri", 256 * h, 256 * h + 256), W("jr"), W("jc", h, h + 1), Op.is_ge)
+        ts(W("wmg", 4 * h, 4 * h + 4), rr4, q0, Op.not_equal)
+    ts(W("r9"), rr4, -9.0, Op.add)
     if r:
         mine = W("l1", 4 * r, 4 * r + 4)
         cp(W("l1", 4 * r, 4 * r + 2), W("pa", 1024, 1026))
         cp(W("l1", 4 * r + 2, 4 * r + 4), W("pa", 1536, 1538), "s")
         send([(mine, mine, peers, alle)], "a1")
     lands("a1", len(alle) * (3 if r == 0 else 2), [W("l1", 4 * o, 4 * o + 4) for o in range(1, N) if o != r])
+    fill(W("zf"), 0.0)
+    fill(W("zt"), 0.0)
+    ts(W("zf"), W("zf"), q0, Op.add)
+    for h in range(2):
+        tt(W("wl", 4 * h, 4 * h + 4), W("r9"), W("wmg", 0, 4), Op.mult)
+    cp(W("ofu"), W("zf"))
+    ts(W("zf"), W("zf"), 4.0, Op.add)
+    ts(W("jpc"), W("jc"), 1.0 / UNIT, Op.mult, 2304.0 / UNIT, Op.add)
+    quant("tw", 320, "zt", 0, 128)
+    cp(W("ofv"), W("zf"))
+    tt(W("jpa"), W("jc"), W("jpc"), Op.add)
+    ready = [("sv", total["sv"])]
+    for b in range(4):
+        cp(W("eb", 512 * b + b, 512 * b + 512, 4), W("idn"), "s")
+    act(W("ub0"), W("ut"), Act.Copy, off=W("ofu"))
+    act(W("ub1"), W("ut"), Act.Copy, off=W("ofv"))
     iota(W("va"), [[0, 2], [1, 64]], R1)
     iota(W("vb"), [[0, 2], [1, 64]], R2)
     iota(W("fr", 0, 512), [[16, 16], [0, 2], [1, 16]])
-    for h in range(2):
-        ts(W("wmg", 4 * h, 4 * h + 4), rr4, q0, Op.not_equal)
-    ts(W("r9"), rr4, -9.0, Op.add)
-    for h in range(2):
-        tt(W("wl", 4 * h, 4 * h + 4), W("r9"), W("wmg", 0, 4), Op.mult)
-    ts(W("jp"), W("jc"), 2304.0, Op.add)
     ts(W("kk"), W("kk"), xf, Op.add)
     ts(W("ofrf"), W("ofrf"), gf, Op.add)
-    cp(W("kki"), W("kk"))
-    cp(W("ofr"), W("ofrf"))
-    fill(W("zt"), 0.0)
-    quant("tw", 320, "zt", 0, 128)
-    ready = [("sv", total["sv"])]
     if r in BUILD[0]:
         quant("eq", 0, "eb", 0, 512)
         quant("psa", 0, "zt", 0, 128)
         fill(W("h0"), 0.0)
+    cp(W("kki"), W("kk"))
+    cp(W("ofr"), W("ofrf"))
     order("y", [W("l0")], [])
     load("y", W("wt"), T.w[:, 0:1024], "dl_w")
 
@@ -340,88 +350,108 @@ def rank_program(g, core, T, topo):
         ts(W("m0"), W("rr"), q1, Op.is_equal)
         cp(W("rho", 0, 1), q1)
         tt(W("rho", 1, 4), W("rr", 0, 12, 4), W("mb", 0, 12, 4), Op.add)
+        fill(W("d0b"), 1.0)
+        fill(W("exo1", 0, 2), 3)
         for h in range(2):
             ts(W("cs", 4 * h, 4 * h + 4), W("rho"), W("jc", h, h + 1), Op.add)
-            ts(W("cs2", 4 * h, 4 * h + 4), W("rho"), 256.0, Op.mult)
+        for h in range(2):
+            ts(W("cs2", 4 * h, 4 * h + 4), W("rho"), 256.0 / UNIT, Op.mult)
         cp(W("csi"), W("cs"))
+        fill(W("exo1", 2, 4), 7)
+        fill(W("d0b", 0, 8, 4), 0.0)
         ts(W("csj"), W("csi"), 255, Op.bitwise_and)
+        fill(W("d0b", 1, 8, 4), -1.0)
+
+    def roles2():
         cp(W("csf"), W("csj"))
-        tt(W("csf"), W("csf"), W("cs2"), Op.add)
         for h in range(2):
             ts(W("wl1", 3 * h, 3 * h + 3), W("rho", 1, 4), -9.0, Op.add)
-        ts(W("cso"), i1, 256.0 * r, Op.add)
+        ts(W("cso"), i1, 1.0 + 1.0 / UNIT, Op.mult, 256.0 * r / UNIT, Op.add)
+        ts(W("cs"), W("csf"), 1.0 + 1.0 / UNIT, Op.mult)
         for h in range(2):
             cp(W("pm", 65 * h + 64, 65 * h + 65), W("cf", 4 + h, 5 + h))
-        ts(W("tr"), W("tr"), xf, Op.add)
-        cp(W("tri32"), W("tr"))
-        fill(W("zf"), 0.0)
-        ts(W("zf"), W("zf"), q0, Op.add)
-        cp(W("ofu"), W("zf"))
-        ts(W("zf"), W("zf"), 4.0, Op.add)
-        cp(W("ofv"), W("zf"))
-        fill(W("fr", 512, 640), 0.0)
-    roles()
+        tt(W("csf"), W("cs"), W("cs2"), Op.add)
 
-    def count(t, gap1, gap2):
+    def keep():
+        cp(W("l1", 0, 4), W("l0", 0, 4))
+        tt(W("krb"), W("l1", 4, 16), W("mb"), Op.mult)
+        tt(W("kra"), W("l1", 0, 12), W("ma"), Op.mult)
+        tt(W("kr0"), W("l1"), W("m0"), Op.mult)
+        tt(W("kro", 4, 16), W("kra"), W("krb"), Op.add)
+        for h in range(2):
+            red(W("kro", 2 * h, 2 * h + 1), W("kr0", 2 * h, 16, 4), Op.add)
+
+    def count(t, early, late, last):
         n = str(t)
         src, off = (W("sc0"), W("exo0")) if t == 0 else (W("sc1", 0, 8), W("exo1"))
-        s2 = W("sc0", 7, 16, 8) if t == 0 else W("sc1", 3, 8, 4)
-        rn = "row" + n
+        s2 = W("sc0", 14, 16) if t == 0 else W("sc1", 3, 8, 4)
+        rn, th, cm = "row" + n, "th" + n, "cm" + n
         act(W("sa" + n), s2, Act.Abs)
         act(W("ex" + n), src, Act.Abs, off=off)
-        gap1()
+        early()
         for h in range(2):
             s = W("sa" + n, h, h + 1)
             ts(W("nd" + n, h, h + 1), s, 1.5 * 2.0 ** -24, Op.mult, s, Op.add)
         for h in range(2):
+            turn(C(rn, h, h + 1, 0, 32), W("ex" + n, 32 * h, 32 * h + 32))
+        for h in range(2):
             ts(W("dl" + n, h, h + 1), W("nd" + n, h, h + 1), TINY, Op.max, W("sa" + n, h, h + 1), Op.subtract)
-        turn(W(rn, 0, 64), W("ex" + n))
-        near(rn)
+        for a in range(4):
+            b = a ^ 1
+            cp(C(rn, 0, 2, 32, 64, 32 * a, 32 * a + 32), C(rn, 0, 2, 0, 32, 32 * b, 32 * b + 32), "v" if a < 2 else "s")
         for h in range(2):
-            act(W("xx" + n, 256 * h, 256 * h + 256), W("tri", 256 * h, 256 * h + 256), Act.Identity, scale=W("dl" + n, h, h + 1), bias=W("sa" + n, h, h + 1))
-        far(rn)
-        for c in (0, 128):
-            for h in range(2):
-                tt(W("cm" + n, 256 * h + c, 256 * h + c + 128), W(rn, c, c + 128), W("xx" + n, 256 * h + c, 256 * h + c + 128), Op.is_ge)
+            ts(W(th, 40 * h, 40 * h + 35), W("gm", 0, 35), W("dl" + n, h, h + 1), Op.mult, W("sa" + n, h, h + 1), Op.add)
+        for a in range(2):
+            cp(C(rn, 0, 2, 64, 128, 64 * a, 64 * a + 64), C(rn, 0, 2, 0, 64, 64 - 64 * a, 128 - 64 * a), "s")
         for h in range(2):
-            acc(W("po" + n, h, h + 1), W("cm" + n, 256 * h, 256 * h + 256))
-        gap2()
+            tt(W(cm, 272 * h + 232, 272 * h + 264), C(rn, h, h + 1, 0, 32), W(th, 40 * h + 3, 40 * h + 35), Op.is_ge)
+        for h in range(2):
+            ts(W(cm, 272 * h + 200, 272 * h + 232), C(rn, h, h + 1, 32, 64), W(th, 40 * h, 40 * h + 1), Op.is_ge)
+        for h in range(2):
+            acc(W(cm, 272 * h + 192, 272 * h + 193), W(cm, 272 * h + 200, 272 * h + 264))
+        late()
+        for h in range(2):
+            other = W(th, 2, 3) if h == 0 else W("sa" + n, 1, 2)
+            ts(W(cm, 272 * h, 272 * h + 128), C(rn, 1 - h, 2 - h, 0, 128), other, Op.is_ge)
+            ts(W(cm, 272 * h + 128, 272 * h + 192), C(rn, h, h + 1, 64, 128), W(th, 40 * h + 1, 40 * h + 2), Op.is_ge)
+        for h in range(2):
+            acc(W("po" + n, h, h + 1), W(cm, 272 * h, 272 * h + 193))
+        last()
 
-    def listed(t, names, vals):
-        m, mt, lw, a, b, c = [x + str(t) for x in names]
+    def listed(t):
+        m, mt, lw, b, c = [x + str(t) for x in ("mm", "mt", "lw", "ab", "ac")]
         for h in range(2):
-            ts(W(m, 128 * h, 128 * h + 128), W("kt"), W("po%d" % t, h, h + 1), Op.is_equal, W(vals, h, h + 1), Op.mult)
-        for h in range(2):
-            turn(W(mt, 128 * h, 128 * h + 128), W(m, 128 * h, 128 * h + 128))
-        for y in range(4):
-            acc(W(lw, y, y + 1), W(mt, 32 * y, 32 * y + 32))
-        for y in range(4):
-            red(W(lw, 4 + y, 5 + y), W(mt, 128 + 32 * y, 160 + 32 * y), Op.add)
-        tt(W(a), W(lw, 0, 4), W(lw, 4, 8), Op.add)
+            ts(C(m, 0, 4, 32 * h, 32 * h + 32), C("kt", 0, 4, 0, 32), W("po%d" % t, h, h + 1), Op.is_equal, W("pay%d" % t, h, h + 1), Op.mult)
+        for y in (2, 3, 0, 1):
+            turn(W(mt, 64 * y, 64 * y + 64), C(m, y, y + 1, 0, 64))
+        for y in (2, 3):
+            acc(W(lw, y, y + 1), W(mt, 64 * y, 64 * y + 64))
+        for y in (0, 1):
+            red(W(lw, y, y + 1), W(mt, 64 * y, 64 * y + 64), Op.add)
         for k in range(4):
-            tt(W(b, 0, 4, 1, 32 * k, 32 * k + 32), W(a, 0, 4, 1, 32 * k, 32 * k + 32), W(a, 0, 4, 1, 32 * (k ^ 1), 32 * (k ^ 1) + 32), Op.add)
+            tt(W(b, 0, 4, 1, 32 * k, 32 * k + 32), W(lw, 0, 4, 1, 32 * k, 32 * k + 32), W(lw, 0, 4, 1, 32 * (k ^ 1), 32 * (k ^ 1) + 32), Op.add)
         for k in range(2):
             tt(W(c, 0, 4, 1, 64 * k, 64 * k + 64), W(b, 0, 4, 1, 64 * k, 64 * k + 64), W(b, 0, 4, 1, 64 - 64 * k, 128 - 64 * k), Op.add)
         return W(c, 0, 4)
 
-    def lost(t, n, wl, parts):
+    def lost(t, n, wl, base, parts):
         k = n // 2
         s = str(t)
-        src = "gm0" if t == 0 else "ga1"
+        src = "gy0" if t == 0 else "ga1"
         if 0 in parts:
             if t == 0:
-                tt(W("gm0"), W("ga0"), W("wmg"), Op.mult)
+                tt(W("gy0"), W("ga0"), W("wmg"), Op.mult)
             for h in range(2):
                 red(W("gx" + s, h, h + 1), W(src, k * h, k * h + k), Op.max)
-        if 1 in parts:
             for h in range(2):
                 ts(W("ge" + s, k * h, k * h + k), W(src, k * h, k * h + k), W("gx" + s, h, h + 1), Op.is_equal)
+        if 1 in parts:
             tt(W("gw" + s, 0, n), W("ge" + s, 0, n), W(wl), Op.mult)
         if 2 in parts:
             for h in range(2):
                 red(W("gn" + s, h, h + 1), W("gw" + s, k * h, k * h + k), Op.min)
             for h in range(2):
-                ts(W("pay" + s, h, h + 1), W("gn" + s, h, h + 1), 256.0, Op.mult, W("jp", h, h + 1), Op.add)
+                ts(W("pay" + s, h, h + 1), W("gn" + s, h, h + 1), 256.0 / UNIT, Op.mult, W(base, h, h + 1), Op.add)
 
     def gather(t, lists):
         n = "ab"[t]
@@ -449,22 +479,28 @@ def rank_program(g, core, T, topo):
                 send([(W(sl + s, 32 * d, 32 * d + 32), W(la + s, 32 * r, 32 * r + 32), [T.cores[bs[d]]], topo.engines(core, T.cores[bs[d]])[d::2])
                       for d in range(2)], "ha%d" % t, ready)
 
+    def numbers(t, w):
+        s = str(t)
+        ts(W("wj" + s), w, UNIT, Op.mult)
+        ts(W("wi" + s), W("wj" + s), 1023, Op.bitwise_and)
+
     def buildlist(t):
         s, d = str(t), BUILD[t].index(r)
         wi = W("wi" + s, 2 * d, 2 * d + 2)
         if t == 0:
+            ts(W("rl" + s), wi, 8, Op.arith_shift_right)
             ts(W("rq" + s), wi, 3, Op.bitwise_and)
         else:
             ts(W("ra" + s), wi, 1, Op.add)
+            ts(W("rl" + s), wi, 8, Op.arith_shift_right)
             ts(W("rq" + s), W("ra" + s), 3, Op.bitwise_and)
-        ts(W("rl" + s), wi, 8, Op.arith_shift_right)
         a, b = W("ra" + s), W("rb" + s)
-        tt(a, W("rq" + s), W("rl" + s), Op.min)
         tt(b, W("rq" + s), W("rl" + s), Op.max)
+        tt(a, W("rq" + s), W("rl" + s), Op.min)
         ts(W("rk" + s, 0, 2), W("rq" + s), 32, Op.mult)
-        ts(W("e1" + s), a, 0, Op.is_equal, 32, Op.mult)
         ts(W("e2" + s), b, 1, Op.is_equal, 1, Op.add)
         ts(W("e3" + s), b, 3, Op.is_equal, -32, Op.mult)
+        ts(W("e1" + s), a, 0, Op.is_equal, 32, Op.mult)
         ts(W("e4" + s), a, 2, Op.is_equal, 1, Op.add)
         tt(W("rk" + s, 2, 4), W("e1" + s), W("e2" + s), Op.mult)
         tt(W("rk" + s, 4, 6), W("e3" + s), W("e4" + s), Op.mult)
@@ -506,14 +542,18 @@ def rank_program(g, core, T, topo):
     def mapped(t):
         s = str(t)
         i = W("fi" + s)
+        ts(W("fl" + s), W("wi" + s), 8, Op.arith_shift_right)
         if t == 0 or r == 0:
             ts(i, W("wi" + s), 255, Op.bitwise_and)
         else:
             ts(W("fj" + s), W("wi" + s), r, Op.add)
             ts(i, W("fj" + s), 255, Op.bitwise_and)
-        ts(W("fl" + s), W("wi" + s), 8, Op.arith_shift_right)
-        ts(W("fk" + s), i, 240, Op.bitwise_and)
+        if t == 0:
+            ts(W("tr"), W("tr"), xf, Op.add)
+            fill(W("fr", 512, 640), 0.0)
+            cp(W("tri32"), W("tr"))
         ts(W("fm" + s), W("fl" + s), r, Op.is_equal)
+        ts(W("fk" + s), i, 240, Op.bitwise_and)
         tt(W("fa" + s, 0, 4), i, W("fk" + s), Op.add)
         ts(W("fa" + s, 4, 8), W("fa" + s, 0, 4), 16, Op.add)
         tt(W("fd" + s), W("fa" + s), W("tri32"), Op.subtract)
@@ -521,15 +561,17 @@ def rank_program(g, core, T, topo):
             tt(W("fe" + s, c, c + 4), W("fd" + s, c, c + 4), W("fm" + s), Op.mult)
         tt(W("fo" + s), W("fe" + s), W("tri32"), Op.add)
         cp(W("ofs" + s), W("fo" + s))
-        win, off, src = W("fr"), W("ofs" + s), W("va" if t == 0 else "vb")
+
+    def enter(t):
+        win, off, src = W("fr"), W("ofs%d" % t), W("va" if t == 0 else "vb")
         order("v", [off, src], [win])
         done("v", g.vector.tensor_copy(ap(win).indirect(ap(off)), ap(src)), [off, src], [win])
 
     def bsout(t):
         s = str(t)
-        cp(W("bi" + s, 0, 64, 1, 0, 1), W("lr" + s, 0, 64, 1, 0, 1))
+        ts(W("bi" + s, 0, 64, 1, 0, 1), W("lr" + s, 0, 64, 1, 0, 1), UNIT, Op.mult)
         ts(W("bj" + s, 0, 64, 1, 0, 1), W("bi" + s, 0, 64, 1, 0, 1), 255, Op.bitwise_and)
-        ts(W("bj" + s, 64, 128, 1, 0, 1), W("bi" + s, 0, 64, 1, 0, 1), 8, Op.arith_shift_right)
+        ts(W("bj" + s, 64, 128, 1, 0, 1), W("bi" + s, 0, 64, 1, 0, 1), 8, Op.arith_shift_right, 3, Op.bitwise_and)
         cp(W("bsf" + s, 0, 128, 1, 0, 1), W("bj" + s, 0, 128, 1, 0, 1))
         for i in range(2):
             store("y", T.bs[2 * t + i:2 * t + i + 1, :], W("bsf" + s, 64 * i, 64 * i + 64, 1, 0, 1), "dbs%d" % t)
@@ -539,31 +581,19 @@ def rank_program(g, core, T, topo):
         act(W("er" + s), w, Act.Copy, off=W("ofr"))
         turn(W("lr" + s), W("er" + s))
 
-    for h in range(2):
-        for m in range(2):
-            tt(W("sq0", 8 * h + 4 * m, 8 * h + 4 * m + 4), W("l0", 2 * h, 16, 4), W("wm", 4 * m, 4 * m + 4), Op.mult)
+    for m in range(2):
+        tt(W("sq0", 8 * m, 8 * m + 8), W("l0", 0, 16, 2), W("wm", 8 * m, 8 * m + 8), Op.mult)
     for h in range(2):
         act(W("ga0", 4 * h, 4 * h + 4), W("l0", 2 * h + 1, 16, 4), Act.Abs)
-    scan(W("sc0"), W("d0a"), W("sq0"))
-    count(0, lambda: lost(0, 8, "wl", (0,)), lambda: lost(0, 8, "wl", (1,)))
-    gather(0, listed(0, ("mm", "mt", "lw", "aa", "ab", "ac"), "jc"))
-    lost(0, 8, "wl", (2,))
-    w0 = listed(0, ("nm", "nt", "nw", "na", "nb", "nc"), "pay0")
-    cp(W("wi0"), w0)
+    for h in range(2):
+        scan(W("sc0", h, 16, 2), W("d0a"), W("sq0", h, 16, 2))
+    count(0, lambda: lost(0, 8, "wl", "jpa", (0,)), lambda: lost(0, 8, "wl", "jpa", (1,)), lambda: lost(0, 8, "wl", "jpa", (2,)))
+    w0 = listed(0)
+    gather(0, w0)
+    numbers(0, w0)
     if r in BUILD[0]:
         buildlist(0)
     listrow(0, w0)
-    act(W("ub0"), W("ut"), Act.Copy, off=W("ofu"))
-    act(W("ub1"), W("ut"), Act.Copy, off=W("ofv"))
-
-    def keep():
-        cp(W("l1", 0, 4), W("l0", 0, 4))
-        tt(W("kra"), W("l1", 0, 12), W("ma"), Op.mult)
-        tt(W("krb"), W("l1", 4, 16), W("mb"), Op.mult)
-        tt(W("kro", 4, 16), W("kra"), W("krb"), Op.add)
-        tt(W("kr0"), W("l1"), W("m0"), Op.mult)
-        for h in range(2):
-            red(W("kro", 2 * h, 2 * h + 1), W("kr0", 2 * h, 16, 4), Op.add)
 
     def hot():
         for e in range(8):
@@ -577,6 +607,7 @@ def rank_program(g, core, T, topo):
         for h in range(2):
             red(W("src1", h, h + 1), W("pm", 65 * h, 65 * h + 65), Op.max)
         ts(W("nrep"), W("rep"), -1.0, Op.mult, 1.0, Op.add)
+        tt(W("jpb"), W("src1"), W("jpc"), Op.add)
         for h in range(2):
             tt(W("prc", 260 * h + 64, 260 * h + 260, 65), W("kro", 2 * h, 16, 4), W("nrep", 4 * h, 4 * h + 4), Op.mult)
             tt(W("prg", 195 * h + 64, 195 * h + 195, 65), W("kro", 4 + 2 * h + 1, 16, 4), W("nrep", 4 * h + 1, 4 * h + 4), Op.mult)
@@ -589,52 +620,63 @@ def rank_program(g, core, T, topo):
             quant("psb", 0, "zt", 0, 128)
             fill(W("h1"), 0.0)
 
-    if r in BUILD[0]:
-        build(0)
-    keep()
-    hot()
     quant("uc", 0, "ub0", 0, 128)
     quant("ug", 0, "ub1", 0, 128)
+    roles()
+    if r in BUILD[0]:
+        build(0)
+    roles2()
+    keep()
+    hot()
     quant("tw", 0, "tbt", 0, 256)
     if r in BUILD[1]:
         spare()
         mapped(0)
+        enter(0)
         bsout(0)
     built(0)
 
     mm(0, "uc", 0, "tw", 320)
     mm(1, "ug", 0, "tw", 320)
-    for e in range(8):
-        tt(W("prc", 65 * e, 65 * e + 64), W("pa", 32, 96), W("oh", 64 * e, 64 * e + 64), Op.mult)
-        if e < 6:
-            acc(W("sqc", e, e + 1), W("prc", 65 * e, 65 * e + 65))
-    for e in (6, 7):
-        red(W("sqc", e, e + 1), W("prc", 65 * e, 65 * e + 65), Op.add)
-    scan(W("sc1", 0, 8), W("d0b"), W("sqc"))
 
-    def gs(es):
+    def gnow(es):
         for e in es:
             o = 64 * (4 * (e // 3) + e % 3 + 1)
             tt(W("prg", 65 * e, 65 * e + 64), W("pa", 544, 608), W("oh", o, o + 64), Op.mult)
 
-    count(1, lambda: gs(range(3)), lambda: gs(range(3, 6)))
-    gather(1, listed(1, ("mm", "mt", "lw", "aa", "ab", "ac"), "src1"))
-    for e in range(6):
-        acc(W("gq", e, e + 1), W("prg", 65 * e, 65 * e + 65))
-    act(W("ga1", 0, 6), W("gq"), Act.Abs)
-    lost(1, 6, "wl1", (0, 1, 2))
-    w1 = listed(1, ("nm", "nt", "nw", "na", "nb", "nc"), "pay1")
-    cp(W("wi1"), w1)
+    for e in range(8):
+        tt(W("prc", 65 * e, 65 * e + 64), W("pa", 32, 96), W("oh", 64 * e, 64 * e + 64), Op.mult)
+        if e < 6:
+            acc(W("sqc", e, e + 1), W("prc", 65 * e, 65 * e + 65))
+    gnow((0, 1))
+    for e in (6, 7):
+        red(W("sqc", e, e + 1), W("prc", 65 * e, 65 * e + 65), Op.add)
+    gnow((2,))
+    scan(W("sc1", 0, 8), W("d0b"), W("sqc"))
+
+    def gsums():
+        gnow((3, 4, 5))
+        for e in range(6):
+            acc(W("gq", e, e + 1), W("prg", 65 * e, 65 * e + 65))
+        act(W("ga1", 0, 6), W("gq"), Act.Abs)
+
+    count(1, gsums, lambda: lost(1, 6, "wl1", "jpb", (0, 1)), lambda: lost(1, 6, "wl1", "jpb", (2,)))
+    w1 = listed(1)
+    gather(1, w1)
+    numbers(1, w1)
     if r in BUILD[1]:
         buildlist(1)
+        mapped(1)
         build(1)
     else:
         spare()
         mapped(0)
+        enter(0)
+        mapped(1)
     built(1)
     for x in ("", "_s"):
         move("y", W("tx" + x, R1, R1 + 64), W("tw" + x, R1, R1 + 64), "dl_x" + x)
-    mapped(1)
+    enter(1)
     turn(W("ft"), W("fr", 0, 512))
     cp(W("fou"), W("ft", 0, 512, 32))
     if r in BUILD[0]:

@@ -41,20 +41,20 @@ for _n in ("pa", "pu"):
     LOG[_n] = (_n, 0, 2048, F)
 _own(F, ones=128, idn=128, l0=16, l1=16, xs=256, xd=128, ys=512, fr=640, ft=512)
 _cube(row0=(2, 128), row1=(2, 128), kt=(4, 32), mm0=(4, 64), mm1=(4, 64))
-_slab("fs", F, jc=2, jpa=2, jpc=2, jpb=2, cf=12, rr=16, rh=8, wm=16, wl=8, wl1=6, wmg=8, r9=4, ma=12, mb=12, m0=16, rho=4, cs=8, cs2=8,
+_slab("fs", F, jc=2, jpa=2, jpc=2, jpb=2, cf=12, rr=16, rh=8, wm=16, wl=8, wl1=6, wmg=4, r9=4, ma=12, mb=12, m0=16, rho=4, cs=8, cs2=8,
       csf=8, cso=2, gm=40, mrow=32, kk=6, tr=8, ofrf=4, zf=32, va=128, vb=128, d0a=8, d0b=8,
       oh=512, prc=520, prg=390, rep=8, nrep=8, kra=12, krb=12, kro=16, kr0=16, pm=130, src1=2,
-      oho=128, sqc=8, gq=6, junk=1024)
+      oho=128, sqc=8, gq=6, lr=128, bsf=256, junk=1024)
 for _t in "01":
     _slab("fs", F, **{n + _t: c for n, c in dict(sq=16, sc=16, ex=64, sa=2, nd=2, dl=2, th=80, cm=544, po=2, mt=256, lw=4, ab=4, ac=4,
-                                                 ga=8, gx=2, gy=8, ge=8, gw=8, gn=2, pay=2, er=64, lr=64, bsf=128).items()})
+                                                 ga=8, gx=2, gy=8, ge=8, gw=8, gn=2, pay=2, er=64).items()})
     _slab("is_", I, **{n + _t: c for n, c in dict(wj=4, wi=4, rq=2, rl=2, ra=2, rb=2, e1=2, e2=2, e3=2, e4=2, rk=6, rf=6,
-                                                  fi=4, fj=4, fk=4, fa=8, fl=4, fm=4, fd=8, fe=8, fo=8, bi=64, bj=128).items()})
+                                                  fi=4, fj=4, fk=4, fa=8, fl=4, fm=4, fd=8, fe=8, fo=8).items()})
     _slab("us", U16, **{n + _t: c for n, c in dict(off=4, rfo=6, ofs=8, exo=4).items()})
-_slab("is_", I, pi=4, ci=12, csi=8, csj=8, kki=6, tri32=8)
+_slab("is_", I, bi=128, bj=256, pi=4, ci=12, csi=8, csj=8, kki=6, tri32=8)
 _slab("us", U16, ofr=4, ofu=32, ofv=32, fou=16)
 
-SEMAPHORES = ["sv", "ss", "st", "sg", "dl_u", "dl_t0", "dl_t1", "dl_w", "dl_x", "dl_x_s", "dbs0", "dbs1", "dy0", "dy1", "doc", "ls",
+SEMAPHORES = ["sv", "ss", "st", "sg", "dl_u", "dl_t0", "dl_t1", "dl_w", "dl_x", "dl_x_s", "dbs", "dy0", "dy1", "doc", "ls",
               "a0", "a1", "ha0", "ha1", "hb0", "hb1"]
 _QS = {"v": "sv", "s": "ss", "t": "st", "g": "sg"}
 
@@ -129,11 +129,31 @@ def rank_program(g, core, T, topo):
         record(q, reads, writes, tok)
         return tok
 
+    held = []
+
+    def listof(f, *args):
+        held.append([])
+        f(*args)
+        return held.pop()
+
+    def run(calls):
+        for c in calls:
+            c[0](*c[1:])
+
+    def weave(a, b):
+        for i in range(len(a)):
+            run(a[i:i + 1] + b[i:i + 1])
+        return b[len(a):]
+
     def tt(out, a, b, op):
+        if held:
+            return held[-1].append((tt, out, a, b, op))
         order("v", [a, b], [out])
         return done("v", g.vector.tensor_tensor(ap(out), ap(a), ap(b), op), [a, b], [out])
 
     def ts(out, a, s1, op0, s2=None, op1=None):
+        if held:
+            return held[-1].append((ts, out, a, s1, op0, s2, op1))
         rd = [a] + [s for s in (s1, s2) if isinstance(s, tuple)]
         order("v", rd, [out])
         x1, x2 = [ap(s) if isinstance(s, tuple) else s for s in (s1, s2)]
@@ -141,15 +161,21 @@ def rank_program(g, core, T, topo):
         return done("v", ins, rd, [out])
 
     def cp(out, a, q="v"):
+        if held:
+            return held[-1].append((cp, out, a, q))
         order(q, [a], [out])
         ins = g.vector.tensor_copy(ap(out), ap(a)) if q == "v" else g.scalar.activation(ap(out), ap(a), Act.Copy)
         return done(q, ins, [a], [out])
 
     def red(out, a, op):
+        if held:
+            return held[-1].append((red, out, a, op))
         order("v", [a], [out])
         return done("v", g.vector.tensor_reduce(ap(out), ap(a), AxisListType.X, op), [a], [out])
 
     def fill(out, c):
+        if held:
+            return held[-1].append((fill, out, c))
         order("v", [], [out])
         return done("v", g.vector.memset(ap(out), c), [], [out])
 
@@ -294,10 +320,16 @@ def rank_program(g, core, T, topo):
     mm(0, "tq", 0, "uq", 0)
     quant("tq", 128, "tbt", 512, 128)
     mm(1, "tq", 128, "uq", 0)
-    cp(W("l0", 4 * r, 4 * r + 2), W("pa", 0, 2))
-    cp(W("l0", 4 * r + 2, 4 * r + 4), W("pa", 512, 514), "s")
-    mine = W("l0", 4 * r, 4 * r + 4)
-    send([(mine, mine, peers, alle)], "a0")
+
+    def mine(l, bank):
+        for h in range(2):
+            o = 512 * (bank + h)
+            cp(W(l, 4 * r + 2 * h, 4 * r + 2 * h + 1), W("pa", o, o + 1), "s")
+            act(W(l, 4 * r + 2 * h + 1, 4 * r + 2 * h + 2), W("pa", o + 1, o + 2), Act.Abs)
+        v = W(l, 4 * r, 4 * r + 4)
+        send([(v, v, peers, alle)], "a" + l[1])
+
+    mine("l0", 0)
     lands("a0", 3 * len(alle), [W("l0", 4 * o, 4 * o + 4) for o in range(N) if o != r])
 
     if r:
@@ -305,20 +337,15 @@ def rank_program(g, core, T, topo):
         quant("tz", 0, "tbt", 4 * r, 256)
         mm(2, "tz", 0, "uq", 0)
         mm(3, "tz", 128, "uq", 0)
-    for h in range(2):
-        ts(W("wmg", 4 * h, 4 * h + 4), rr4, q0, Op.not_equal)
-    ts(W("r9"), rr4, -9.0, Op.add)
-    if r:
-        mine = W("l1", 4 * r, 4 * r + 4)
-        cp(W("l1", 4 * r, 4 * r + 2), W("pa", 1024, 1026))
-        cp(W("l1", 4 * r + 2, 4 * r + 4), W("pa", 1536, 1538), "s")
-        send([(mine, mine, peers, alle)], "a1")
+        mine("l1", 2)
     lands("a1", len(alle) * (3 if r == 0 else 2), [W("l1", 4 * o, 4 * o + 4) for o in range(1, N) if o != r])
+    ts(W("wmg"), rr4, q0, Op.not_equal)
+    ts(W("r9"), rr4, -9.0, Op.add)
     fill(W("zf"), 0.0)
     fill(W("zt"), 0.0)
     ts(W("zf"), W("zf"), q0, Op.add)
     for h in range(2):
-        tt(W("wl", 4 * h, 4 * h + 4), W("r9"), W("wmg", 0, 4), Op.mult)
+        tt(W("wl", 4 * h, 4 * h + 4), W("r9"), W("wmg"), Op.mult)
     cp(W("ofu"), W("zf"))
     ts(W("zf"), W("zf"), 4.0, Op.add)
     ts(W("jpc"), W("jc"), 1.0 / UNIT, Op.mult, 2304.0 / UNIT, Op.add)
@@ -335,45 +362,43 @@ def rank_program(g, core, T, topo):
     iota(W("fr", 0, 512), [[16, 16], [0, 2], [1, 16]])
     ts(W("kk"), W("kk"), xf, Op.add)
     ts(W("ofrf"), W("ofrf"), gf, Op.add)
-    if r in BUILD[0]:
-        quant("eq", 0, "eb", 0, 512)
-        quant("psa", 0, "zt", 0, 128)
-        fill(W("h0"), 0.0)
+    when = 0 if r in BUILD[0] else 1
+    quant("eq", 0, "eb", 0, 512)
+    quant(("psa", "psb")[when], 0, "zt", 0, 128)
+    fill(W(("h0", "h1")[when]), 0.0)
     cp(W("kki"), W("kk"))
     cp(W("ofr"), W("ofrf"))
+    quant("tw", 0, "tbt", 0, 256)
     order("y", [W("l0")], [])
     load("y", W("wt"), T.w[:, 0:1024], "dl_w")
 
-    def roles():
-        ts(W("ma"), W("rr", 0, 12), q1, Op.is_lt)
-        ts(W("mb"), W("rr", 0, 12), q1, Op.is_ge)
-        ts(W("m0"), W("rr"), q1, Op.is_equal)
-        cp(W("rho", 0, 1), q1)
-        tt(W("rho", 1, 4), W("rr", 0, 12, 4), W("mb", 0, 12, 4), Op.add)
-        fill(W("d0b"), 1.0)
-        fill(W("exo1", 0, 2), 3)
-        for h in range(2):
-            ts(W("cs", 4 * h, 4 * h + 4), W("rho"), W("jc", h, h + 1), Op.add)
-        for h in range(2):
-            ts(W("cs2", 4 * h, 4 * h + 4), W("rho"), 256.0 / UNIT, Op.mult)
-        cp(W("csi"), W("cs"))
-        fill(W("exo1", 2, 4), 7)
-        fill(W("d0b", 0, 8, 4), 0.0)
-        ts(W("csj"), W("csi"), 255, Op.bitwise_and)
-        fill(W("d0b", 1, 8, 4), -1.0)
+    ts(W("ma"), W("rr", 0, 12), q1, Op.is_lt)
+    ts(W("mb"), W("rr", 0, 12), q1, Op.is_ge)
+    ts(W("m0"), W("rr"), q1, Op.is_equal)
+    cp(W("rho", 0, 1), q1)
+    tt(W("rho", 1, 4), W("rr", 0, 12, 4), W("mb", 0, 12, 4), Op.add)
+    fill(W("d0b"), 1.0)
+    fill(W("exo1", 0, 2), 3)
+    for h in range(2):
+        ts(W("cs", 4 * h, 4 * h + 4), W("rho"), W("jc", h, h + 1), Op.add)
+    for h in range(2):
+        ts(W("cs2", 4 * h, 4 * h + 4), W("rho"), 256.0 / UNIT, Op.mult)
+    cp(W("csi"), W("cs"))
+    fill(W("exo1", 2, 4), 7)
+    fill(W("d0b", 0, 8, 4), 0.0)
+    ts(W("csj"), W("csi"), 255, Op.bitwise_and)
+    fill(W("d0b", 1, 8, 4), -1.0)
 
-    def roles2():
+    def before():
         cp(W("csf"), W("csj"))
+        cp(W("l1", 0, 4), W("l0", 0, 4))
         for h in range(2):
             ts(W("wl1", 3 * h, 3 * h + 3), W("rho", 1, 4), -9.0, Op.add)
-        ts(W("cso"), i1, 1.0 + 1.0 / UNIT, Op.mult, 256.0 * r / UNIT, Op.add)
         ts(W("cs"), W("csf"), 1.0 + 1.0 / UNIT, Op.mult)
+        ts(W("cso"), i1, 1.0 + 1.0 / UNIT, Op.mult, 256.0 * r / UNIT, Op.add)
         for h in range(2):
             cp(W("pm", 65 * h + 64, 65 * h + 65), W("cf", 4 + h, 5 + h))
         tt(W("csf"), W("cs"), W("cs2"), Op.add)
-
-    def keep():
-        cp(W("l1", 0, 4), W("l0", 0, 4))
         tt(W("krb"), W("l1", 4, 16), W("mb"), Op.mult)
         tt(W("kra"), W("l1", 0, 12), W("ma"), Op.mult)
         tt(W("kr0"), W("l1"), W("m0"), Op.mult)
@@ -437,15 +462,15 @@ def rank_program(g, core, T, topo):
     def lost(t, n, wl, base, parts):
         k = n // 2
         s = str(t)
-        src = "gy0" if t == 0 else "ga1"
+
+        def size(h):
+            return W("gy0", h, 8, 2) if t == 0 else W("ga1", k * h, k * h + k)
         if 0 in parts:
-            if t == 0:
-                tt(W("gy0"), W("ga0"), W("wmg"), Op.mult)
             for h in range(2):
-                red(W("gx" + s, h, h + 1), W(src, k * h, k * h + k), Op.max)
-            for h in range(2):
-                ts(W("ge" + s, k * h, k * h + k), W(src, k * h, k * h + k), W("gx" + s, h, h + 1), Op.is_equal)
+                red(W("gx" + s, h, h + 1), size(h), Op.max)
         if 1 in parts:
+            for h in range(2):
+                ts(W("ge" + s, k * h, k * h + k), size(h), W("gx" + s, h, h + 1), Op.is_equal)
             tt(W("gw" + s, 0, n), W("ge" + s, 0, n), W(wl), Op.mult)
         if 2 in parts:
             for h in range(2):
@@ -567,41 +592,29 @@ def rank_program(g, core, T, topo):
         order("v", [off, src], [win])
         done("v", g.vector.tensor_copy(ap(win).indirect(ap(off)), ap(src)), [off, src], [win])
 
-    def bsout(t):
-        s = str(t)
-        ts(W("bi" + s, 0, 64, 1, 0, 1), W("lr" + s, 0, 64, 1, 0, 1), UNIT, Op.mult)
-        ts(W("bj" + s, 0, 64, 1, 0, 1), W("bi" + s, 0, 64, 1, 0, 1), 255, Op.bitwise_and)
-        ts(W("bj" + s, 64, 128, 1, 0, 1), W("bi" + s, 0, 64, 1, 0, 1), 8, Op.arith_shift_right, 3, Op.bitwise_and)
-        cp(W("bsf" + s, 0, 128, 1, 0, 1), W("bj" + s, 0, 128, 1, 0, 1))
-        for i in range(2):
-            store("y", T.bs[2 * t + i:2 * t + i + 1, :], W("bsf" + s, 64 * i, 64 * i + 64, 1, 0, 1), "dbs%d" % t)
-
     def listrow(t, w):
         s = str(t)
         act(W("er" + s), w, Act.Copy, off=W("ofr"))
-        turn(W("lr" + s), W("er" + s))
+        turn(W("lr", 64 * t, 64 * t + 64), W("er" + s))
 
     for m in range(2):
         tt(W("sq0", 8 * m, 8 * m + 8), W("l0", 0, 16, 2), W("wm", 8 * m, 8 * m + 8), Op.mult)
-    for h in range(2):
-        act(W("ga0", 4 * h, 4 * h + 4), W("l0", 2 * h + 1, 16, 4), Act.Abs)
+    tt(W("gy0"), W("l0", 1, 16, 2), W("wm", 8, 16), Op.mult)
     for h in range(2):
         scan(W("sc0", h, 16, 2), W("d0a"), W("sq0", h, 16, 2))
-    count(0, lambda: lost(0, 8, "wl", "jpa", (0,)), lambda: lost(0, 8, "wl", "jpa", (1,)), lambda: lost(0, 8, "wl", "jpa", (2,)))
+    lost(0, 8, "wl", "jpa", (0,))
+    count(0, lambda: lost(0, 8, "wl", "jpa", (1,)), lambda: None, lambda: lost(0, 8, "wl", "jpa", (2,)))
     w0 = listed(0)
     gather(0, w0)
     numbers(0, w0)
-    if r in BUILD[0]:
-        buildlist(0)
-    listrow(0, w0)
 
     def hot():
         for e in range(8):
-            ts(W("oh", 64 * e, 64 * e + 64), W("lr0"), W("csf", e, e + 1), Op.is_equal)
+            ts(W("oh", 64 * e, 64 * e + 64), W("lr", 0, 64), W("csf", e, e + 1), Op.is_equal)
         for e in range(8):
             acc(W("rep", e, e + 1), W("oh", 64 * e, 64 * e + 64))
         for h in range(2):
-            ts(W("oho", 64 * h, 64 * h + 64), W("lr0"), W("cso", h, h + 1), Op.is_equal)
+            ts(W("oho", 64 * h, 64 * h + 64), W("lr", 0, 64), W("cso", h, h + 1), Op.is_equal)
         for h in range(2):
             tt(W("pm", 65 * h, 65 * h + 64), W("oho", 64 * h, 64 * h + 64), W("va", 0, 64), Op.mult)
         for h in range(2):
@@ -615,25 +628,21 @@ def rank_program(g, core, T, topo):
     def spare():
         quant("tx", 0, "tbt", 0, 256)
         quant("wq", 0, "wt", 0, 256)
-        if r in BUILD[1]:
-            quant("eq", 0, "eb", 0, 512)
-            quant("psb", 0, "zt", 0, 128)
-            fill(W("h1"), 0.0)
 
+    if r in BUILD[0]:
+        rest = weave(listof(buildlist, 0), listof(before))
+        listrow(0, w0)
+        build(0)
+    else:
+        listrow(0, w0)
+        rest = weave(listof(mapped, 0), listof(before))
     quant("uc", 0, "ub0", 0, 128)
     quant("ug", 0, "ub1", 0, 128)
-    roles()
-    if r in BUILD[0]:
-        build(0)
-    roles2()
-    keep()
+    run(rest)
     hot()
-    quant("tw", 0, "tbt", 0, 256)
     if r in BUILD[1]:
         spare()
-        mapped(0)
         enter(0)
-        bsout(0)
     built(0)
 
     mm(0, "uc", 0, "tw", 320)
@@ -643,6 +652,8 @@ def rank_program(g, core, T, topo):
         for e in es:
             o = 64 * (4 * (e // 3) + e % 3 + 1)
             tt(W("prg", 65 * e, 65 * e + 64), W("pa", 544, 608), W("oh", o, o + 64), Op.mult)
+        for e in es:
+            acc(W("gq", e, e + 1), W("prg", 65 * e, 65 * e + 65))
 
     for e in range(8):
         tt(W("prc", 65 * e, 65 * e + 64), W("pa", 32, 96), W("oh", 64 * e, 64 * e + 64), Op.mult)
@@ -656,8 +667,6 @@ def rank_program(g, core, T, topo):
 
     def gsums():
         gnow((3, 4, 5))
-        for e in range(6):
-            acc(W("gq", e, e + 1), W("prg", 65 * e, 65 * e + 65))
         act(W("ga1", 0, 6), W("gq"), Act.Abs)
 
     count(1, gsums, lambda: lost(1, 6, "wl1", "jpb", (0, 1)), lambda: lost(1, 6, "wl1", "jpb", (2,)))
@@ -665,29 +674,29 @@ def rank_program(g, core, T, topo):
     gather(1, w1)
     numbers(1, w1)
     if r in BUILD[1]:
-        buildlist(1)
-        mapped(1)
+        rest = weave(listof(buildlist, 1), listof(mapped, 1))
         build(1)
+        run(rest)
     else:
         spare()
-        mapped(0)
+        run(weave(listof(mapped, 0), listof(mapped, 1)))
         enter(0)
-        mapped(1)
     built(1)
     for x in ("", "_s"):
         move("y", W("tx" + x, R1, R1 + 64), W("tw" + x, R1, R1 + 64), "dl_x" + x)
     enter(1)
     turn(W("ft"), W("fr", 0, 512))
     cp(W("fou"), W("ft", 0, 512, 32))
-    if r in BUILD[0]:
-        bsout(0)
     listrow(1, w1)
-    bsout(1)
 
     for c in range(2):
         pick("ou", 128 * c, "tx", 672, "fou", 8 * c, 128)
         for o in range(2):
             mm(2 * c + o, "wq", 128 * o, "ou", 128 * c)
+    ts(W("bi", 0, 128, 1, 0, 1), W("lr", 0, 128, 1, 0, 1), UNIT, Op.mult)
+    for t in range(2):
+        ts(W("bj", 128 * t, 128 * t + 64, 1, 0, 1), W("bi", 64 * t, 64 * t + 64, 1, 0, 1), 255, Op.bitwise_and)
+        ts(W("bj", 128 * t + 64, 128 * t + 128, 1, 0, 1), W("bi", 64 * t, 64 * t + 64, 1, 0, 1), 8, Op.arith_shift_right, 3, Op.bitwise_and)
 
     def scales(ks):
         for k in ks:
@@ -700,6 +709,9 @@ def rank_program(g, core, T, topo):
             v = W("ys", 256 * o + 128 * c, 256 * o + 128 * c + 128)
             cp(v, W("pa", 512 * (2 * c + o), 512 * (2 * c + o) + 128), "vs"[o])
             store("ys"[o], T.y[:, 256 * o + 128 * c:256 * o + 128 * c + 128], v, "dy%d" % o)
+        if c == 0:
+            cp(W("bsf", 0, 256, 1, 0, 1), W("bj", 0, 256, 1, 0, 1))
     scales((2, 3))
+    store("y", T.bs[:, :], W("bsf", 0, 256, 1, 0, 1), "dbs")
     for s in sorted(total):
         wait("g", (s, total[s]))

@@ -5,7 +5,8 @@ N, P, K = 4, 256, 64
 R1, R2 = 352, 608
 BUILD = ((0, 2), (1, 3))
 TINY = 2.0 ** -110
-UNIT = 4096.0
+UNIT = 32768.0
+TUNE = dict(wake=150.0, fac=1.2, load=900.0, issue=60.0, rissue=250.0, hop=700.0, row=12.0, byte=0.06, tol=20.0, bias=60.0)
 
 F, B, I, U16, CODES = "float32", "bfloat16", "int32", "uint16", "float8_e4m3fn_x4"
 SCRATCH, LOG, _TOP = {}, {}, {}
@@ -31,7 +32,7 @@ def _slab(slab, dtype, **kw):
         SCRATCH[slab] = ("sbuf", [128, _TOP[slab]], dtype)
 
 
-_own(B, tbt=1040, ut=512, wt=1024, zt=512, eb=2048, ub0=512, ub1=512, h0=512, h1=512)
+_own(B, onb=512, tbt=1040, ut=512, wt=1024, eb=2048, ub0=512, ub1=512, h0=512, h1=512)
 for _n, _c in dict(tq=256, tw=512, tx=768, uq=128, uc=128, ug=128, eq=512, wq=256, tz=256, sla=64, slb=64,
                    laa=128, lab=128, psa=128, psb=128, ou=256).items():
     _own(CODES, **{_n: _c})
@@ -39,24 +40,24 @@ for _n, _c in dict(tq=256, tw=512, tx=768, uq=128, uc=128, ug=128, eq=512, wq=25
 for _n in ("pa", "pu"):
     SCRATCH[_n] = ("psum", [128, 2048], F)
     LOG[_n] = (_n, 0, 2048, F)
-_own(F, ones=128, idn=128, l0=16, l1=16, xs=256, xd=128, ys=512, fr=640, ft=512)
+_own(F, l0=16, l1=16, xs=256, xd=128, ys=512, fr=640, ft=512)
 _cube(row0=(2, 128), row1=(2, 128), kt=(4, 32), mm0=(4, 64), mm1=(4, 64))
-_slab("fs", F, jc=2, jpa=2, jpc=2, jpb=2, cf=12, rr=16, rh=8, wm=16, wl=8, wl1=6, wmg=4, r9=4, ma=12, mb=12, m0=16, rho=4, cs=8, cs2=8,
-      csf=8, cso=2, gm=40, mrow=32, kk=6, tr=8, ofrf=4, zf=32, va=128, vb=128, d0a=8, d0b=8,
-      oh=512, prc=520, prg=390, rep=8, nrep=8, kra=12, krb=12, kro=16, kr0=16, pm=130, src1=2,
-      oho=128, sqc=8, gq=6, lr=128, bsf=256, junk=1024)
+_slab("fs", F, jc=2, jp0=2, jp1=2, jp2=2, jpb=2, cf=12, rr=16, rh=8, rk8=8, wm=16, nq=8, ca=8, cb=8, c1=8, c2=8, c3=8, c4=8,
+      s1=8, s2=8, s3=8, s4=8, s5=8, wl=8, wa=3, wb=1, wc=1, wd=3, wl1=6, ma=12, mb=12, m0=16, rho=4, csf=8, cso=2, gm=40, mrow=32,
+      kf=2, kg=2, tr=8, ofrf=4, va=128, vb=128, d0a=8, d0b=8, oh=512, prc=520, prg=390, rep=8, nrep=8, kra=12, krb=12, kro=16, kr0=16,
+      pm=130, src1=2, oho=128, sqc=8, gq=6, lr=128, bsf=256, junk=4096)
 for _t in "01":
     _slab("fs", F, **{n + _t: c for n, c in dict(sq=16, sc=16, ex=64, sa=2, nd=2, dl=2, th=80, cm=544, po=2, mt=256, lw=4, ab=4, ac=4,
                                                  ga=8, gx=2, gy=8, ge=8, gw=8, gn=2, pay=2, er=64).items()})
-    _slab("is_", I, **{n + _t: c for n, c in dict(wj=4, wi=4, rq=2, rl=2, ra=2, rb=2, e1=2, e2=2, e3=2, e4=2, rk=6, rf=6,
-                                                  fi=4, fj=4, fk=4, fa=8, fl=4, fm=4, fd=8, fe=8, fo=8).items()})
+    _slab("is_", I, **{n + _t: c for n, c in dict(wj=4, rk=6, fi=4, fj=4, fk=4, fa=8, fl=4, fm=4, fe=4, fo=8).items()})
     _slab("us", U16, **{n + _t: c for n, c in dict(off=4, rfo=6, ofs=8, exo=4).items()})
-_slab("is_", I, bi=128, bj=256, pi=4, ci=12, csi=8, csj=8, kki=6, tri32=8)
+_slab("is_", I, bi=128, key=64, bj=256, ji=2, jj=2, pi=4, ci=12, csi=8, csj=8, tri32=8)
 _slab("us", U16, ofr=4, ofu=32, ofv=32, fou=16)
 
-SEMAPHORES = ["sv", "ss", "st", "sg", "dl_u", "dl_t0", "dl_t1", "dl_w", "dl_x", "dl_x_s", "dbs", "dy0", "dy1", "doc", "ls",
-              "a0", "a1", "ha0", "ha1", "hb0", "hb1"]
+SEMAPHORES = ["sv", "ss", "st", "sg", "dl_u", "dl_t0", "dl_t1", "dl_t2", "dl_w", "dl_x", "dl_x_s", "dl_m", "dl_m_s", "dl_n", "dl_n_s",
+              "dbs", "dy0", "dy1", "doc", "ls", "a0", "a1", "ha0", "ha1", "hb0", "hb1"]
 _QS = {"v": "sv", "s": "ss", "t": "st", "g": "sg"}
+_PLANS = {}
 
 
 def W(name, c0=0, c1=None, step=1, p0=0, p1=128):
@@ -67,187 +68,119 @@ def C(name, a0, a1, b0, b1, p0=0, p1=128):
     return (name, 0, LOG[name][2], 1, p0, p1, (a0, a1, b0, b1))
 
 
-def rank_program(g, core, T, topo):
-    r = T.rank_of(core)
-    if r is None:
-        return
-    queue = {"v": g.vector, "s": g.scalar, "t": g.tensor, "g": g, "y": g.sync}
-    total, known, snap, log = {}, {q: {} for q in queue}, {}, {}
+def width(w):
+    if len(w) > 6:
+        a0, a1, b0, b1 = w[6]
+        return (a1 - a0) * (b1 - b0)
+    return len(range(w[1], w[2], w[3]))
 
-    def ap(w):
-        n, c0, c1, st, p0, p1 = w[:6]
-        if len(w) > 6:
-            a0, a1, b0, b1 = w[6]
-            return T[n][p0:p1, a0, b0:b1] if a1 == a0 + 1 else T[n][p0:p1, a0:a1, b0:b1]
-        n, at = LOG[n][:2]
-        c0, c1 = c0 + at, c1 + at
-        return T[n][p0:p1, c0:c1] if st == 1 else T[n][p0:p1, c0:c1:st]
 
-    def wait(q, tok):
-        s, v = tok
-        if known[q].get(s, 0) >= v:
-            return
-        queue[q].wait_ge(T.sem[s], v)
-        known[q][s] = v
-        for a, b in snap.get(tok, {}).items():
-            if known[q].get(a, 0) < b:
-                known[q][a] = b
+def meet(a, b):
+    if a[4] >= b[5] or b[4] >= a[5]:
+        return False
+    if a[0] in ("pa", "pu"):
+        return a[1] // 512 <= (b[2] - 1) // 512 and b[1] // 512 <= (a[2] - 1) // 512
+    if len(a) > 6 and len(b) > 6:
+        x, y = a[6], b[6]
+        return x[0] < y[1] and y[0] < x[1] and x[2] < y[3] and y[2] < x[3]
+    if a[1] >= b[2] or b[1] >= a[2]:
+        return False
+    return not (a[3] == b[3] and a[3] > 1 and (a[1] - b[1]) % a[3])
 
-    def meet(a, b):
-        if a[4] >= b[5] or b[4] >= a[5]:
-            return False
-        if a[0] in ("pa", "pu"):
-            return a[1] // 512 <= (b[2] - 1) // 512 and b[1] // 512 <= (a[2] - 1) // 512
-        if len(a) > 6 and len(b) > 6:
-            x, y = a[6], b[6]
-            return x[0] < y[1] and y[0] < x[1] and x[2] < y[3] and y[2] < x[3]
-        if a[1] >= b[2] or b[1] >= a[2]:
-            return False
-        return not (a[3] == b[3] and a[3] > 1 and (a[1] - b[1]) % a[3])
 
-    def order(q, reads, writes):
-        need = {}
-        for ws, isw in ((reads, False), (writes, True)):
-            for w in ws:
-                for w2, isw2, tok, q2 in log.get(w[0], ()):
-                    if (isw or isw2 or (w[0] in ("pa", "pu") and q != q2)) and meet(w, w2):
-                        need[tok[0]] = max(need.get(tok[0], 0), tok[1])
-        for s in sorted(need):
-            wait(q, (s, need[s]))
+def calls(r, cores, topo):
+    core = cores[r]
+    nodes = []
+    cyc = 0.83 * TUNE["fac"]
 
-    def record(q, reads, writes, tok):
-        for ws, isw in ((reads, False), (writes, True)):
-            for w in ws:
-                log.setdefault(w[0], []).append((w, isw, tok, q))
+    def node(rd, wr, fns, cost, sem=None, by=1, lag=0.0, after=(), to=(), cast=False):
+        nodes.append(dict(rd=rd, wr=wr, fns=fns, cost=cost, sem=sem, by=by, lag=lag, after=list(after), to=to, cast=cast, i=len(nodes)))
+        return nodes[-1]
 
-    def done(q, ins, reads, writes, sem=None, by=1):
-        s = sem or _QS[q]
-        total[s] = total.get(s, 0) + by
-        ins.then_inc(T.sem[s], by)
-        tok = (s, total[s])
-        snap[tok] = dict(known[q])
-        record(q, reads, writes, tok)
-        return tok
-
-    held = []
-
-    def listof(f, *args):
-        held.append([])
-        f(*args)
-        return held.pop()
-
-    def run(calls):
-        for c in calls:
-            c[0](*c[1:])
-
-    def weave(a, b):
-        for i in range(len(a)):
-            run(a[i:i + 1] + b[i:i + 1])
-        return b[len(a):]
+    def small(n):
+        return max(64, n) * cyc
 
     def tt(out, a, b, op):
-        if held:
-            return held[-1].append((tt, out, a, b, op))
-        order("v", [a, b], [out])
-        return done("v", g.vector.tensor_tensor(ap(out), ap(a), ap(b), op), [a, b], [out])
+        both = a[0] not in ("pa", "pu") and b[0] not in ("pa", "pu")
+        return node([a, b], [out], {"v": lambda e: e["v"].tensor_tensor(e["ap"](out), e["ap"](a), e["ap"](b), op)},
+                    {"v": small(width(out) * (2 if both else 1))})
 
     def ts(out, a, s1, op0, s2=None, op1=None):
-        if held:
-            return held[-1].append((ts, out, a, s1, op0, s2, op1))
         rd = [a] + [s for s in (s1, s2) if isinstance(s, tuple)]
-        order("v", rd, [out])
-        x1, x2 = [ap(s) if isinstance(s, tuple) else s for s in (s1, s2)]
-        ins = g.vector.tensor_scalar(ap(out), ap(a), x1, x2, op0, op1) if op1 is not None else g.vector.tensor_scalar(ap(out), ap(a), x1, None, op0)
-        return done("v", ins, rd, [out])
+
+        def f(e):
+            x1, x2 = [e["ap"](s) if isinstance(s, tuple) else s for s in (s1, s2)]
+            if op1 is not None:
+                return e["v"].tensor_scalar(e["ap"](out), e["ap"](a), x1, x2, op0, op1)
+            return e["v"].tensor_scalar(e["ap"](out), e["ap"](a), x1, None, op0)
+        return node(rd, [out], {"v": f}, {"v": small(width(out))})
 
     def cp(out, a, q="v"):
-        if held:
-            return held[-1].append((cp, out, a, q))
-        order(q, [a], [out])
-        ins = g.vector.tensor_copy(ap(out), ap(a)) if q == "v" else g.scalar.activation(ap(out), ap(a), Act.Copy)
-        return done(q, ins, [a], [out])
+        fns = {"v": lambda e: e["v"].tensor_copy(e["ap"](out), e["ap"](a)), "s": lambda e: e["s"].activation(e["ap"](out), e["ap"](a), Act.Copy)}
+        return node([a], [out], {x: fns[x] for x in q}, {x: small(width(out)) for x in q})
 
     def red(out, a, op):
-        if held:
-            return held[-1].append((red, out, a, op))
-        order("v", [a], [out])
-        return done("v", g.vector.tensor_reduce(ap(out), ap(a), AxisListType.X, op), [a], [out])
+        return node([a], [out], {"v": lambda e: e["v"].tensor_reduce(e["ap"](out), e["ap"](a), AxisListType.X, op)}, {"v": small(width(a))})
 
     def fill(out, c):
-        if held:
-            return held[-1].append((fill, out, c))
-        order("v", [], [out])
-        return done("v", g.vector.memset(ap(out), c), [], [out])
+        return node([], [out], {"v": lambda e: e["v"].memset(e["ap"](out), c)}, {"v": small(width(out) * (0.5 if LOG[out[0]][3] in (B, U16) else 1))})
 
     def turn(out, a):
-        order("v", [a], [out])
-        return done("v", g.vector.transpose(ap(out), ap(a)), [a], [out])
+        return node([a], [out], {"v": lambda e: e["v"].transpose(e["ap"](out), e["ap"](a))}, {"v": small(width(a))})
 
     def scan(out, d0, d1):
-        order("v", [d0, d1], [out])
-        return done("v", g.vector.tensor_tensor_scan(ap(out), ap(d0), ap(d1), 0.0, Op.mult, Op.subtract), [d0, d1], [out])
+        return node([d0, d1], [out], {"v": lambda e: e["v"].tensor_tensor_scan(e["ap"](out), e["ap"](d0), e["ap"](d1), 0.0, Op.mult, Op.subtract)},
+                    {"v": small(width(out))})
 
-    def act(out, a, f, off=None, acc=None):
+    def act(out, a, f, off=None):
         rd = [a] + [w for w in (off,) if w is not None]
-        wr = [out] + ([acc] if acc is not None else [])
-        order("s", rd, wr)
-        src = ap(a) if off is None else ap(a).indirect(ap(off))
-        ins = g.scalar.activation(ap(out), src, f) if acc is None else g.scalar.activation(ap(out), src, f, accum_out=ap(acc))
-        return done("s", ins, rd, wr)
+        n = width(out)
+        return node(rd, [out], {"s": lambda e: e["s"].activation(e["ap"](out), e["ap"](a) if off is None else e["ap"](a).indirect(e["ap"](off)), f)},
+                    {"s": small(n) if off is None else (65 + 1.56 * 0.83 * n) * TUNE["fac"]})
 
     junk = [0]
 
-    def acc(out, a):
-        n = a[2] - a[1]
-        if junk[0] + n > 1024:
-            junk[0] = 0
+    def total(out, a, q="vs"):
+        n = width(a)
         j = W("junk", junk[0], junk[0] + n)
         junk[0] += n
-        return act(j, a, Act.Copy, acc=out)
+        fns = {"v": lambda e: e["v"].tensor_reduce(e["ap"](out), e["ap"](a), AxisListType.X, Op.add),
+               "s": lambda e: e["s"].activation(e["ap"](j), e["ap"](a), Act.Copy, accum_out=e["ap"](out))}
+        return node([a], [out, j], {x: fns[x] for x in q}, {x: small(n) + (20 if x == "s" else 0) for x in q})
 
     def iota(out, pattern, base=0, cm=0):
-        order("g", [], [out])
         kw = {} if LOG[out[0]][3] == I else {"allow_small_or_imprecise_dtypes": True}
-        return done("g", g.iota(ap(out), pattern, base, cm, **kw), [], [out])
+        return node([], [out], {"g": lambda e: e["g"].iota(e["ap"](out), pattern, base, cm, **kw)}, {"g": 130 * TUNE["fac"] + 2 * cyc * width(out)})
 
     def quant(name, c0, src, s0, n):
         q, s, x = W(name, c0, c0 + n), W(name + "_s", c0, c0 + n), W(src, s0, s0 + 4 * n)
-        order("v", [x], [q, s])
-        return done("v", g.vector.quantize_mx(ap(q), ap(s), ap(x)), [x], [q, s])
+        return node([x], [q, s], {"v": lambda e: e["v"].quantize_mx(e["ap"](q), e["ap"](s), e["ap"](x))}, {"v": (12 + 0.88 * n) * TUNE["fac"]})
 
     def mm(bank, lhs, l0, rhs, r0, n=128):
         rd = [W(lhs, l0, l0 + 128), W(lhs + "_s", l0, l0 + 128), W(rhs, r0, r0 + n), W(rhs + "_s", r0, r0 + n)]
         o = W("pu" if bank > 3 else "pa", 512 * (bank % 4), 512 * (bank % 4) + n)
-        order("t", rd, [o])
-        return done("t", g.tensor.matmul_mx(ap(o), ap(rd[0]), ap(rd[1]), ap(rd[2]), ap(rd[3]), True, True), rd, [o])
+        return node(rd, [o], {"t": lambda e: e["t"].matmul_mx(e["ap"](o), e["ap"](rd[0]), e["ap"](rd[1]), e["ap"](rd[2]), e["ap"](rd[3]), True, True)},
+                    {"t": 1.3 * (n + 16) * cyc})
 
-    def pick(dst, d0, src, width, off, o0, n):
-        o, a, f = W(dst, d0, d0 + n), W(src, 0, width), W(off, o0, o0 + n // 16)
-        order("v", [a, f], [o])
-        done("v", g.vector.tensor_copy(ap(o).bitcast(dt.uint32), ap(a).bitcast(dt.uint32).indirect(ap(f))), [a, f], [o])
-        o, a = W(dst + "_s", d0, d0 + n), W(src + "_s", 0, width)
-        act(o, a, Act.Copy, off=f)
+    def pick(dst, d0, src, width_, off, o0, n):
+        o, a, f = W(dst, d0, d0 + n), W(src, 0, width_), W(off, o0, o0 + n // 16)
+        node([a, f], [o], {"v": lambda e: e["v"].tensor_copy(e["ap"](o).bitcast(dt.uint32), e["ap"](a).bitcast(dt.uint32).indirect(e["ap"](f)))},
+             {"v": (50 + 1.56 * 0.83 * n) * TUNE["fac"]})
+        act(W(dst + "_s", d0, d0 + n), W(src + "_s", 0, width_), Act.Copy, off=f)
 
-    def raw(w):
-        return ap(w).bitcast(dt.uint8) if LOG[w[0]][3] == CODES else ap(w)
+    def raw(e, w):
+        return e["ap"](w).bitcast(dt.uint8) if LOG[w[0]][3] == CODES else e["ap"](w)
 
-    def load(q, w, src, sem):
-        order(q, [], [w])
-        return done(q, queue[q].dma_start(ap(w), src), [], [w], sem, 16)
+    def load(q, w, tensor, c0, c1, sem, first=()):
+        return node(list(first), [w], {q: lambda e: e[q].dma_start(e["ap"](w), e["T"][tensor][:, c0:c1])}, {q: TUNE["issue"]}, sem, 16, TUNE["load"])
 
     def move(q, out, a, sem):
-        order(q, [a], [out])
-        return done(q, queue[q].dma_start(raw(out), raw(a)), [a], [out], sem, 16)
+        return node([a], [out], {q: lambda e: e[q].dma_start(raw(e, out), raw(e, a))}, {q: TUNE["issue"]}, sem, 16, TUNE["load"])
 
     def store(q, dst, a, sem):
-        order(q, [a], [])
-        return done(q, queue[q].dma_start(dst, raw(a)), [a], [], sem, 16)
+        return node([a], [], {q: lambda e: e[q].dma_start(dst(e["T"]), raw(e, a))}, {q: TUNE["issue"]}, sem, 16, TUNE["load"])
 
-    peers = [c for c in T.cores if c != core]
-
-    def did(c):
-        a = topo.addr(c)
-        return DstId(rid=a[0], pnc=a[1])
+    peers = [c for c in cores if c != core]
 
     def mask(engs):
         m = 0
@@ -256,23 +189,29 @@ def rank_program(g, core, T, topo):
         return m
 
     def send(parts, sem, after=()):
-        order("g", [p[0] for p in parts], [])
-        for tok in after:
-            wait("g", tok)
-        g.remote_dma_fused([RemoteDMATransfer(dst_ids=[did(c) for c in cs], dma_engine_mask=mask(es), remote_sem=T.sem[sem],
-                                              srcs=[raw(a)], dsts=[raw(b)] * len(cs)) for a, b, cs, es in parts], local_sem=T.sem["ls"])
-        total["ls"] = total.get("ls", 0) + sum(len(p[3]) for p in parts)
-        record("g", [p[0] for p in parts], [], ("ls", total["ls"]))
+        def did(c):
+            a = topo.addr(c)
+            return DstId(rid=a[0], pnc=a[1])
+
+        def f(e):
+            return e["g"].remote_dma_fused([RemoteDMATransfer(dst_ids=[did(c) for c in cs], dma_engine_mask=mask(es), remote_sem=e["T"].sem[sem],
+                                                              srcs=[raw(e, a)], dsts=[raw(e, b)] * len(cs)) for a, b, cs, es in parts],
+                                           local_sem=e["T"].sem["ls"])
+        lag = 0.0
+        for a, b, cs, es in parts:
+            row = width(a) * {F: 4, CODES: 4}.get(LOG[a[0]][3], 1)
+            lag = max(lag, TUNE["hop"] + 128 // len(es) * len(cs) * (TUNE["row"] + row * TUNE["byte"]))
+        return node([p[0] for p in parts], [], {"g": f}, {"g": TUNE["rissue"]}, "ls", sum(len(p[3]) for p in parts), lag, after,
+                    [(cores.index(c), sem) for p in parts for c in p[2]], True)
 
     def lands(sem, count, views):
-        total[sem] = count
-        record("r", [], views, (sem, count))
+        return node([], views, {"r": None}, {"r": 0.0}, sem, count)
 
     alle = topo.engines(core, peers[0])
 
-    load("y", W("ut", 0, 8), T.u[:, 0:8], "dl_u")
-    load("y", W("tbt", 0, 512), T.tb[:, 0:512], "dl_t0")
-    load("s", W("tbt", 512, 1024), T.tb[:, 512:1024], "dl_t1")
+    load("y", W("ut", 0, 8), "u", 0, 8, "dl_u")
+    load("y", W("tbt", 0, 512), "tb", 0, 512, "dl_t0")
+    load("s", W("tbt", 512, 1024), "tb", 512, 1024, "dl_t1")
 
     iota(W("pi", 0, 1), [[0, 1]], 0, 1)
     iota(W("pi", 1, 2), [[0, 1]], 1, 1)
@@ -280,19 +219,23 @@ def rank_program(g, core, T, topo):
     iota(W("jc"), [[128, 2]], 0, 1)
     iota(W("rr"), [[1, 4], [0, 4]])
     iota(W("rh"), [[1, 4], [0, 2]])
+    iota(W("rk8"), [[0, 2], [1, 4]])
     iota(W("mrow"), [[1, 32]])
     fill(W("ut", 8, 512), 0.0)
-    fill(W("ones"), 1.0)
-    order("g", [W("ones")], [W("idn")])
-    done("g", g.affine_select(ap(W("idn")), ap(W("ones")), [[-1, 128]], Op.is_equal, 0.0, 0, 1), [W("ones")], [W("idn")])
+    fill(W("onb"), 1.0)
+
+    def unit(b):
+        o = W("eb", 512 * b, 512 * b + 512)
+        node([W("onb")], [o], {"g": lambda e: e["g"].affine_select(e["ap"](o), e["ap"](W("onb")), [[-8, 128], [-1, 4]], Op.is_equal, 0.0, b, 8)},
+             {"g": 170 * TUNE["fac"] + 1024 * cyc})
+    for b in range(4):
+        unit(b)
     for y in range(4):
         iota(C("kt", y, y + 1, 0, 32), [[0, 2], [1, 16]], 16 * y)
-    iota(W("kk", 0, 4), [[0, 2], [16, 2]])
-    iota(W("kk", 4, 6), [[16, 2]], 96)
+    iota(W("kf"), [[16, 2]])
     iota(W("tr"), [[16, 8]], 512)
     iota(W("ofrf"), [[2, 2], [0, 2]])
 
-    fill(W("eb"), 0.0)
     pp = W("pi", 0, 1)
     ts(W("ci", 0, 2), W("pi", 0, 2), 3, Op.bitwise_and)
     ts(W("ci", 2, 3), pp, 15, Op.bitwise_and)
@@ -301,16 +244,15 @@ def rank_program(g, core, T, topo):
     ts(W("ci", 6, 7), pp, 31, Op.bitwise_and)
     ts(W("ci", 7, 8), pp, 5, Op.arith_shift_right, 1, Op.bitwise_and)
     ts(W("ci", 8, 9), pp, 6, Op.arith_shift_right)
-    fill(W("d0a"), 1.0)
     fill(W("exo0", 0, 2), 14)
-    cp(W("cf", 0, 9), W("ci", 0, 9))
     fill(W("exo0", 2, 4), 15)
+    fill(W("d0a"), 1.0)
     fill(W("d0a", 0, 1), 0.0)
+    fill(W("d0a", 4, 5), -1.0)
+    cp(W("cf", 0, 9), W("ci", 0, 9))
     q0, q1, xf, gf, i1 = W("cf", 0, 1), W("cf", 1, 2), W("cf", 2, 3), W("cf", 3, 4), W("cf", 4, 6)
-    rr4 = W("rr", 0, 16, 4)
     ts(W("wm", 0, 8), W("rh"), q0, Op.is_equal)
     ts(W("wm", 8, 16), W("rh"), q0, Op.not_equal)
-    fill(W("d0a", 4, 5), -1.0)
     fill(W("gm", 2, 3), 1.0)
     ts(W("gm", 0, 2), W("cf", 7, 9), -1.0, Op.mult, 1.0, Op.add)
     ts(W("gm", 3, 35), W("mrow"), W("cf", 6, 7), Op.is_ge)
@@ -333,154 +275,154 @@ def rank_program(g, core, T, topo):
     lands("a0", 3 * len(alle), [W("l0", 4 * o, 4 * o + 4) for o in range(N) if o != r])
 
     if r:
-        cp(W("tbt", 1024, 1040), W("tbt", 0, 16))
+        load("y", W("tbt", 1024, 1040), "tb", 0, 16, "dl_t2")
         quant("tz", 0, "tbt", 4 * r, 256)
         mm(2, "tz", 0, "uq", 0)
         mm(3, "tz", 128, "uq", 0)
         mine("l1", 2)
     lands("a1", len(alle) * (3 if r == 0 else 2), [W("l1", 4 * o, 4 * o + 4) for o in range(1, N) if o != r])
-    ts(W("wmg"), rr4, q0, Op.not_equal)
-    ts(W("r9"), rr4, -9.0, Op.add)
-    fill(W("zf"), 0.0)
-    fill(W("zt"), 0.0)
-    ts(W("zf"), W("zf"), q0, Op.add)
-    for h in range(2):
-        tt(W("wl", 4 * h, 4 * h + 4), W("r9"), W("wmg"), Op.mult)
-    cp(W("ofu"), W("zf"))
-    ts(W("zf"), W("zf"), 4.0, Op.add)
-    ts(W("jpc"), W("jc"), 1.0 / UNIT, Op.mult, 2304.0 / UNIT, Op.add)
-    quant("tw", 320, "zt", 0, 128)
-    cp(W("ofv"), W("zf"))
-    tt(W("jpa"), W("jc"), W("jpc"), Op.add)
-    ready = [("sv", total["sv"])]
-    for b in range(4):
-        cp(W("eb", 512 * b + b, 512 * b + 512, 4), W("idn"), "s")
+
+    u1, u2, u3 = 4096 / UNIT, 1024 / UNIT, 256 / UNIT
+    ts(W("nq"), W("rk8"), q0, Op.not_equal)
+    ts(W("ca"), W("rk8"), q0, Op.min)
+    ts(W("cb"), W("rk8"), q0, Op.max)
+    ts(W("s4"), W("rk8"), u1, Op.mult, 3 * u3 - 0.5, Op.add)
+    ts(W("c1"), W("ca"), 0.0, Op.is_equal, u2, Op.mult)
+    ts(W("c2"), W("cb"), 1.0, Op.is_equal, 1.0, Op.add)
+    ts(W("c3"), W("cb"), 3.0, Op.is_equal, -u3, Op.mult)
+    ts(W("c4"), W("ca"), 2.0, Op.is_equal, 1.0, Op.add)
+    tt(W("s1"), W("c1"), W("c2"), Op.mult)
+    tt(W("s2"), W("c3"), W("c4"), Op.mult)
+    tt(W("s3"), W("s1"), W("s4"), Op.add)
+    tt(W("s5"), W("s3"), W("s2"), Op.add)
+    tt(W("wl"), W("s5"), W("nq"), Op.mult)
+    ts(W("jp1"), W("jc"), 1.0 / UNIT, Op.mult, 0.5, Op.add)
+    tt(W("jp0"), W("jc"), W("jp1"), Op.add)
+
+    ts(W("ofu"), W("mrow"), 0.0, Op.is_ge, q0, Op.mult)
+    ts(W("ofv"), W("ofu"), 4.0, Op.add)
+    ready = [quant("tw", 320, "tbt", 0, 128)]
     act(W("ub0"), W("ut"), Act.Copy, off=W("ofu"))
     act(W("ub1"), W("ut"), Act.Copy, off=W("ofv"))
     iota(W("va"), [[0, 2], [1, 64]], R1)
     iota(W("vb"), [[0, 2], [1, 64]], R2)
     iota(W("fr", 0, 512), [[16, 16], [0, 2], [1, 16]])
-    ts(W("kk"), W("kk"), xf, Op.add)
-    ts(W("ofrf"), W("ofrf"), gf, Op.add)
+    fill(W("fr", 512, 640), 0.0)
+    ts(W("kg"), W("kf"), xf, Op.add)
+    ts(W("ofr"), W("ofrf"), gf, Op.add)
+    ts(W("tri32"), W("tr"), xf, Op.add)
     when = 0 if r in BUILD[0] else 1
     quant("eq", 0, "eb", 0, 512)
-    quant(("psa", "psb")[when], 0, "zt", 0, 128)
-    fill(W(("h0", "h1")[when]), 0.0)
-    cp(W("kki"), W("kk"))
-    cp(W("ofr"), W("ofrf"))
-    quant("tw", 0, "tbt", 0, 256)
-    order("y", [W("l0")], [])
-    load("y", W("wt"), T.w[:, 0:1024], "dl_w")
+    quant(("psa", "psb")[when], 0, "tbt", 0, 128)
+    cp(W(("h0", "h1")[when]), W("tbt", 0, 512), "vs")
+    for x in ("", "_s"):
+        move("y", W("tw" + x, 0, 256), W("tq" + x), "dl_m" + x)
+    quant("uc", 0, "ub0", 0, 128)
+    quant("ug", 0, "ub1", 0, 128)
+    load("y", W("wt"), "w", 0, 1024, "dl_w", [W("l0")])
+    for x in ("", "_s"):
+        move("y", W("tx" + x, 0, 256), W("tq" + x), "dl_n" + x)
+    quant("wq", 0, "wt", 0, 256)
 
     ts(W("ma"), W("rr", 0, 12), q1, Op.is_lt)
     ts(W("mb"), W("rr", 0, 12), q1, Op.is_ge)
     ts(W("m0"), W("rr"), q1, Op.is_equal)
     cp(W("rho", 0, 1), q1)
     tt(W("rho", 1, 4), W("rr", 0, 12, 4), W("mb", 0, 12, 4), Op.add)
+    r1, r2, r3 = W("rho", 1, 2), W("rho", 2, 3), W("rho", 3, 4)
+    ts(W("wa"), W("rho", 1, 4), u1, Op.mult, -0.5, Op.add)
+    ts(W("wb"), r1, u2, Op.mult)
+    ts(W("wc"), r3, u3, Op.mult)
+    ts(W("wd", 0, 1), r2, u2, Op.mult, W("wa", 0, 1), Op.add)
+    ts(W("wd", 1, 3), W("wa", 1, 3), W("wb"), Op.add)
+    for h in range(2):
+        ts(W("wl1", 3 * h, 3 * h + 2), W("wd", 0, 2), W("wc"), Op.add)
+        ts(W("wl1", 3 * h + 2, 3 * h + 3), r2, u3, Op.mult, W("wd", 2, 3), Op.add)
     fill(W("d0b"), 1.0)
-    fill(W("exo1", 0, 2), 3)
-    for h in range(2):
-        ts(W("cs", 4 * h, 4 * h + 4), W("rho"), W("jc", h, h + 1), Op.add)
-    for h in range(2):
-        ts(W("cs2", 4 * h, 4 * h + 4), W("rho"), 256.0 / UNIT, Op.mult)
-    cp(W("csi"), W("cs"))
-    fill(W("exo1", 2, 4), 7)
     fill(W("d0b", 0, 8, 4), 0.0)
-    ts(W("csj"), W("csi"), 255, Op.bitwise_and)
     fill(W("d0b", 1, 8, 4), -1.0)
+    fill(W("exo1", 0, 2), 3)
+    fill(W("exo1", 2, 4), 7)
+    for h in range(2):
+        ts(W("csi", 4 * h, 4 * h + 4), W("rho"), 4097.0, Op.mult, W("jc", h, h + 1), Op.add)
+    ts(W("csj"), W("csi"), 3 * 4096 + 255, Op.bitwise_and)
+    cp(W("csf"), W("csj"))
+    ts(W("cso"), i1, 4096.0 * r, Op.add)
+    ts(W("ji"), W("jc"), 1.0, Op.add)
+    ts(W("jj"), W("ji"), 255, Op.bitwise_and)
+    ts(W("jp2"), W("jj"), 1.0 / UNIT, Op.mult, 0.5, Op.add)
+    cp(W("pm", 64, 130, 65), W("cf", 4, 6), "vs")
 
-    def before():
-        cp(W("csf"), W("csj"))
-        cp(W("l1", 0, 4), W("l0", 0, 4))
-        for h in range(2):
-            ts(W("wl1", 3 * h, 3 * h + 3), W("rho", 1, 4), -9.0, Op.add)
-        ts(W("cs"), W("csf"), 1.0 + 1.0 / UNIT, Op.mult)
-        ts(W("cso"), i1, 1.0 + 1.0 / UNIT, Op.mult, 256.0 * r / UNIT, Op.add)
-        for h in range(2):
-            cp(W("pm", 65 * h + 64, 65 * h + 65), W("cf", 4 + h, 5 + h))
-        tt(W("csf"), W("cs"), W("cs2"), Op.add)
-        tt(W("krb"), W("l1", 4, 16), W("mb"), Op.mult)
-        tt(W("kra"), W("l1", 0, 12), W("ma"), Op.mult)
-        tt(W("kr0"), W("l1"), W("m0"), Op.mult)
-        tt(W("kro", 4, 16), W("kra"), W("krb"), Op.add)
-        for h in range(2):
-            red(W("kro", 2 * h, 2 * h + 1), W("kr0", 2 * h, 16, 4), Op.add)
+    cp(W("l1", 0, 4), W("l0", 0, 4), "vs")
+    tt(W("krb"), W("l1", 4, 16), W("mb"), Op.mult)
+    tt(W("kra"), W("l1", 0, 12), W("ma"), Op.mult)
+    tt(W("kr0"), W("l1"), W("m0"), Op.mult)
+    tt(W("kro", 4, 16), W("kra"), W("krb"), Op.add)
+    for h in range(2):
+        red(W("kro", 2 * h, 2 * h + 1), W("kr0", 2 * h, 16, 4), Op.add)
 
-    def count(t, early, late, last):
+    def count(t):
         n = str(t)
         src, off = (W("sc0"), W("exo0")) if t == 0 else (W("sc1", 0, 8), W("exo1"))
         s2 = W("sc0", 14, 16) if t == 0 else W("sc1", 3, 8, 4)
         rn, th, cm = "row" + n, "th" + n, "cm" + n
-        act(W("sa" + n), s2, Act.Abs)
         act(W("ex" + n), src, Act.Abs, off=off)
-        early()
-        for h in range(2):
-            s = W("sa" + n, h, h + 1)
-            ts(W("nd" + n, h, h + 1), s, 1.5 * 2.0 ** -24, Op.mult, s, Op.add)
+        act(W("sa" + n), s2, Act.Abs)
         for h in range(2):
             turn(C(rn, h, h + 1, 0, 32), W("ex" + n, 32 * h, 32 * h + 32))
         for h in range(2):
+            s = W("sa" + n, h, h + 1)
+            ts(W("nd" + n, h, h + 1), s, 1.5 * 2.0 ** -24, Op.mult, s, Op.add)
             ts(W("dl" + n, h, h + 1), W("nd" + n, h, h + 1), TINY, Op.max, W("sa" + n, h, h + 1), Op.subtract)
-        for a in range(4):
-            b = a ^ 1
-            cp(C(rn, 0, 2, 32, 64, 32 * a, 32 * a + 32), C(rn, 0, 2, 0, 32, 32 * b, 32 * b + 32), "v" if a < 2 else "s")
+        for a in range(2):
+            cp(C(rn, 0, 2, 64, 96, 64 * a, 64 * a + 64), C(rn, 0, 2, 0, 32, 64 - 64 * a, 128 - 64 * a), "vs")
+        for x in (1, 3):
+            for a in range(4):
+                b = a ^ x
+                cp(C(rn, 0, 2, 32 * x, 32 * x + 32, 32 * a, 32 * a + 32), C(rn, 0, 2, 0, 32, 32 * b, 32 * b + 32), "vs")
         for h in range(2):
             ts(W(th, 40 * h, 40 * h + 35), W("gm", 0, 35), W("dl" + n, h, h + 1), Op.mult, W("sa" + n, h, h + 1), Op.add)
-        for a in range(2):
-            cp(C(rn, 0, 2, 64, 128, 64 * a, 64 * a + 64), C(rn, 0, 2, 0, 64, 64 - 64 * a, 128 - 64 * a), "s")
         for h in range(2):
             tt(W(cm, 272 * h + 232, 272 * h + 264), C(rn, h, h + 1, 0, 32), W(th, 40 * h + 3, 40 * h + 35), Op.is_ge)
-        for h in range(2):
             ts(W(cm, 272 * h + 200, 272 * h + 232), C(rn, h, h + 1, 32, 64), W(th, 40 * h, 40 * h + 1), Op.is_ge)
-        for h in range(2):
-            acc(W(cm, 272 * h + 192, 272 * h + 193), W(cm, 272 * h + 200, 272 * h + 264))
-        late()
-        for h in range(2):
             other = W(th, 2, 3) if h == 0 else W("sa" + n, 1, 2)
             ts(W(cm, 272 * h, 272 * h + 128), C(rn, 1 - h, 2 - h, 0, 128), other, Op.is_ge)
             ts(W(cm, 272 * h + 128, 272 * h + 192), C(rn, h, h + 1, 64, 128), W(th, 40 * h + 1, 40 * h + 2), Op.is_ge)
-        for h in range(2):
-            acc(W("po" + n, h, h + 1), W(cm, 272 * h, 272 * h + 193))
-        last()
+            total(W(cm, 272 * h + 192, 272 * h + 193), W(cm, 272 * h + 200, 272 * h + 264))
+            total(W("po" + n, h, h + 1), W(cm, 272 * h, 272 * h + 193))
 
     def listed(t):
         m, mt, lw, b, c = [x + str(t) for x in ("mm", "mt", "lw", "ab", "ac")]
         for h in range(2):
             ts(C(m, 0, 4, 32 * h, 32 * h + 32), C("kt", 0, 4, 0, 32), W("po%d" % t, h, h + 1), Op.is_equal, W("pay%d" % t, h, h + 1), Op.mult)
-        for y in (2, 3, 0, 1):
+        for y in range(4):
             turn(W(mt, 64 * y, 64 * y + 64), C(m, y, y + 1, 0, 64))
-        for y in (2, 3):
-            acc(W(lw, y, y + 1), W(mt, 64 * y, 64 * y + 64))
-        for y in (0, 1):
-            red(W(lw, y, y + 1), W(mt, 64 * y, 64 * y + 64), Op.add)
+        for y in range(4):
+            total(W(lw, y, y + 1), W(mt, 64 * y, 64 * y + 64))
         for k in range(4):
             tt(W(b, 0, 4, 1, 32 * k, 32 * k + 32), W(lw, 0, 4, 1, 32 * k, 32 * k + 32), W(lw, 0, 4, 1, 32 * (k ^ 1), 32 * (k ^ 1) + 32), Op.add)
         for k in range(2):
             tt(W(c, 0, 4, 1, 64 * k, 64 * k + 64), W(b, 0, 4, 1, 64 * k, 64 * k + 64), W(b, 0, 4, 1, 64 - 64 * k, 128 - 64 * k), Op.add)
         return W(c, 0, 4)
 
-    def lost(t, n, wl, base, parts):
+    def lost(t, n, wl, base):
         k = n // 2
         s = str(t)
 
         def size(h):
             return W("gy0", h, 8, 2) if t == 0 else W("ga1", k * h, k * h + k)
-        if 0 in parts:
-            for h in range(2):
-                red(W("gx" + s, h, h + 1), size(h), Op.max)
-        if 1 in parts:
-            for h in range(2):
-                ts(W("ge" + s, k * h, k * h + k), size(h), W("gx" + s, h, h + 1), Op.is_equal)
-            tt(W("gw" + s, 0, n), W("ge" + s, 0, n), W(wl), Op.mult)
-        if 2 in parts:
-            for h in range(2):
-                red(W("gn" + s, h, h + 1), W("gw" + s, k * h, k * h + k), Op.min)
-            for h in range(2):
-                ts(W("pay" + s, h, h + 1), W("gn" + s, h, h + 1), 256.0 / UNIT, Op.mult, W(base, h, h + 1), Op.add)
+        for h in range(2):
+            red(W("gx" + s, h, h + 1), size(h), Op.max)
+        for h in range(2):
+            ts(W("ge" + s, k * h, k * h + k), size(h), W("gx" + s, h, h + 1), Op.is_equal)
+        tt(W("gw" + s, 0, n), W("ge" + s, 0, n), W(wl), Op.mult)
+        for h in range(2):
+            red(W("gn" + s, h, h + 1), W("gw" + s, k * h, k * h + k), Op.min)
+        tt(W("pay" + s), W("gn" + s), W(base), Op.add)
 
     def gather(t, lists):
         n = "ab"[t]
-        src, width = (("tq", 256), ("tw", 448))[t]
+        src, width_ = (("tq", 256), ("tw", 448))[t]
         off = "off%d" % t
         cp(W(off), lists)
         sl, la = "sl" + n, "la" + n
@@ -488,49 +430,33 @@ def rank_program(g, core, T, topo):
         if r in bs:
             d = bs.index(r)
             o = 1 - d
-            pick(sl, 32 * o, src, width, off, 2 * o, 32)
-            to = T.cores[bs[o]]
+            pick(sl, 32 * o, src, width_, off, 2 * o, 32)
+            to = cores[bs[o]]
             for s in ("", "_s"):
                 send([(W(sl + s, 32 * o, 32 * o + 32), W(la + s, 32 * r, 32 * r + 32), [to], topo.engines(core, to))], "ha%d" % t, ready)
-            pick(la, 32 * r, src, width, off, 2 * d, 32)
+            pick(la, 32 * r, src, width_, off, 2 * d, 32)
             cnt = 0
             for i in range(N):
                 if i != r:
-                    cnt += 2 * len(topo.engines(T.cores[i], core)) // (1 if i in bs else 2)
+                    cnt += 2 * len(topo.engines(cores[i], core)) // (1 if i in bs else 2)
             lands("ha%d" % t, cnt, [W(la + s, 32 * i, 32 * i + 32) for s in ("", "_s") for i in range(N) if i != r])
         else:
-            pick(sl, 0, src, width, off, 0, 64)
+            pick(sl, 0, src, width_, off, 0, 64)
             for s in ("", "_s"):
-                send([(W(sl + s, 32 * d, 32 * d + 32), W(la + s, 32 * r, 32 * r + 32), [T.cores[bs[d]]], topo.engines(core, T.cores[bs[d]])[d::2])
+                send([(W(sl + s, 32 * d, 32 * d + 32), W(la + s, 32 * r, 32 * r + 32), [cores[bs[d]]], topo.engines(core, cores[bs[d]])[d::2])
                       for d in range(2)], "ha%d" % t, ready)
 
     def numbers(t, w):
-        s = str(t)
-        ts(W("wj" + s), w, UNIT, Op.mult)
-        ts(W("wi" + s), W("wj" + s), 1023, Op.bitwise_and)
+        ts(W("wj%d" % t), w, UNIT, Op.mult)
 
     def buildlist(t):
         s, d = str(t), BUILD[t].index(r)
-        wi = W("wi" + s, 2 * d, 2 * d + 2)
-        if t == 0:
-            ts(W("rl" + s), wi, 8, Op.arith_shift_right)
-            ts(W("rq" + s), wi, 3, Op.bitwise_and)
-        else:
-            ts(W("ra" + s), wi, 1, Op.add)
-            ts(W("rl" + s), wi, 8, Op.arith_shift_right)
-            ts(W("rq" + s), W("ra" + s), 3, Op.bitwise_and)
-        a, b = W("ra" + s), W("rb" + s)
-        tt(b, W("rq" + s), W("rl" + s), Op.max)
-        tt(a, W("rq" + s), W("rl" + s), Op.min)
-        ts(W("rk" + s, 0, 2), W("rq" + s), 32, Op.mult)
-        ts(W("e2" + s), b, 1, Op.is_equal, 1, Op.add)
-        ts(W("e3" + s), b, 3, Op.is_equal, -32, Op.mult)
-        ts(W("e1" + s), a, 0, Op.is_equal, 32, Op.mult)
-        ts(W("e4" + s), a, 2, Op.is_equal, 1, Op.add)
-        tt(W("rk" + s, 2, 4), W("e1" + s), W("e2" + s), Op.mult)
-        tt(W("rk" + s, 4, 6), W("e3" + s), W("e4" + s), Op.mult)
-        tt(W("rf" + s), W("rk" + s), W("kki"), Op.add)
-        cp(W("rfo" + s), W("rf" + s))
+        v = W("wj" + s, 2 * d, 2 * d + 2)
+        ts(W("rk" + s, 0, 2), v, 3, Op.bitwise_and)
+        ts(W("rk" + s, 2, 4), v, 10, Op.arith_shift_right, 3, Op.bitwise_and)
+        ts(W("rk" + s, 4, 6), v, 8, Op.arith_shift_right, 3, Op.bitwise_and)
+        for y in range(2):
+            ts(W("rfo" + s, y, 6, 2), W("rk" + s, y, 6, 2), 32.0, Op.mult, W("kg", y, y + 1), Op.add)
 
     def build(t):
         s, n, d = str(t), "ab"[t], BUILD[t].index(r)
@@ -541,17 +467,8 @@ def rank_program(g, core, T, topo):
         at = 96 if d == 0 else 0
         for b in range(4):
             cp(W("xs", 64 * b, 64 * b + 64), W("pu", 512 * b + 32, 512 * b + 96), "s")
-
-        def first(b):
             tt(W("xd", 32 * b, 32 * b + 32), W("pu", 512 * b, 512 * b + 32), W("xs", 64 * b, 64 * b + 32), Op.subtract)
-
-        def second(b):
             tt(W(hh, 4 * at + b, 4 * at + 128, 4), W("xd", 32 * b, 32 * b + 32), W("xs", 64 * b + 32, 64 * b + 64), Op.subtract)
-        first(0)
-        for b in range(1, 4):
-            first(b)
-            second(b - 1)
-        second(3)
         dst, base = ("tw", 256) if t == 0 else ("tx", 512)
         quant(dst, base + 128 * d, hh, 0, 128)
         c = base + 96 + 32 * d
@@ -561,126 +478,95 @@ def rank_program(g, core, T, topo):
 
     def built(t):
         dst, base = ("tw", 256) if t == 0 else ("tx", 512)
-        lands("hb%d" % t, sum(2 * len(topo.engines(T.cores[b], core)) for b in BUILD[t] if b != r),
+        lands("hb%d" % t, sum(2 * len(topo.engines(cores[b], core)) for b in BUILD[t] if b != r),
               [W(dst + x, base + 96 + 32 * d, base + 128 + 32 * d) for x in ("", "_s") for d in range(2) if BUILD[t][d] != r])
 
     def mapped(t):
         s = str(t)
-        i = W("fi" + s)
-        ts(W("fl" + s), W("wi" + s), 8, Op.arith_shift_right)
-        if t == 0 or r == 0:
-            ts(i, W("wi" + s), 255, Op.bitwise_and)
-        else:
-            ts(W("fj" + s), W("wi" + s), r, Op.add)
-            ts(i, W("fj" + s), 255, Op.bitwise_and)
-        if t == 0:
-            ts(W("tr"), W("tr"), xf, Op.add)
-            fill(W("fr", 512, 640), 0.0)
-            cp(W("tri32"), W("tr"))
-        ts(W("fm" + s), W("fl" + s), r, Op.is_equal)
-        ts(W("fk" + s), i, 240, Op.bitwise_and)
-        tt(W("fa" + s, 0, 4), i, W("fk" + s), Op.add)
-        ts(W("fa" + s, 4, 8), W("fa" + s, 0, 4), 16, Op.add)
-        tt(W("fd" + s), W("fa" + s), W("tri32"), Op.subtract)
-        for c in (0, 4):
-            tt(W("fe" + s, c, c + 4), W("fd" + s, c, c + 4), W("fm" + s), Op.mult)
-        tt(W("fo" + s), W("fe" + s), W("tri32"), Op.add)
+        i, a = W("fi" + s), W("wj" + s)
+        ts(W("fl" + s), a, 12, Op.arith_shift_right, 3, Op.bitwise_and)
+        if t and r != 1:
+            ts(W("fj" + s), a, float(r - 1), Op.add)
+            a = W("fj" + s)
+        ts(i, a, 255, Op.bitwise_and)
+        ts(W("fk" + s), a, 240, Op.bitwise_and)
+        ts(W("fm" + s), W("fl" + s), float(r), Op.not_equal, 4096.0, Op.mult)
+        tt(W("fe" + s), i, W("fk" + s), Op.add)
+        tt(W("fa" + s, 0, 4), W("fe" + s), W("fm" + s), Op.add)
+        ts(W("fa" + s, 4, 8), W("fa" + s, 0, 4), 16.0, Op.add)
+        tt(W("fo" + s), W("fa" + s), W("tri32"), Op.min)
         cp(W("ofs" + s), W("fo" + s))
 
     def enter(t):
         win, off, src = W("fr"), W("ofs%d" % t), W("va" if t == 0 else "vb")
-        order("v", [off, src], [win])
-        done("v", g.vector.tensor_copy(ap(win).indirect(ap(off)), ap(src)), [off, src], [win])
+        node([off, src], [win], {"v": lambda e: e["v"].tensor_copy(e["ap"](win).indirect(e["ap"](off)), e["ap"](src))},
+             {"v": (50 + 3 * 0.83 * 128) * TUNE["fac"]})
 
     def listrow(t, w):
         s = str(t)
         act(W("er" + s), w, Act.Copy, off=W("ofr"))
         turn(W("lr", 64 * t, 64 * t + 64), W("er" + s))
+        ts(W("bi", 64 * t, 64 * t + 64), W("lr", 64 * t, 64 * t + 64), UNIT, Op.mult, -1.0 * t, Op.add)
+
+    def stripes(t):
+        o = 128 * t
+        b = W("bi", 64 * t, 64 * t + 64, 1, 0, 1)
+        ts(W("bj", o, o + 64, 1, 0, 1), b, 255, Op.bitwise_and)
+        ts(W("bj", o + 64, o + 128, 1, 0, 1), b, 12, Op.arith_shift_right, 3, Op.bitwise_and)
+        cp(W("bsf", o, o + 128, 1, 0, 1), W("bj", o, o + 128, 1, 0, 1))
 
     for m in range(2):
         tt(W("sq0", 8 * m, 8 * m + 8), W("l0", 0, 16, 2), W("wm", 8 * m, 8 * m + 8), Op.mult)
-    tt(W("gy0"), W("l0", 1, 16, 2), W("wm", 8, 16), Op.mult)
     for h in range(2):
         scan(W("sc0", h, 16, 2), W("d0a"), W("sq0", h, 16, 2))
-    lost(0, 8, "wl", "jpa", (0,))
-    count(0, lambda: lost(0, 8, "wl", "jpa", (1,)), lambda: None, lambda: lost(0, 8, "wl", "jpa", (2,)))
+    tt(W("gy0"), W("l0", 1, 16, 2), W("wm", 8, 16), Op.mult)
+    lost(0, 8, "wl", "jp0")
+    count(0)
     w0 = listed(0)
     gather(0, w0)
     numbers(0, w0)
-
-    def hot():
-        for e in range(8):
-            ts(W("oh", 64 * e, 64 * e + 64), W("lr", 0, 64), W("csf", e, e + 1), Op.is_equal)
-        for e in range(8):
-            acc(W("rep", e, e + 1), W("oh", 64 * e, 64 * e + 64))
-        for h in range(2):
-            ts(W("oho", 64 * h, 64 * h + 64), W("lr", 0, 64), W("cso", h, h + 1), Op.is_equal)
-        for h in range(2):
-            tt(W("pm", 65 * h, 65 * h + 64), W("oho", 64 * h, 64 * h + 64), W("va", 0, 64), Op.mult)
-        for h in range(2):
-            red(W("src1", h, h + 1), W("pm", 65 * h, 65 * h + 65), Op.max)
-        ts(W("nrep"), W("rep"), -1.0, Op.mult, 1.0, Op.add)
-        tt(W("jpb"), W("src1"), W("jpc"), Op.add)
-        for h in range(2):
-            tt(W("prc", 260 * h + 64, 260 * h + 260, 65), W("kro", 2 * h, 16, 4), W("nrep", 4 * h, 4 * h + 4), Op.mult)
-            tt(W("prg", 195 * h + 64, 195 * h + 195, 65), W("kro", 4 + 2 * h + 1, 16, 4), W("nrep", 4 * h + 1, 4 * h + 4), Op.mult)
-
-    def spare():
-        quant("tx", 0, "tbt", 0, 256)
-        quant("wq", 0, "wt", 0, 256)
-
     if r in BUILD[0]:
-        rest = weave(listof(buildlist, 0), listof(before))
-        listrow(0, w0)
+        buildlist(0)
         build(0)
-    else:
-        listrow(0, w0)
-        rest = weave(listof(mapped, 0), listof(before))
-    quant("uc", 0, "ub0", 0, 128)
-    quant("ug", 0, "ub1", 0, 128)
-    run(rest)
-    hot()
-    if r in BUILD[1]:
-        spare()
-        enter(0)
     built(0)
+    listrow(0, w0)
+    ts(W("key"), W("bi", 0, 64), 3 * 4096 + 255, Op.bitwise_and)
+    mapped(0)
+    enter(0)
+    for e in range(8):
+        ts(W("oh", 64 * e, 64 * e + 64), W("key"), W("csf", e, e + 1), Op.is_equal)
+    for e in range(8):
+        total(W("rep", e, e + 1), W("oh", 64 * e, 64 * e + 64))
+    for h in range(2):
+        ts(W("oho", 64 * h, 64 * h + 64), W("key"), W("cso", h, h + 1), Op.is_equal)
+        tt(W("pm", 65 * h, 65 * h + 64), W("oho", 64 * h, 64 * h + 64), W("va", 0, 64), Op.mult)
+        red(W("src1", h, h + 1), W("pm", 65 * h, 65 * h + 65), Op.max)
+    ts(W("nrep"), W("rep"), -1.0, Op.mult, 1.0, Op.add)
+    tt(W("jpb"), W("src1"), W("jp2"), Op.add)
+    for h in range(2):
+        tt(W("prc", 260 * h + 64, 260 * h + 260, 65), W("kro", 2 * h, 16, 4), W("nrep", 4 * h, 4 * h + 4), Op.mult)
+        tt(W("prg", 195 * h + 64, 195 * h + 195, 65), W("kro", 4 + 2 * h + 1, 16, 4), W("nrep", 4 * h + 1, 4 * h + 4), Op.mult)
 
     mm(0, "uc", 0, "tw", 320)
     mm(1, "ug", 0, "tw", 320)
-
-    def gnow(es):
-        for e in es:
-            o = 64 * (4 * (e // 3) + e % 3 + 1)
-            tt(W("prg", 65 * e, 65 * e + 64), W("pa", 544, 608), W("oh", o, o + 64), Op.mult)
-        for e in es:
-            acc(W("gq", e, e + 1), W("prg", 65 * e, 65 * e + 65))
-
     for e in range(8):
         tt(W("prc", 65 * e, 65 * e + 64), W("pa", 32, 96), W("oh", 64 * e, 64 * e + 64), Op.mult)
-        if e < 6:
-            acc(W("sqc", e, e + 1), W("prc", 65 * e, 65 * e + 65))
-    gnow((0, 1))
-    for e in (6, 7):
-        red(W("sqc", e, e + 1), W("prc", 65 * e, 65 * e + 65), Op.add)
-    gnow((2,))
+        total(W("sqc", e, e + 1), W("prc", 65 * e, 65 * e + 65))
     scan(W("sc1", 0, 8), W("d0b"), W("sqc"))
-
-    def gsums():
-        gnow((3, 4, 5))
-        act(W("ga1", 0, 6), W("gq"), Act.Abs)
-
-    count(1, gsums, lambda: lost(1, 6, "wl1", "jpb", (0, 1)), lambda: lost(1, 6, "wl1", "jpb", (2,)))
+    for e in range(6):
+        o = 64 * (4 * (e // 3) + e % 3 + 1)
+        tt(W("prg", 65 * e, 65 * e + 64), W("pa", 544, 608), W("oh", o, o + 64), Op.mult)
+        total(W("gq", e, e + 1), W("prg", 65 * e, 65 * e + 65))
+    act(W("ga1", 0, 6), W("gq"), Act.Abs)
+    lost(1, 6, "wl1", "jpb")
+    count(1)
     w1 = listed(1)
     gather(1, w1)
     numbers(1, w1)
     if r in BUILD[1]:
-        rest = weave(listof(buildlist, 1), listof(mapped, 1))
+        buildlist(1)
         build(1)
-        run(rest)
-    else:
-        spare()
-        run(weave(listof(mapped, 0), listof(mapped, 1)))
-        enter(0)
+    mapped(1)
     built(1)
     for x in ("", "_s"):
         move("y", W("tx" + x, R1, R1 + 64), W("tw" + x, R1, R1 + 64), "dl_x" + x)
@@ -688,30 +574,183 @@ def rank_program(g, core, T, topo):
     turn(W("ft"), W("fr", 0, 512))
     cp(W("fou"), W("ft", 0, 512, 32))
     listrow(1, w1)
+    for t in range(2):
+        stripes(t)
+    store("y", lambda T: T.bs[:, :], W("bsf", 0, 256, 1, 0, 1), "dbs")
 
     for c in range(2):
         pick("ou", 128 * c, "tx", 672, "fou", 8 * c, 128)
         for o in range(2):
             mm(2 * c + o, "wq", 128 * o, "ou", 128 * c)
-    ts(W("bi", 0, 128, 1, 0, 1), W("lr", 0, 128, 1, 0, 1), UNIT, Op.mult)
-    for t in range(2):
-        ts(W("bj", 128 * t, 128 * t + 64, 1, 0, 1), W("bi", 64 * t, 64 * t + 64, 1, 0, 1), 255, Op.bitwise_and)
-        ts(W("bj", 128 * t + 64, 128 * t + 128, 1, 0, 1), W("bi", 64 * t, 64 * t + 64, 1, 0, 1), 8, Op.arith_shift_right, 3, Op.bitwise_and)
 
-    def scales(ks):
-        for k in ks:
-            store("y", T.osc[4 * k:4 * k + 4, 0:256], W("ou_s", 0, 256, 1, 32 * k, 32 * k + 4), "doc")
+    def scales(k):
+        store("y", lambda T: T.osc[4 * k:4 * k + 4, 0:256], W("ou_s", 0, 256, 1, 32 * k, 32 * k + 4), "doc")
 
-    store("y", T.oc[:, 0:1024], W("ou"), "doc")
-    scales((0, 1))
+    def block(c, o):
+        a, b = 256 * o + 128 * c, 256 * o + 128 * c + 128
+        cp(W("ys", a, b), W("pa", 512 * (2 * c + o), 512 * (2 * c + o) + 128), "vs"[o])
+        store("ys"[o], lambda T: T.y[:, a:b], W("ys", a, b), "dy%d" % o)
+
+    store("y", lambda T: T.oc[:, 0:1024], W("ou"), "doc")
+    for k in range(4):
+        scales(k)
     for c in range(2):
         for o in range(2):
-            v = W("ys", 256 * o + 128 * c, 256 * o + 128 * c + 128)
-            cp(v, W("pa", 512 * (2 * c + o), 512 * (2 * c + o) + 128), "vs"[o])
-            store("ys"[o], T.y[:, 256 * o + 128 * c:256 * o + 128 * c + 128], v, "dy%d" % o)
-        if c == 0:
-            cp(W("bsf", 0, 256, 1, 0, 1), W("bj", 0, 256, 1, 0, 1))
-    scales((2, 3))
-    store("y", T.bs[:, :], W("bsf", 0, 256, 1, 0, 1), "dbs")
+            block(c, o)
+    return nodes
+
+
+def arrange(plans):
+    wake = TUNE["wake"]
+    flat, base = [], []
+    for r, ns in enumerate(plans):
+        base.append(len(flat))
+        for n in ns:
+            flat.append((r, n))
+    pred = [set() for _ in flat]
+    for r, ns in enumerate(plans):
+        log = {}
+        for n in ns:
+            me = base[r] + n["i"]
+            qs = list(n["fns"])
+            for ws, isw in ((n["rd"], False), (n["wr"], True)):
+                for w in ws:
+                    for w2, isw2, j, qs2 in log.get(w[0], ()):
+                        if (isw or isw2 or (w[0] in ("pa", "pu") and (len(qs) > 1 or qs != qs2))) and meet(w, w2):
+                            pred[me].add(j)
+            for ws, isw in ((n["rd"], False), (n["wr"], True)):
+                for w in ws:
+                    log.setdefault(w[0], []).append((w, isw, me, qs))
+            for a in n["after"]:
+                pred[me].add(base[r] + a["i"])
+            pred[me].discard(me)
+    sends = {}
+    for k, (r, n) in enumerate(flat):
+        for to in n["to"]:
+            sends.setdefault(to, []).append(k)
+    for k, (r, n) in enumerate(flat):
+        if "r" in n["fns"]:
+            pred[k].update(sends.get((r, n["sem"]), ()))
+    succ = [[] for _ in flat]
+    for k, ps in enumerate(pred):
+        for j in ps:
+            succ[j].append(k)
+
+    def after(j, k):
+        return flat[j][1]["lag"] + (0.0 if "r" in flat[k][1]["fns"] else wake)
+    left = [len(s) for s in succ]
+    way = [0.0] * len(flat)
+    todo = [k for k in range(len(flat)) if not left[k]]
+    while todo:
+        k = todo.pop()
+        n = flat[k][1]
+        way[k] = min(n["cost"].values()) + max([n["lag"]] + [after(k, j) + way[j] for j in succ[k]])
+        for j in pred[k]:
+            left[j] -= 1
+            if not left[j]:
+                todo.append(j)
+
+    count = [len(p) for p in pred]
+    when, free, ready, best, out = [0.0] * len(flat), {}, {}, {}, []
+
+    def choose(q):
+        f = free.get(q, 0.0)
+        top, at = None, 0.0
+        for k in sorted(ready[q], key=lambda k: (-way[k], k)):
+            s = max(f, when[k])
+            if top is None or (s < at and s + flat[k][1]["cost"][q[1]] <= at + TUNE["tol"]):
+                top, at = k, s
+        best[q] = (at, top)
+        if top is None:
+            del best[q]
+
+    def put(k):
+        for q in flat[k][1]["fns"]:
+            ready.setdefault((flat[k][0], q), set()).add(k)
+            choose((flat[k][0], q))
+    for k in range(len(flat)):
+        if not count[k]:
+            put(k)
+
+    def ends(q):
+        n = flat[best[q][1]][1]
+        return best[q][0] + n["cost"][q[1]] + (TUNE["bias"] if q[1] == "v" and len(n["fns"]) > 1 else 0.0), best[q][1]
+    while best:
+        q = min(best, key=ends)
+        at, k = best[q]
+        r, n = flat[k]
+        out.append((r, n, q[1]))
+        end = at + n["cost"][q[1]]
+        free[q] = end if q[1] != "r" else 0.0
+        for x in n["fns"]:
+            ready[(r, x)].discard(k)
+            choose((r, x))
+        for j in succ[k]:
+            when[j] = max(when[j], end + after(k, j))
+            count[j] -= 1
+            if not count[j]:
+                put(j)
+    return out
+
+
+def rank_program(g, core, T, topo):
+    r = T.rank_of(core)
+    if r is None:
+        return
+    cores = list(T.cores)
+    if "order" not in _PLANS:
+        _PLANS["order"] = arrange([calls(i, cores, topo) for i in range(N)])
+    queue = {"v": g.vector, "s": g.scalar, "t": g.tensor, "g": g, "y": g.sync}
+    total, known, snap, log = {}, {q: {} for q in queue}, {}, {}
+
+    def ap(w):
+        n, c0, c1, st, p0, p1 = w[:6]
+        if len(w) > 6:
+            a0, a1, b0, b1 = w[6]
+            return T[n][p0:p1, a0, b0:b1] if a1 == a0 + 1 else T[n][p0:p1, a0:a1, b0:b1]
+        n, at = LOG[n][:2]
+        c0, c1 = c0 + at, c1 + at
+        return T[n][p0:p1, c0:c1] if st == 1 else T[n][p0:p1, c0:c1:st]
+
+    env = dict(queue, T=T, ap=ap)
+
+    def wait(q, tok):
+        s, v = tok
+        if known[q].get(s, 0) >= v:
+            return
+        queue[q].wait_ge(T.sem[s], v)
+        known[q][s] = v
+        for a, b in snap.get(tok, {}).items():
+            if known[q].get(a, 0) < b:
+                known[q][a] = b
+
+    tokens = {}
+    for rank, n, q in _PLANS["order"]:
+        if rank != r:
+            continue
+        s = n["sem"] or _QS[q]
+        if q != "r":
+            need = {}
+            for ws, isw in ((n["rd"], False), (n["wr"], True)):
+                for w in ws:
+                    for w2, isw2, tok, q2 in log.get(w[0], ()):
+                        if (isw or isw2 or (w[0] in ("pa", "pu") and q != q2)) and meet(w, w2):
+                            need[tok[0]] = max(need.get(tok[0], 0), tok[1])
+            for a in n["after"]:
+                tok = tokens[a["i"]]
+                need[tok[0]] = max(need.get(tok[0], 0), tok[1])
+            for x in sorted(need):
+                wait(q, (x, need[x]))
+            ins = n["fns"][q](env)
+            total[s] = total.get(s, 0) + n["by"]
+            if not n["cast"]:
+                ins.then_inc(T.sem[s], n["by"])
+                snap[(s, total[s])] = dict(known[q])
+        else:
+            total[s] = n["by"]
+        tok = tokens[n["i"]] = (s, total[s])
+        for ws, isw in ((n["rd"], False), (n["wr"], True)):
+            for w in ws:
+                log.setdefault(w[0], []).append((w, isw, tok, q))
     for s in sorted(total):
         wait("g", (s, total[s]))

from concourse.bass import DstId, RemoteDMATransfer
from concourse.mybir import dt, AluOpType as Op, AxisListType, ActivationFunctionType as Act

N, P, K = 4, 256, 64
R1, R2 = 352, 608
BUILD = ((0, 2), (1, 3))
TINY = 2.0 ** -110
UNIT = 32768.0
TUNE = dict(wake=150.0, fac=1.2, load=900.0, issue=60.0, rissue=250.0, hop=700.0, row=12.0, byte=0.06, tol=20.0, bias=60.0)

F, B, I, U16, CODES = "float32", "bfloat16", "int32", "uint16", "float8_e4m3fn_x4"
SCRATCH, LOG, _TOP = {}, {}, {}


def _own(dtype, **kw):
    for n, c in kw.items():
        SCRATCH[n] = ("sbuf", [128, c], dtype)
        LOG[n] = (n, 0, c, dtype)


def _cube(**kw):
    for n, (a, b) in kw.items():
        SCRATCH[n] = ("sbuf", [128, a, b], F)
        LOG[n] = (n, 0, a * b, F)


def _slab(slab, dtype, **kw):
    for n, c in kw.items():
        at = _TOP.get(slab, 0)
        LOG[n] = (slab, at, c, dtype)
        _TOP[slab] = at + (c + 15) // 16 * 16
        SCRATCH[slab] = ("sbuf", [128, _TOP[slab]], dtype)


_own(B, onb=512, tbt=1040, ut=512, wt=1024, eb=2048, ub0=512, ub1=512, h0=512, h1=512)
for _n, _c in dict(tq=256, tw=512, tx=768, uq=128, uc=128, ug=128, eq=512, wq=256, tz=256, sla=64, slb=64,
                   laa=128, lab=128, psa=128, psb=128, ou=256).items():
    _own(CODES, **{_n: _c})
    _own("uint8", **{_n + "_s": _c})
for _n in ("pa", "pu"):
    SCRATCH[_n] = ("psum", [128, 2048], F)
    LOG[_n] = (_n, 0, 2048, F)
_own(F, l0=16, l1=16, xs=256, xd=128, ys=512, fr=640, ft=512)
_cube(row0=(2, 128), row1=(2, 128), kt=(4, 32), mm0=(4, 64), mm1=(4, 64))
_slab("fs", F, jc=2, jp0=2, jp1=2, jp2=2, jpb=2, cf=12, rr=16, rh=8, rk8=8, wm=16, nq=8, ca=8, cb=8, c1=8, c2=8, c3=8, c4=8,
      s1=8, s2=8, s3=8, s4=8, s5=8, wl=8, wa=3, wb=1, wc=1, wd=3, wl1=6, ma=12, mb=12, m0=16, rho=4, csf=8, cso=2, gm=40, mrow=32,
      kf=2, kg=2, tr=8, ofrf=4, va=128, vb=128, d0a=8, d0b=8, oh=512, prc=520, prg=390, rep=8, nrep=8, kra=12, krb=12, kro=16, kr0=16,
      pm=130, src1=2, oho=128, sqc=8, gq=6, lr=128, bsf=256, junk=4096)
for _t in "01":
    _slab("fs", F, **{n + _t: c for n, c in dict(sq=16, sc=16, ex=64, sa=2, nd=2, dl=2, th=80, cm=544, po=2, mt=256, lw=4, ab=4, ac=4,
                                                 ga=8, gx=2, gy=8, ge=8, gw=8, gn=2, pay=2, er=64).items()})
    _slab("is_", I, **{n + _t: c for n, c in dict(wj=4, rk=6, fi=4, fj=4, fk=4, fa=8, fl=4, fm=4, fe=4, fo=8).items()})
    _slab("us", U16, **{n + _t: c for n, c in dict(off=4, rfo=6, ofs=8, exo=4).items()})
_slab("is_", I, bi=128, key=64, bj=256, ji=2, jj=2, pi=4, ci=12, csi=8, csj=8, tri32=8)
_slab("us", U16, ofr=4, ofu=32, ofv=32, fou=16)

SEMAPHORES = ["sv", "ss", "st", "sg", "dl_u", "dl_t0", "dl_t1", "dl_t2", "dl_w", "dl_x", "dl_x_s", "dl_m", "dl_m_s", "dl_n", "dl_n_s",
              "dbs", "dy0", "dy1", "doc", "ls", "a0", "a1", "ha0", "ha1", "hb0", "hb1"]
_QS = {"v": "sv", "s": "ss", "t": "st", "g": "sg"}
_PLANS = {}


def W(name, c0=0, c1=None, step=1, p0=0, p1=128):
    return (name, c0, LOG[name][2] if c1 is None else c1, step, p0, p1)


def C(name, a0, a1, b0, b1, p0=0, p1=128):
    return (name, 0, LOG[name][2], 1, p0, p1, (a0, a1, b0, b1))


def width(w):
    if len(w) > 6:
        a0, a1, b0, b1 = w[6]
        return (a1 - a0) * (b1 - b0)
    return len(range(w[1], w[2], w[3]))


def meet(a, b):
    if a[4] >= b[5] or b[4] >= a[5]:
        return False
    if a[0] in ("pa", "pu"):
        return a[1] // 512 <= (b[2] - 1) // 512 and b[1] // 512 <= (a[2] - 1) // 512
    if len(a) > 6 and len(b) > 6:
        x, y = a[6], b[6]
        return x[0] < y[1] and y[0] < x[1] and x[2] < y[3] and y[2] < x[3]
    if a[1] >= b[2] or b[1] >= a[2]:
        return False
    return not (a[3] == b[3] and a[3] > 1 and (a[1] - b[1]) % a[3])


def calls(r, cores, topo):
    core = cores[r]
    nodes = []
    cyc = 0.83 * TUNE["fac"]

    def node(rd, wr, fns, cost, sem=None, by=1, lag=0.0, after=(), to=(), cast=False):
        nodes.append(dict(rd=rd, wr=wr, fns=fns, cost=cost, sem=sem, by=by, lag=lag, after=list(after), to=to, cast=cast, i=len(nodes)))
        return nodes[-1]

    def small(n):
        return max(64, n) * cyc

    def tt(out, a, b, op):
        both = a[0] not in ("pa", "pu") and b[0] not in ("pa", "pu")
        return node([a, b], [out], {"v": lambda e: e["v"].tensor_tensor(e["ap"](out), e["ap"](a), e["ap"](b), op)},
                    {"v": small(width(out) * (2 if both else 1))})

    def ts(out, a, s1, op0, s2=None, op1=None):
        rd = [a] + [s for s in (s1, s2) if isinstance(s, tuple)]

        def f(e):
            x1, x2 = [e["ap"](s) if isinstance(s, tuple) else s for s in (s1, s2)]
            if op1 is not None:
                return e["v"].tensor_scalar(e["ap"](out), e["ap"](a), x1, x2, op0, op1)
            return e["v"].tensor_scalar(e["ap"](out), e["ap"](a), x1, None, op0)
        return node(rd, [out], {"v": f}, {"v": small(width(out))})

    def cp(out, a, q="v"):
        fns = {"v": lambda e: e["v"].tensor_copy(e["ap"](out), e["ap"](a)), "s": lambda e: e["s"].activation(e["ap"](out), e["ap"](a), Act.Copy)}
        return node([a], [out], {x: fns[x] for x in q}, {x: small(width(out)) for x in q})

    def red(out, a, op):
        return node([a], [out], {"v": lambda e: e["v"].tensor_reduce(e["ap"](out), e["ap"](a), AxisListType.X, op)}, {"v": small(width(a))})

    def fill(out, c):
        return node([], [out], {"v": lambda e: e["v"].memset(e["ap"](out), c)}, {"v": small(width(out) * (0.5 if LOG[out[0]][3] in (B, U16) else 1))})

    def turn(out, a):
        return node([a], [out], {"v": lambda e: e["v"].transpose(e["ap"](out), e["ap"](a))}, {"v": small(width(a))})

    def scan(out, d0, d1):
        return node([d0, d1], [out], {"v": lambda e: e["v"].tensor_tensor_scan(e["ap"](out), e["ap"](d0), e["ap"](d1), 0.0, Op.mult, Op.subtract)},
                    {"v": small(width(out))})

    def act(out, a, f, off=None):
        rd = [a] + [w for w in (off,) if w is not None]
        n = width(out)
        return node(rd, [out], {"s": lambda e: e["s"].activation(e["ap"](out), e["ap"](a) if off is None else e["ap"](a).indirect(e["ap"](off)), f)},
                    {"s": small(n) if off is None else (65 + 1.56 * 0.83 * n) * TUNE["fac"]})

    junk = [0]

    def total(out, a, q="vs"):
        n = width(a)
        j = W("junk", junk[0], junk[0] + n)
        junk[0] += n
        fns = {"v": lambda e: e["v"].tensor_reduce(e["ap"](out), e["ap"](a), AxisListType.X, Op.add),
               "s": lambda e: e["s"].activation(e["ap"](j), e["ap"](a), Act.Copy, accum_out=e["ap"](out))}
        return node([a], [out, j], {x: fns[x] for x in q}, {x: small(n) + (20 if x == "s" else 0) for x in q})

    def iota(out, pattern, base=0, cm=0):
        kw = {} if LOG[out[0]][3] == I else {"allow_small_or_imprecise_dtypes": True}
        return node([], [out], {"g": lambda e: e["g"].iota(e["ap"](out), pattern, base, cm, **kw)}, {"g": 130 * TUNE["fac"] + 2 * cyc * width(out)})

    def quant(name, c0, src, s0, n):
        q, s, x = W(name, c0, c0 + n), W(name + "_s", c0, c0 + n), W(src, s0, s0 + 4 * n)
        return node([x], [q, s], {"v": lambda e: e["v"].quantize_mx(e["ap"](q), e["ap"](s), e["ap"](x))}, {"v": (12 + 0.88 * n) * TUNE["fac"]})

    def mm(bank, lhs, l0, rhs, r0, n=128):
        rd = [W(lhs, l0, l0 + 128), W(lhs + "_s", l0, l0 + 128), W(rhs, r0, r0 + n), W(rhs + "_s", r0, r0 + n)]
        o = W("pu" if bank > 3 else "pa", 512 * (bank % 4), 512 * (bank % 4) + n)
        return node(rd, [o], {"t": lambda e: e["t"].matmul_mx(e["ap"](o), e["ap"](rd[0]), e["ap"](rd[1]), e["ap"](rd[2]), e["ap"](rd[3]), True, True)},
                    {"t": 1.3 * (n + 16) * cyc})

    def pick(dst, d0, src, width_, off, o0, n):
        o, a, f = W(dst, d0, d0 + n), W(src, 0, width_), W(off, o0, o0 + n // 16)
        node([a, f], [o], {"v": lambda e: e["v"].tensor_copy(e["ap"](o).bitcast(dt.uint32), e["ap"](a).bitcast(dt.uint32).indirect(e["ap"](f)))},
             {"v": (50 + 1.56 * 0.83 * n) * TUNE["fac"]})
        act(W(dst + "_s", d0, d0 + n), W(src + "_s", 0, width_), Act.Copy, off=f)

    def raw(e, w):
        return e["ap"](w).bitcast(dt.uint8) if LOG[w[0]][3] == CODES else e["ap"](w)

    def load(q, w, tensor, c0, c1, sem, first=()):
        return node(list(first), [w], {q: lambda e: e[q].dma_start(e["ap"](w), e["T"][tensor][:, c0:c1])}, {q: TUNE["issue"]}, sem, 16, TUNE["load"])

    def move(q, out, a, sem):
        return node([a], [out], {q: lambda e: e[q].dma_start(raw(e, out), raw(e, a))}, {q: TUNE["issue"]}, sem, 16, TUNE["load"])

    def store(q, dst, a, sem):
        return node([a], [], {q: lambda e: e[q].dma_start(dst(e["T"]), raw(e, a))}, {q: TUNE["issue"]}, sem, 16, TUNE["load"])

    peers = [c for c in cores if c != core]

    def mask(engs):
        m = 0
        for e in engs:
            m |= 1 << e
        return m

    def send(parts, sem, after=()):
        def did(c):
            a = topo.addr(c)
            return DstId(rid=a[0], pnc=a[1])

        def f(e):
            return e["g"].remote_dma_fused([RemoteDMATransfer(dst_ids=[did(c) for c in cs], dma_engine_mask=mask(es), remote_sem=e["T"].sem[sem],
                                                              srcs=[raw(e, a)], dsts=[raw(e, b)] * len(cs)) for a, b, cs, es in parts],
                                           local_sem=e["T"].sem["ls"])
        lag = 0.0
        for a, b, cs, es in parts:
            row = width(a) * {F: 4, CODES: 4}.get(LOG[a[0]][3], 1)
            lag = max(lag, TUNE["hop"] + 128 // len(es) * len(cs) * (TUNE["row"] + row * TUNE["byte"]))
        return node([p[0] for p in parts], [], {"g": f}, {"g": TUNE["rissue"]}, "ls", sum(len(p[3]) for p in parts), lag, after,
                    [(cores.index(c), sem) for p in parts for c in p[2]], True)

    def lands(sem, count, views):
        return node([], views, {"r": None}, {"r": 0.0}, sem, count)

    alle = topo.engines(core, peers[0])

    load("y", W("ut", 0, 8), "u", 0, 8, "dl_u")
    load("y", W("tbt", 0, 512), "tb", 0, 512, "dl_t0")
    load("s", W("tbt", 512, 1024), "tb", 512, 1024, "dl_t1")

    iota(W("pi", 0, 1), [[0, 1]], 0, 1)
    iota(W("pi", 1, 2), [[0, 1]], 1, 1)
    iota(W("pi", 2, 4), [[128, 2]], r, 1)
    iota(W("jc"), [[128, 2]], 0, 1)
    iota(W("rr"), [[1, 4], [0, 4]])
    iota(W("rh"), [[1, 4], [0, 2]])
    iota(W("rk8"), [[0, 2], [1, 4]])
    iota(W("mrow"), [[1, 32]])
    fill(W("ut", 8, 512), 0.0)
    fill(W("onb"), 1.0)

    def unit(b):
        o = W("eb", 512 * b, 512 * b + 512)
        node([W("onb")], [o], {"g": lambda e: e["g"].affine_select(e["ap"](o), e["ap"](W("onb")), [[-8, 128], [-1, 4]], Op.is_equal, 0.0, b, 8)},
             {"g": 170 * TUNE["fac"] + 1024 * cyc})
    for b in range(4):
        unit(b)
    for y in range(4):
        iota(C("kt", y, y + 1, 0, 32), [[0, 2], [1, 16]], 16 * y)
    iota(W("kf"), [[16, 2]])
    iota(W("tr"), [[16, 8]], 512)
    iota(W("ofrf"), [[2, 2], [0, 2]])

    pp = W("pi", 0, 1)
    ts(W("ci", 0, 2), W("pi", 0, 2), 3, Op.bitwise_and)
    ts(W("ci", 2, 3), pp, 15, Op.bitwise_and)
    ts(W("ci", 3, 4), pp, 4, Op.arith_shift_right, 1, Op.bitwise_and)
    ts(W("ci", 4, 6), W("pi", 2, 4), 255, Op.bitwise_and)
    ts(W("ci", 6, 7), pp, 31, Op.bitwise_and)
    ts(W("ci", 7, 8), pp, 5, Op.arith_shift_right, 1, Op.bitwise_and)
    ts(W("ci", 8, 9), pp, 6, Op.arith_shift_right)
    fill(W("exo0", 0, 2), 14)
    fill(W("exo0", 2, 4), 15)
    fill(W("d0a"), 1.0)
    fill(W("d0a", 0, 1), 0.0)
    fill(W("d0a", 4, 5), -1.0)
    cp(W("cf", 0, 9), W("ci", 0, 9))
    q0, q1, xf, gf, i1 = W("cf", 0, 1), W("cf", 1, 2), W("cf", 2, 3), W("cf", 3, 4), W("cf", 4, 6)
    ts(W("wm", 0, 8), W("rh"), q0, Op.is_equal)
    ts(W("wm", 8, 16), W("rh"), q0, Op.not_equal)
    fill(W("gm", 2, 3), 1.0)
    ts(W("gm", 0, 2), W("cf", 7, 9), -1.0, Op.mult, 1.0, Op.add)
    ts(W("gm", 3, 35), W("mrow"), W("cf", 6, 7), Op.is_ge)

    quant("uq", 0, "ut", 0, 128)
    quant("tq", 0, "tbt", 0, 128)
    mm(0, "tq", 0, "uq", 0)
    quant("tq", 128, "tbt", 512, 128)
    mm(1, "tq", 128, "uq", 0)

    def mine(l, bank):
        for h in range(2):
            o = 512 * (bank + h)
            cp(W(l, 4 * r + 2 * h, 4 * r + 2 * h + 1), W("pa", o, o + 1), "s")
            act(W(l, 4 * r + 2 * h + 1, 4 * r + 2 * h + 2), W("pa", o + 1, o + 2), Act.Abs)
        v = W(l, 4 * r, 4 * r + 4)
        send([(v, v, peers, alle)], "a" + l[1])

    mine("l0", 0)
    lands("a0", 3 * len(alle), [W("l0", 4 * o, 4 * o + 4) for o in range(N) if o != r])

    if r:
        load("y", W("tbt", 1024, 1040), "tb", 0, 16, "dl_t2")
        quant("tz", 0, "tbt", 4 * r, 256)
        mm(2, "tz", 0, "uq", 0)
        mm(3, "tz", 128, "uq", 0)
        mine("l1", 2)
    lands("a1", len(alle) * (3 if r == 0 else 2), [W("l1", 4 * o, 4 * o + 4) for o in range(1, N) if o != r])

    u1, u2, u3 = 4096 / UNIT, 1024 / UNIT, 256 / UNIT
    ts(W("nq"), W("rk8"), q0, Op.not_equal)
    ts(W("ca"), W("rk8"), q0, Op.min)
    ts(W("cb"), W("rk8"), q0, Op.max)
    ts(W("s4"), W("rk8"), u1, Op.mult, 3 * u3 - 0.5, Op.add)
    ts(W("c1"), W("ca"), 0.0, Op.is_equal, u2, Op.mult)
    ts(W("c2"), W("cb"), 1.0, Op.is_equal, 1.0, Op.add)
    ts(W("c3"), W("cb"), 3.0, Op.is_equal, -u3, Op.mult)
    ts(W("c4"), W("ca"), 2.0, Op.is_equal, 1.0, Op.add)
    tt(W("s1"), W("c1"), W("c2"), Op.mult)
    tt(W("s2"), W("c3"), W("c4"), Op.mult)
    tt(W("s3"), W("s1"), W("s4"), Op.add)
    tt(W("s5"), W("s3"), W("s2"), Op.add)
    tt(W("wl"), W("s5"), W("nq"), Op.mult)
    ts(W("jp1"), W("jc"), 1.0 / UNIT, Op.mult, 0.5, Op.add)
    tt(W("jp0"), W("jc"), W("jp1"), Op.add)

    ts(W("ofu"), W("mrow"), 0.0, Op.is_ge, q0, Op.mult)
    ts(W("ofv"), W("ofu"), 4.0, Op.add)
    ready = [quant("tw", 320, "tbt", 0, 128)]
    act(W("ub0"), W("ut"), Act.Copy, off=W("ofu"))
    act(W("ub1"), W("ut"), Act.Copy, off=W("ofv"))
    iota(W("va"), [[0, 2], [1, 64]], R1)
    iota(W("vb"), [[0, 2], [1, 64]], R2)
    iota(W("fr", 0, 512), [[16, 16], [0, 2], [1, 16]])
    fill(W("fr", 512, 640), 0.0)
    ts(W("kg"), W("kf"), xf, Op.add)
    ts(W("ofr"), W("ofrf"), gf, Op.add)
    ts(W("tri32"), W("tr"), xf, Op.add)
    when = 0 if r in BUILD[0] else 1
    quant("eq", 0, "eb", 0, 512)
    quant(("psa", "psb")[when], 0, "tbt", 0, 128)
    cp(W(("h0", "h1")[when]), W("tbt", 0, 512), "vs")
    for x in ("", "_s"):
        move("y", W("tw" + x, 0, 256), W("tq" + x), "dl_m" + x)
    quant("uc", 0, "ub0", 0, 128)
    quant("ug", 0, "ub1", 0, 128)
    load("y", W("wt"), "w", 0, 1024, "dl_w", [W("l0")])
    for x in ("", "_s"):
        move("y", W("tx" + x, 0, 256), W("tq" + x), "dl_n" + x)
    quant("wq", 0, "wt", 0, 256)

    ts(W("ma"), W("rr", 0, 12), q1, Op.is_lt)
    ts(W("mb"), W("rr", 0, 12), q1, Op.is_ge)
    ts(W("m0"), W("rr"), q1, Op.is_equal)
    cp(W("rho", 0, 1), q1)
    tt(W("rho", 1, 4), W("rr", 0, 12, 4), W("mb", 0, 12, 4), Op.add)
    r1, r2, r3 = W("rho", 1, 2), W("rho", 2, 3), W("rho", 3, 4)
    ts(W("wa"), W("rho", 1, 4), u1, Op.mult, -0.5, Op.add)
    ts(W("wb"), r1, u2, Op.mult)
    ts(W("wc"), r3, u3, Op.mult)
    ts(W("wd", 0, 1), r2, u2, Op.mult, W("wa", 0, 1), Op.add)
    ts(W("wd", 1, 3), W("wa", 1, 3), W("wb"), Op.add)
    for h in range(2):
        ts(W("wl1", 3 * h, 3 * h + 2), W("wd", 0, 2), W("wc"), Op.add)
        ts(W("wl1", 3 * h + 2, 3 * h + 3), r2, u3, Op.mult, W("wd", 2, 3), Op.add)
    fill(W("d0b"), 1.0)
    fill(W("d0b", 0, 8, 4), 0.0)
    fill(W("d0b", 1, 8, 4), -1.0)
    fill(W("exo1", 0, 2), 3)
    fill(W("exo1", 2, 4), 7)
    for h in range(2):
        ts(W("csi", 4 * h, 4 * h + 4), W("rho"), 4097.0, Op.mult, W("jc", h, h + 1), Op.add)
    ts(W("csj"), W("csi"), 3 * 4096 + 255, Op.bitwise_and)
    cp(W("csf"), W("csj"))
    ts(W("cso"), i1, 4096.0 * r, Op.add)
    ts(W("ji"), W("jc"), 1.0, Op.add)
    ts(W("jj"), W("ji"), 255, Op.bitwise_and)
    ts(W("jp2"), W("jj"), 1.0 / UNIT, Op.mult, 0.5, Op.add)
    cp(W("pm", 64, 130, 65), W("cf", 4, 6), "vs")

    cp(W("l1", 0, 4), W("l0", 0, 4), "vs")
    tt(W("krb"), W("l1", 4, 16), W("mb"), Op.mult)
    tt(W("kra"), W("l1", 0, 12), W("ma"), Op.mult)
    tt(W("kr0"), W("l1"), W("m0"), Op.mult)
    tt(W("kro", 4, 16), W("kra"), W("krb"), Op.add)
    for h in range(2):
        red(W("kro", 2 * h, 2 * h + 1), W("kr0", 2 * h, 16, 4), Op.add)

    def count(t):
        n = str(t)
        src, off = (W("sc0"), W("exo0")) if t == 0 else (W("sc1", 0, 8), W("exo1"))
        s2 = W("sc0", 14, 16) if t == 0 else W("sc1", 3, 8, 4)
        rn, th, cm = "row" + n, "th" + n, "cm" + n
        act(W("ex" + n), src, Act.Abs, off=off)
        act(W("sa" + n), s2, Act.Abs)
        for h in range(2):
            turn(C(rn, h, h + 1, 0, 32), W("ex" + n, 32 * h, 32 * h + 32))
        for h in range(2):
            s = W("sa" + n, h, h + 1)
            ts(W("nd" + n, h, h + 1), s, 1.5 * 2.0 ** -24, Op.mult, s, Op.add)
            ts(W("dl" + n, h, h + 1), W("nd" + n, h, h + 1), TINY, Op.max, W("sa" + n, h, h + 1), Op.subtract)
        for a in range(2):
            cp(C(rn, 0, 2, 64, 96, 64 * a, 64 * a + 64), C(rn, 0, 2, 0, 32, 64 - 64 * a, 128 - 64 * a), "vs")
        for x in (1, 3):
            for a in range(4):
                b = a ^ x
                cp(C(rn, 0, 2, 32 * x, 32 * x + 32, 32 * a, 32 * a + 32), C(rn, 0, 2, 0, 32, 32 * b, 32 * b + 32), "vs")
        for h in range(2):
            ts(W(th, 40 * h, 40 * h + 35), W("gm", 0, 35), W("dl" + n, h, h + 1), Op.mult, W("sa" + n, h, h + 1), Op.add)
        for h in range(2):
            tt(W(cm, 272 * h + 232, 272 * h + 264), C(rn, h, h + 1, 0, 32), W(th, 40 * h + 3, 40 * h + 35), Op.is_ge)
            ts(W(cm, 272 * h + 200, 272 * h + 232), C(rn, h, h + 1, 32, 64), W(th, 40 * h, 40 * h + 1), Op.is_ge)
            other = W(th, 2, 3) if h == 0 else W("sa" + n, 1, 2)
            ts(W(cm, 272 * h, 272 * h + 128), C(rn, 1 - h, 2 - h, 0, 128), other, Op.is_ge)
            ts(W(cm, 272 * h + 128, 272 * h + 192), C(rn, h, h + 1, 64, 128), W(th, 40 * h + 1, 40 * h + 2), Op.is_ge)
            total(W(cm, 272 * h + 192, 272 * h + 193), W(cm, 272 * h + 200, 272 * h + 264))
            total(W("po" + n, h, h + 1), W(cm, 272 * h, 272 * h + 193))

    def listed(t):
        m, mt, lw, b, c = [x + str(t) for x in ("mm", "mt", "lw", "ab", "ac")]
        for h in range(2):
            ts(C(m, 0, 4, 32 * h, 32 * h + 32), C("kt", 0, 4, 0, 32), W("po%d" % t, h, h + 1), Op.is_equal, W("pay%d" % t, h, h + 1), Op.mult)
        for y in range(4):
            turn(W(mt, 64 * y, 64 * y + 64), C(m, y, y + 1, 0, 64))
        for y in range(4):
            total(W(lw, y, y + 1), W(mt, 64 * y, 64 * y + 64))
        for k in range(4):
            tt(W(b, 0, 4, 1, 32 * k, 32 * k + 32), W(lw, 0, 4, 1, 32 * k, 32 * k + 32), W(lw, 0, 4, 1, 32 * (k ^ 1), 32 * (k ^ 1) + 32), Op.add)
        for k in range(2):
            tt(W(c, 0, 4, 1, 64 * k, 64 * k + 64), W(b, 0, 4, 1, 64 * k, 64 * k + 64), W(b, 0, 4, 1, 64 - 64 * k, 128 - 64 * k), Op.add)
        return W(c, 0, 4)

    def lost(t, n, wl, base):
        k = n // 2
        s = str(t)

        def size(h):
            return W("gy0", h, 8, 2) if t == 0 else W("ga1", k * h, k * h + k)
        for h in range(2):
            red(W("gx" + s, h, h + 1), size(h), Op.max)
        for h in range(2):
            ts(W("ge" + s, k * h, k * h + k), size(h), W("gx" + s, h, h + 1), Op.is_equal)
        tt(W("gw" + s, 0, n), W("ge" + s, 0, n), W(wl), Op.mult)
        for h in range(2):
            red(W("gn" + s, h, h + 1), W("gw" + s, k * h, k * h + k), Op.min)
        tt(W("pay" + s), W("gn" + s), W(base), Op.add)

    def gather(t, lists):
        n = "ab"[t]
        src, width_ = (("tq", 256), ("tw", 448))[t]
        off = "off%d" % t
        cp(W(off), lists)
        sl, la = "sl" + n, "la" + n
        bs = BUILD[t]
        if r in bs:
            d = bs.index(r)
            o = 1 - d
            pick(sl, 32 * o, src, width_, off, 2 * o, 32)
            to = cores[bs[o]]
            for s in ("", "_s"):
                send([(W(sl + s, 32 * o, 32 * o + 32), W(la + s, 32 * r, 32 * r + 32), [to], topo.engines(core, to))], "ha%d" % t, ready)
            pick(la, 32 * r, src, width_, off, 2 * d, 32)
            cnt = 0
            for i in range(N):
                if i != r:
                    cnt += 2 * len(topo.engines(cores[i], core)) // (1 if i in bs else 2)
            lands("ha%d" % t, cnt, [W(la + s, 32 * i, 32 * i + 32) for s in ("", "_s") for i in range(N) if i != r])
        else:
            pick(sl, 0, src, width_, off, 0, 64)
            for s in ("", "_s"):
                send([(W(sl + s, 32 * d, 32 * d + 32), W(la + s, 32 * r, 32 * r + 32), [cores[bs[d]]], topo.engines(core, cores[bs[d]])[d::2])
                      for d in range(2)], "ha%d" % t, ready)

    def numbers(t, w):
        ts(W("wj%d" % t), w, UNIT, Op.mult)

    def buildlist(t):
        s, d = str(t), BUILD[t].index(r)
        v = W("wj" + s, 2 * d, 2 * d + 2)
        ts(W("rk" + s, 0, 2), v, 3, Op.bitwise_and)
        ts(W("rk" + s, 2, 4), v, 10, Op.arith_shift_right, 3, Op.bitwise_and)
        ts(W("rk" + s, 4, 6), v, 8, Op.arith_shift_right, 3, Op.bitwise_and)
        for y in range(2):
            ts(W("rfo" + s, y, 6, 2), W("rk" + s, y, 6, 2), 32.0, Op.mult, W("kg", y, y + 1), Op.add)

    def build(t):
        s, n, d = str(t), "ab"[t], BUILD[t].index(r)
        la, ps, hh = "la" + n, "ps" + n, "h" + s
        pick(ps, 0, la, 128, "rfo" + s, 0, 96)
        for b in range(4):
            mm(4 + b, "eq", 128 * b, ps, 0)
        at = 96 if d == 0 else 0
        for b in range(4):
            cp(W("xs", 64 * b, 64 * b + 64), W("pu", 512 * b + 32, 512 * b + 96), "s")
            tt(W("xd", 32 * b, 32 * b + 32), W("pu", 512 * b, 512 * b + 32), W("xs", 64 * b, 64 * b + 32), Op.subtract)
            tt(W(hh, 4 * at + b, 4 * at + 128, 4), W("xd", 32 * b, 32 * b + 32), W("xs", 64 * b + 32, 64 * b + 64), Op.subtract)
        dst, base = ("tw", 256) if t == 0 else ("tx", 512)
        quant(dst, base + 128 * d, hh, 0, 128)
        c = base + 96 + 32 * d
        for x in ("", "_s"):
            v = W(dst + x, c, c + 32)
            send([(v, v, peers, alle)], "hb%d" % t)

    def built(t):
        dst, base = ("tw", 256) if t == 0 else ("tx", 512)
        lands("hb%d" % t, sum(2 * len(topo.engines(cores[b], core)) for b in BUILD[t] if b != r),
              [W(dst + x, base + 96 + 32 * d, base + 128 + 32 * d) for x in ("", "_s") for d in range(2) if BUILD[t][d] != r])

    def mapped(t):
        s = str(t)
        i, a = W("fi" + s), W("wj" + s)
        ts(W("fl" + s), a, 12, Op.arith_shift_right, 3, Op.bitwise_and)
        if t and r != 1:
            ts(W("fj" + s), a, float(r - 1), Op.add)
            a = W("fj" + s)
        ts(i, a, 255, Op.bitwise_and)
        ts(W("fk" + s), a, 240, Op.bitwise_and)
        ts(W("fm" + s), W("fl" + s), float(r), Op.not_equal, 4096.0, Op.mult)
        tt(W("fe" + s), i, W("fk" + s), Op.add)
        tt(W("fa" + s, 0, 4), W("fe" + s), W("fm" + s), Op.add)
        ts(W("fa" + s, 4, 8), W("fa" + s, 0, 4), 16.0, Op.add)
        tt(W("fo" + s), W("fa" + s), W("tri32"), Op.min)
        cp(W("ofs" + s), W("fo" + s))

    def enter(t):
        win, off, src = W("fr"), W("ofs%d" % t), W("va" if t == 0 else "vb")
        node([off, src], [win], {"v": lambda e: e["v"].tensor_copy(e["ap"](win).indirect(e["ap"](off)), e["ap"](src))},
             {"v": (50 + 3 * 0.83 * 128) * TUNE["fac"]})

    def listrow(t, w):
        s = str(t)
        act(W("er" + s), w, Act.Copy, off=W("ofr"))
        turn(W("lr", 64 * t, 64 * t + 64), W("er" + s))
        ts(W("bi", 64 * t, 64 * t + 64), W("lr", 64 * t, 64 * t + 64), UNIT, Op.mult, -1.0 * t, Op.add)

    def stripes(t):
        o = 128 * t
        b = W("bi", 64 * t, 64 * t + 64, 1, 0, 1)
        ts(W("bj", o, o + 64, 1, 0, 1), b, 255, Op.bitwise_and)
        ts(W("bj", o + 64, o + 128, 1, 0, 1), b, 12, Op.arith_shift_right, 3, Op.bitwise_and)
        cp(W("bsf", o, o + 128, 1, 0, 1), W("bj", o, o + 128, 1, 0, 1))

    for m in range(2):
        tt(W("sq0", 8 * m, 8 * m + 8), W("l0", 0, 16, 2), W("wm", 8 * m, 8 * m + 8), Op.mult)
    for h in range(2):
        scan(W("sc0", h, 16, 2), W("d0a"), W("sq0", h, 16, 2))
    tt(W("gy0"), W("l0", 1, 16, 2), W("wm", 8, 16), Op.mult)
    lost(0, 8, "wl", "jp0")
    count(0)
    w0 = listed(0)
    gather(0, w0)
    numbers(0, w0)
    if r in BUILD[0]:
        buildlist(0)
        build(0)
    built(0)
    listrow(0, w0)
    ts(W("key"), W("bi", 0, 64), 3 * 4096 + 255, Op.bitwise_and)
    mapped(0)
    enter(0)
    for e in range(8):
        ts(W("oh", 64 * e, 64 * e + 64), W("key"), W("csf", e, e + 1), Op.is_equal)
    for e in range(8):
        total(W("rep", e, e + 1), W("oh", 64 * e, 64 * e + 64))
    for h in range(2):
        ts(W("oho", 64 * h, 64 * h + 64), W("key"), W("cso", h, h + 1), Op.is_equal)
        tt(W("pm", 65 * h, 65 * h + 64), W("oho", 64 * h, 64 * h + 64), W("va", 0, 64), Op.mult)
        red(W("src1", h, h + 1), W("pm", 65 * h, 65 * h + 65), Op.max)
    ts(W("nrep"), W("rep"), -1.0, Op.mult, 1.0, Op.add)
    tt(W("jpb"), W("src1"), W("jp2"), Op.add)
    for h in range(2):
        tt(W("prc", 260 * h + 64, 260 * h + 260, 65), W("kro", 2 * h, 16, 4), W("nrep", 4 * h, 4 * h + 4), Op.mult)
        tt(W("prg", 195 * h + 64, 195 * h + 195, 65), W("kro", 4 + 2 * h + 1, 16, 4), W("nrep", 4 * h + 1, 4 * h + 4), Op.mult)

    mm(0, "uc", 0, "tw", 320)
    mm(1, "ug", 0, "tw", 320)
    for e in range(8):
        tt(W("prc", 65 * e, 65 * e + 64), W("pa", 32, 96), W("oh", 64 * e, 64 * e + 64), Op.mult)
        total(W("sqc", e, e + 1), W("prc", 65 * e, 65 * e + 65))
    scan(W("sc1", 0, 8), W("d0b"), W("sqc"))
    for e in range(6):
        o = 64 * (4 * (e // 3) + e % 3 + 1)
        tt(W("prg", 65 * e, 65 * e + 64), W("pa", 544, 608), W("oh", o, o + 64), Op.mult)
        total(W("gq", e, e + 1), W("prg", 65 * e, 65 * e + 65))
    act(W("ga1", 0, 6), W("gq"), Act.Abs)
    lost(1, 6, "wl1", "jpb")
    count(1)
    w1 = listed(1)
    gather(1, w1)
    numbers(1, w1)
    if r in BUILD[1]:
        buildlist(1)
        build(1)
    mapped(1)
    built(1)
    for x in ("", "_s"):
        move("y", W("tx" + x, R1, R1 + 64), W("tw" + x, R1, R1 + 64), "dl_x" + x)
    enter(1)
    turn(W("ft"), W("fr", 0, 512))
    cp(W("fou"), W("ft", 0, 512, 32))
    listrow(1, w1)
    for t in range(2):
        stripes(t)
    store("y", lambda T: T.bs[:, :], W("bsf", 0, 256, 1, 0, 1), "dbs")

    for c in range(2):
        pick("ou", 128 * c, "tx", 672, "fou", 8 * c, 128)
        for o in range(2):
            mm(2 * c + o, "wq", 128 * o, "ou", 128 * c)

    def scales(k):
        store("y", lambda T: T.osc[4 * k:4 * k + 4, 0:256], W("ou_s", 0, 256, 1, 32 * k, 32 * k + 4), "doc")

    def block(c, o):
        a, b = 256 * o + 128 * c, 256 * o + 128 * c + 128
        cp(W("ys", a, b), W("pa", 512 * (2 * c + o), 512 * (2 * c + o) + 128), "vs"[o])
        store("ys"[o], lambda T: T.y[:, a:b], W("ys", a, b), "dy%d" % o)

    store("y", lambda T: T.oc[:, 0:1024], W("ou"), "doc")
    for k in range(4):
        scales(k)
    for c in range(2):
        for o in range(2):
            block(c, o)
    return nodes


def arrange(plans):
    wake = TUNE["wake"]
    flat, base = [], []
    for r, ns in enumerate(plans):
        base.append(len(flat))
        for n in ns:
            flat.append((r, n))
    pred = [set() for _ in flat]
    for r, ns in enumerate(plans):
        log = {}
        for n in ns:
            me = base[r] + n["i"]
            qs = list(n["fns"])
            for ws, isw in ((n["rd"], False), (n["wr"], True)):
                for w in ws:
                    for w2, isw2, j, qs2 in log.get(w[0], ()):
                        if (isw or isw2 or (w[0] in ("pa", "pu") and (len(qs) > 1 or qs != qs2))) and meet(w, w2):
                            pred[me].add(j)
            for ws, isw in ((n["rd"], False), (n["wr"], True)):
                for w in ws:
                    log.setdefault(w[0], []).append((w, isw, me, qs))
            for a in n["after"]:
                pred[me].add(base[r] + a["i"])
            pred[me].discard(me)
    sends = {}
    for k, (r, n) in enumerate(flat):
        for to in n["to"]:
            sends.setdefault(to, []).append(k)
    for k, (r, n) in enumerate(flat):
        if "r" in n["fns"]:
            pred[k].update(sends.get((r, n["sem"]), ()))
    succ = [[] for _ in flat]
    for k, ps in enumerate(pred):
        for j in ps:
            succ[j].append(k)

    def after(j, k):
        return flat[j][1]["lag"] + (0.0 if "r" in flat[k][1]["fns"] else wake)
    left = [len(s) for s in succ]
    way = [0.0] * len(flat)
    todo = [k for k in range(len(flat)) if not left[k]]
    while todo:
        k = todo.pop()
        n = flat[k][1]
        way[k] = min(n["cost"].values()) + max([n["lag"]] + [after(k, j) + way[j] for j in succ[k]])
        for j in pred[k]:
            left[j] -= 1
            if not left[j]:
                todo.append(j)

    count = [len(p) for p in pred]
    when, free, ready, best, out = [0.0] * len(flat), {}, {}, {}, []

    def choose(q):
        f = free.get(q, 0.0)
        top, at = None, 0.0
        for k in sorted(ready[q], key=lambda k: (-way[k], k)):
            s = max(f, when[k])
            if top is None or (s < at and s + flat[k][1]["cost"][q[1]] <= at + TUNE["tol"]):
                top, at = k, s
        best[q] = (at, top)
        if top is None:
            del best[q]

    def put(k):
        for q in flat[k][1]["fns"]:
            ready.setdefault((flat[k][0], q), set()).add(k)
            choose((flat[k][0], q))
    for k in range(len(flat)):
        if not count[k]:
            put(k)

    def ends(q):
        n = flat[best[q][1]][1]
        return best[q][0] + n["cost"][q[1]] + (TUNE["bias"] if q[1] == "v" and len(n["fns"]) > 1 else 0.0), best[q][1]
    while best:
        q = min(best, key=ends)
        at, k = best[q]
        r, n = flat[k]
        out.append((r, n, q[1]))
        end = at + n["cost"][q[1]]
        free[q] = end if q[1] != "r" else 0.0
        for x in n["fns"]:
            ready[(r, x)].discard(k)
            choose((r, x))
        for j in succ[k]:
            when[j] = max(when[j], end + after(k, j))
            count[j] -= 1
            if not count[j]:
                put(j)
    return out


def rank_program(g, core, T, topo):
    r = T.rank_of(core)
    if r is None:
        return
    cores = list(T.cores)
    if "order" not in _PLANS:
        _PLANS["order"] = arrange([calls(i, cores, topo) for i in range(N)])
    queue = {"v": g.vector, "s": g.scalar, "t": g.tensor, "g": g, "y": g.sync}
    total, known, snap, log = {}, {q: {} for q in queue}, {}, {}

    def ap(w):
        n, c0, c1, st, p0, p1 = w[:6]
        if len(w) > 6:
            a0, a1, b0, b1 = w[6]
            return T[n][p0:p1, a0, b0:b1] if a1 == a0 + 1 else T[n][p0:p1, a0:a1, b0:b1]
        n, at = LOG[n][:2]
        c0, c1 = c0 + at, c1 + at
        return T[n][p0:p1, c0:c1] if st == 1 else T[n][p0:p1, c0:c1:st]

    env = dict(queue, T=T, ap=ap)

    def wait(q, tok):
        s, v = tok
        if known[q].get(s, 0) >= v:
            return
        queue[q].wait_ge(T.sem[s], v)
        known[q][s] = v
        for a, b in snap.get(tok, {}).items():
            if known[q].get(a, 0) < b:
                known[q][a] = b

    tokens = {}
    for rank, n, q in _PLANS["order"]:
        if rank != r:
            continue
        s = n["sem"] or _QS[q]
        if q != "r":
            need = {}
            for ws, isw in ((n["rd"], False), (n["wr"], True)):
                for w in ws:
                    for w2, isw2, tok, q2 in log.get(w[0], ()):
                        if (isw or isw2 or (w[0] in ("pa", "pu") and q != q2)) and meet(w, w2):
                            need[tok[0]] = max(need.get(tok[0], 0), tok[1])
            for a in n["after"]:
                tok = tokens[a["i"]]
                need[tok[0]] = max(need.get(tok[0], 0), tok[1])
            for x in sorted(need):
                wait(q, (x, need[x]))
            ins = n["fns"][q](env)
            total[s] = total.get(s, 0) + n["by"]
            if not n["cast"]:
                ins.then_inc(T.sem[s], n["by"])
                snap[(s, total[s])] = dict(known[q])
        else:
            total[s] = n["by"]
        tok = tokens[n["i"]] = (s, total[s])
        for ws, isw in ((n["rd"], False), (n["wr"], True)):
            for w in ws:
                log.setdefault(w[0], []).append((w, isw, tok, q))
    for s in sorted(total):
        wait("g", (s, total[s]))
